import numpy as np, ml_dtypes
CORES = [24,48,72,152,176,200]
N = 6
BF = ml_dtypes.bfloat16
def gentries(a):
    return np.ascontiguousarray(a.reshape(8, 16, -1).transpose(0, 2, 1)).reshape(8, -1)
def gtable(e):
    e = np.asarray(e); return np.ascontiguousarray(e.reshape(8, -1, 16).transpose(0, 2, 1)).reshape(128, -1).astype(np.int32)
W, L, RO = 1536, 192, 4
NONE = W - 1
def link(rng, n, m, share):
    q, g, k, c = np.nonzero((m != NONE) & (rng.random(m.shape) < share))
    n[q, g, rng.integers(0, 16, len(q)), m[q, g, k, c]] = c
def world(rng, fill, stray, share):
    s = (N, 8, 16, W)
    m = np.where(rng.random(s) < fill, rng.integers(0, NONE, s), NONE); n = np.where(rng.random(s) < stray, rng.integers(0, NONE, s), NONE)
    link(rng, n, m, share)
    return n, m
def words(rng):
    pool = rng.integers(0, NONE, (N, 8, 40)); a = np.take_along_axis(pool, rng.integers(0, 40, (N, 8, L)), 2)
    return np.where(rng.random((N, 8, L)) < 0.5, a, rng.integers(0, NONE, (N, 8, L)))
def pack(x, n, m, w, z, th):
    x[..., NONE] = 255; n[..., NONE] = NONE; m[..., NONE] = NONE
    return {"x": x.reshape(N, 128, W).astype(np.float32).astype(BF), "nm": np.ascontiguousarray((n + 4096 * m).reshape(N, 128, W)).astype(np.int32),
            "w": np.stack([gtable(a) for a in w]), "z": z.reshape(N, 128, L).astype(np.float32).astype(BF),
            "th": np.repeat(th, 16, axis=1).reshape(N, 128, 1).astype(np.int32)}
def setup_inputs(rng):
    n, m = world(rng, rng.choice(np.array([0.0, 0.1, 0.4, 0.8, 1.0]), (N, 8, 1, W)), 0.3, 0.75)
    return pack(rng.integers(0, 16, (N, 8, 16, W)), n, m, words(rng), rng.integers(0, 16, (N, 8, 16, L)), rng.integers(55, 86, (N, 8)))
def setup_inputs_crowd(rng):
    n, m = world(rng, 0.7, 0.3, 0.7); x = rng.integers(0, 16, (N, 8, 16, W)); z = rng.integers(0, 16, (N, 8, 16, L)); w = np.zeros((N, 8, L), np.int64)
    for g in range(8):
        pw = rng.permutation(NONE)[:12]; po = rng.permutation(NONE)[:6]
        for q in range(N):
            mm = po[rng.integers(0, 6, (16, 12))]; mm[rng.random((16, 12)) < 0.3] = NONE; mm[:, 0] = NONE; mm[0, 0] = po[0]
            m[q, g][:, pw] = mm; n[q, g][:, po] = NONE
            k, c = np.nonzero(mm != NONE); n[q, g][rng.integers(0, 16, len(k)), mm[k, c]] = pw[c]
            n[q, g][0, po[0]] = pw[0]
            v = int(rng.integers(1, 13)); w[q, g] = pw[rng.integers(0, v, L)]; w[q, g, 0] = pw[0]; w[q, g, L - 1] = pw[0]
            near = np.clip(x[q, g][:, po[rng.integers(0, 6, L)]] + rng.integers(-1, 2, (16, L)), 0, 15)
            z[q, g] = np.where(rng.random(L) < 0.5, near, z[q, g])
            a = x[q, g][:, po[0]].copy(); far = np.where(a < 8, 15, 0)
            z[q, g][:, 0] = far if g % 2 == 0 else a
            z[q, g][:, L - 1] = a if g % 2 == 0 else far
    return pack(x, n, m, w, z, rng.integers(20, 91, (N, 8)))
def setup_inputs_ties(rng):
    proto = rng.integers(0, 12, (8, 16, 4)); kind = rng.integers(0, 4, (N, 8, W))
    x = np.stack([np.take_along_axis(proto, kind[q][:, None, :], 2) for q in range(N)])
    m = np.take_along_axis(rng.integers(0, NONE, (N, 8, 4, W)), rng.integers(0, 4, (N, 8, 16, W)), 2)
    n = np.full((N, 8, 16, W), NONE, np.int64); link(rng, n, m, 0.6)
    w = words(rng); one = np.take_along_axis(m, w[:, :, None, :], 3)[:, :, :1]
    z = np.take_along_axis(x, one, 3) + 2; z[:, :, 0] += rng.integers(-1, 2, (N, 8, L))
    return pack(x, n, m, w, z, np.full((N, 8), 32, np.int64))
def setup_inputs_hollow(rng):
    n, m = world(rng, 0.6, 0.2, 0.7); w = words(rng)
    n[:, 0::4] = NONE
    for g in (0, 4):
        o = rng.permutation(NONE); a, b = o[:L // 2], o[L // 2:]
        for q in range(N):
            if q % 2 == 0:
                m[q, g][:, a] = NONE; w[q, g, rng.permutation(L)[:L // 2]] = a
            else:
                m[q, g][:, a] = rng.integers(0, NONE, (16, L // 2))
                w[q, g] = np.where(rng.random(L) < 0.5, b[rng.integers(0, 40, L)], b[rng.integers(0, len(b), L)])
    m[:, 1::4] = np.where(rng.random((N, 2, 1, W)) < 0.8, NONE, m[:, 1::4])
    m[:, 2::4] = np.where(rng.random((N, 2, 16, W)) < 0.9, NONE, m[:, 2::4]); n[:, 2::4] = np.where(rng.random((N, 2, 16, W)) < 0.8, rng.integers(0, NONE, (N, 2, 16, W)), n[:, 2::4])
    for c in (0, NONE - 1):
        m[:, 3::4, :, c] = rng.choice(np.array([0, NONE - 1, NONE]), (N, 2, 16)); n[:, 3::4, :, c] = rng.choice(np.array([0, NONE - 1, NONE]), (N, 2, 16))
    w[:, 3::4] = rng.choice(np.array([0, NONE - 1]), (N, 2, L))
    return pack(rng.integers(0, 16, (N, 8, 16, W)), n, m, w, rng.integers(0, 16, (N, 8, 16, L)), rng.choice(np.array([0, 1, 90, 255]), (N, 8)))
def setup_inputs_mutual(rng):
    n = np.full((N, 8, 16, W), NONE, np.int64); m = np.full((N, 8, 16, W), NONE, np.int64); i = np.arange(NONE)[None, :]
    for q in range(N):
        for g in range(8):
            ob = rng.permutation(NONE); wo = rng.permutation(NONE); s = rng.permutation(NONE)[:16]; s2 = rng.permutation(s)
            m[q, g][:, wo] = ob[(i + s[:, None]) % NONE]; n[q, g][:, ob] = wo[(i - s2[:, None]) % NONE]
    th = rng.integers(40, 80, (N, 8)); th[:, ::2] = 255
    x = rng.integers(0, 16, (N, 8, 16, W)); w = words(rng); z = rng.integers(0, 16, (N, 8, 16, L))
    r = int(rng.integers(0, N)); r1, r2, r3 = (r - 1) % N, (r - 2) % N, (r - 3) % N
    th[r] = rng.permutation(np.array([241, 244, 247, 250, 253, 254, 255, 255])); won = int(rng.integers(3, 16)); h = int(rng.integers(0, 8))
    for g in range(8):
        pw = rng.permutation(np.setdiff1d(np.arange(NONE), w[[r, r1, r2], g]))[:33]; ob = rng.permutation(NONE)[:33]; tb = rng.permutation(NONE)[:32]
        m[r, g][np.isin(m[r, g], ob)] = NONE; m[r, g][:, pw] = ob; n[r, g][0::2][:, ob] = pw; x[r, g][:, ob] = 15
        m[r2, g][np.isin(m[r2, g], tb)] = NONE; m[r2, g][:, pw[:32]] = tb; n[r2, g][:, tb] = pw[:32]
        x[r2, g][:, tb] = (np.arange(32)[None, :] + rng.permutation(16)[:, None]) // 16
        p = rng.permutation(L); w[r1, g, p[:32]] = pw[:32]; w[r3, g, rng.permutation(L)[:32]] = pw[:32]
        if g == h: w[r1, g, p[32:32 + won]] = pw[32]
        m[r1, g][:, w[r1, g]] = NONE; m[r3, g][:, pw[:32]] = NONE
        if g == h:
            c = int(rng.integers(0, NONE)); m[r1, g][:, pw[32]] = c; n[r1, g][:, c] = pw[32]
    return pack(x, n, m, w, z, th)
def setup_inputs_spread(rng):
    n, m = world(rng, rng.random((N, 8, 1, W)), rng.random((N, 8, 1, W)), 0.7)
    x = rng.integers(0, 16, (N, 8, 16, W)) >> rng.integers(0, 5, (N, 8, 1, W)); z = rng.integers(0, 16, (N, 8, 16, L)) >> rng.integers(0, 5, (N, 8, 1, L))
    th = rng.integers(0, 256, (N, 8)); th[0, 0] = 0; th[1, 1] = 255
    return pack(x, n, m, words(rng), z, th)
def check_inputs(d):
    bad = []; x = np.asarray(d["x"]).astype(np.float32); z = np.asarray(d["z"]).astype(np.float32); p = np.asarray(d["nm"]).astype(np.int64); th = np.asarray(d["th"])
    if not np.all((x[..., :NONE] >= 0) & (x[..., :NONE] <= 15) & (np.floor(x[..., :NONE]) == x[..., :NONE])): bad.append("range of x")
    if not np.all(x[..., NONE] == 255): bad.append("last column of x")
    if not np.all((p >= 0) & ((p & 4095) <= NONE) & ((p >> 12) <= NONE)): bad.append("range of nm")
    if not np.all(p[..., NONE] == NONE + 4096 * NONE): bad.append("last column of nm")
    if np.min(d["w"]) < 0 or np.max(d["w"]) > NONE - 1: bad.append("range of w")
    if not np.all((z >= 0) & (z <= 15) & (np.floor(z) == z)): bad.append("range of z")
    if np.min(th) < 0 or np.max(th) > 255: bad.append("range of th")
    if not np.all(th.reshape(N, 8, 16) == th.reshape(N, 8, 16)[:, :, :1]): bad.append("th alike in a group")
    return bad
def reference(x, nm, w, z, th):
    X = x.astype(np.float32).astype(np.int32).reshape(N, 8, 16, W); P = nm.astype(np.int32).reshape(N, 8, 16, W); NA = P & 4095; MA = P >> 12
    wl = np.stack([gentries(a) for a in w]).astype(np.int32); zl = z.astype(np.float32).astype(np.int32).reshape(N, 8, 16, L)
    t0 = th.astype(np.int32).reshape(N, 8, 16)[:, :, :1]; wins = [0] * N
    lane = np.arange(L); earlier = lane[None, :] < lane[:, None]; rows = np.arange(16)[:, None]
    for t in range(RO):
        nw, nz, cnt = [], [], []
        for a in range(N):
            n, m, xx, ww, zz = NA[a], MA[a], X[a], wl[a], zl[a]
            e = np.take_along_axis(m, ww[:, None, :], 2); ef = e.reshape(8, 1, 16 * L)
            D = np.add.reduce(np.abs(zz[:, :, None, :] - np.take_along_axis(xx, ef, 2).reshape(8, 16, 16, L)), axis=1)
            real = np.any(np.take_along_axis(n, ef, 2).reshape(8, 16, 16, L) == ww[:, None, None, :], axis=1)
            key = np.where(real, D, D + 8192); k = np.argmin(key, axis=1)[:, None, :]
            o = np.take_along_axis(e, k, 1)[:, 0]; hit = np.take_along_axis(key, k, 1)[:, 0] < t0[a] + (wins[a] & 31)
            no = np.take_along_axis(n, o[:, None, :], 2); xo = np.take_along_axis(xx, o[:, None, :], 2)
            mn = np.take_along_axis(m, no.reshape(8, 1, 16 * L), 2).reshape(8, 16, 16, L)
            cand = np.any(mn == o[:, None, None, :], axis=1) & (no != NONE)
            few = np.where(cand, np.add.reduce((mn != NONE).astype(np.int32), axis=1), 17); j = np.argmin(few, axis=1)[:, None, :]
            nw.append(np.where(np.any(cand, axis=1), np.take_along_axis(no, j, 1)[:, 0], ww)); nz.append(xo); cnt.append(int(np.count_nonzero(hit)))
            h = hit[:, None, :]
            n2 = np.where(h, np.where(no == ww[:, None, :], no, NONE), np.where(rows == ((lane + t) & 15), ww[:, None, :], no))
            x2 = np.where(h, xo, xo + np.clip(zz - xo, -2, 2)); m2 = np.where(e == o[:, None, :], e, NONE)
            go = ~np.any((o[:, :, None] == o[:, None, :]) & earlier, axis=2) & (o != NONE)
            gw = ~np.any((ww[:, :, None] == ww[:, None, :]) & earlier, axis=2) & hit
            for g in range(8):
                c = o[g][go[g]]; n[g][:, c] = n2[g][:, go[g]]; xx[g][:, c] = x2[g][:, go[g]]
                m[g][:, ww[g][gw[g]]] = m2[g][:, gw[g]]
        d = 1 + t % (N - 1); wins = cnt
        wl = np.stack([nw[(a - d) % N] for a in range(N)]).astype(np.int32); zl = np.stack([nz[(a - d) % N] for a in range(N)])
    return {"ynm": (NA + 4096 * MA).reshape(N, 128, W).astype(np.float32), "yw": np.stack([gtable(a) for a in wl]).astype(np.float32), "yz": zl.reshape(N, 128, L).astype(np.float32).astype(BF)}

@@ -1,0 +1,511 @@
+from concourse.mybir import AluOpType as A, AxisListType, ActivationFunctionType as F
+
+W, L, RO, NR = 1536, 192, 4, 6
+NONE = W - 1
+EMPTY = 2559
+H = 96
+XS = 64
+SEG = [8 * a * (a + 1) + a for a in range(13)]
+EL = SEG[12]
+U = 32768.0
+
+f32, bf, f16, i32, u16 = "float32", "bfloat16", "float16", "int32", "uint16"
+SCRATCH = {}
+for _n, _c, _d in [
+    ("NM", W, i32), ("NT", 4096, f32), ("MT", 4096, f32), ("XT", 4096, bf), ("FT", W, f32), ("OUT", W, f32),
+    ("IO", W, f32), ("IC", W, bf), ("NG", 3072, bf), ("XG", 3072, bf), ("MX", 3072, bf), ("EQ", 3072, bf),
+    ("W32", 12, i32), ("TH", 1, i32), ("Z0", L, bf), ("WI", 12, u16),
+    ("IA", 272, i32), ("RR", 272, f32), ("PI", 2, i32), ("PJ", 2, i32), ("PF", 4, f32),
+    ("CI", 128, f32), ("KI", 256, f32), ("GI", 128, f32), ("RS", 256, f32), ("CR", 256, bf), ("CK", 16, bf), ("LR", L, bf),
+    ("ONE", 128, bf), ("ID", 128, f32), ("Ih", 128, f16), ("Ib", 128, bf), ("nI", 128, bf), ("I15", H, bf), ("IMa", H, bf),
+    ("IMb", H, bf), ("If1", H, bf), ("If2", H, bf), ("BOX", 128, bf), ("W1", 8, bf), ("W2", 8, bf), ("Wm", 8, bf),
+    ("Wp", 8, bf), ("Wf", 8, f32), ("Wt", 8, bf), ("BOh", 8, f16), ("REP", 16, u16), ("END", 2, u16), ("LL", 12, f32),
+    ("DF", 12, f32), ("C1", 12, f32), ("C2", 12, f32), ("BA", 12, f32), ("BB", 12, f32),
+    ("AC", 12, f32), ("BC", 12, f32), ("JK", 2 * EL, bf), ("G1", 12, f32),
+    ("DL", 12, bf), ("TRI", 16, f32), ("MS", EL, bf), ("T1", 4, f32), ("THB", H, bf), ("TH0", 16, f32), ("THR", 16, f32),
+    ("E16", L, u16), ("U16", L, u16), ("EF", L, f16), ("WC", L, bf), ("OC", 208, bf), ("ZT", L, bf), ("ZR", L, bf),
+    ("FL", 256, bf), ("SC", 256, f32), ("S32", 16, i32), ("O32", 16, i32), ("OA", 256, f16), ("OL", 12, u16),
+    ("OLF", 16, f32), ("WLF", 12, f32), ("OCL", 12, bf), ("HT", 16, bf), ("HA", 256, bf), ("WB", L, f32),
+    ("EE", EL, bf), ("ES", EL, bf), ("OF", 16, f32), ("OFO", 12, u16), ("OFW", 12, u16),
+    ("E4", L, f32), ("EC", L, bf), ("NO", L, f32), ("DN", L, f32), ("DA", L, f32), ("Q", L, bf), ("AM", L, f32), ("AN", L, f32),
+    ("T3", L, f32), ("DX", L, bf), ("CL", L, bf), ("CM", L, bf), ("SS", 2, f32), ("SI", 2, i32),
+]:
+    SCRATCH[_n] = ("sbuf", [128, _c], _d)
+for _t in range(RO):
+    SCRATCH["ZO%d" % _t] = ("sbuf", [128, L], bf)
+    SCRATCH["ZL%d" % _t] = ("sbuf", [128, L], bf)
+    SCRATCH["WO%d" % _t] = ("sbuf", [128, 12], u16 if _t < RO - 1 else f32)
+    SCRATCH["WL%d" % _t] = ("sbuf", [128, 12], u16 if _t < RO - 1 else f32)
+SCRATCH["PA"] = ("psum", [128, 1024], bf)
+for _n in ["PD", "PC", "PX0", "PX1", "PL", "PM", "PH"]:
+    SCRATCH[_n] = ("psum", [128, 512], f32)
+
+SEMAPHORES = (["sV", "sA", "sP", "sG", "sent", "lw", "lz", "lt", "lx", "ln0", "ln1", "ln2", "st"]
+              + ["za%d" % t for t in range(RO)] + ["wa%d" % t for t in range(RO)])
+
+
+def route(T, topo, r, t):
+    src = T.cores[r]
+    dst = T.cores[(r + 1 + t % (NR - 1)) % NR]
+    if topo.may_write(src, dst):
+        return src, None, dst
+    cand = [c for c in topo.cores_of(src) if c != src and T.rank_of(c) is None and topo.may_write(c, dst)]
+    cand.sort(key=lambda c: topo.die(c) != topo.die(src))
+    return src, cand[0], dst
+
+
+def put(g, T, topo, src, dst, out, in_, sem):
+    rid, pid = topo.addr(dst, src)
+    g.remote_dma(out, in_, T.sem[sem], T.sem.sent, pid, rid, topo.mask(src, dst))
+    return len(topo.engines(src, dst))
+
+
+def relay_program(g, core, T, topo):
+    sent = 0
+    for t in range(RO):
+        for r in range(NR):
+            src, via, dst = route(T, topo, r, t)
+            if via != core:
+                continue
+            n = len(topo.engines(src, core))
+            for buf, sem in (("ZL%d" % t, "za%d" % t), ("WL%d" % t, "wa%d" % t)):
+                g.wait_ge(T.sem[sem], n)
+                sent += put(g, T, topo, core, dst, T[buf][:], T[buf][:], sem)
+    if sent:
+        g.wait_ge(T.sem.sent, sent)
+
+
+def rank_program(g, core, T, topo):
+    rank = T.rank_of(core)
+    if rank is None:
+        relay_program(g, core, T, topo)
+        return
+    Q = {"V": g.vector, "A": g.scalar, "P": g.tensor, "G": g, "S": g.sync}
+    cnt = {}
+    waited = {q: {} for q in Q}
+    lastw, readers, bank = {}, {}, {}
+
+    def need(q, toks):
+        best = {}
+        for s, n in toks:
+            best[s] = max(best.get(s, 0), n)
+        for s, n in best.items():
+            if waited[q].get(s, 0) < n:
+                Q[q].wait_ge(T.sem[s], n)
+                waited[q][s] = n
+
+    def order(q, r, w, b):
+        own = "s" + q
+        toks = []
+        for k in r:
+            if k in lastw:
+                toks.append(lastw[k])
+        for k in w:
+            if k in lastw:
+                toks.append(lastw[k])
+            toks.extend(readers.get(k, {}).items())
+        for k in b:
+            toks.extend((s, n) for s, n in bank.get(k, {}).items() if s != own)
+        if q == "P":
+            toks = [x for x in toks if x[0] != own]
+        need(q, toks)
+
+    def note(tok, r, w, b):
+        for k in r:
+            readers.setdefault(k, {})[tok[0]] = tok[1]
+        for k in w:
+            lastw[k] = tok
+            readers[k] = {}
+        for k in b:
+            bank.setdefault(k, {})[tok[0]] = tok[1]
+
+    def op(q, fn, r=(), w=(), b=()):
+        order(q, r, w, b)
+        s = "s" + q
+        cnt[s] = cnt.get(s, 0) + 1
+        fn().then_inc(T.sem[s], 1)
+        note((s, cnt[s]), r, w, b)
+
+    def dma(q, out, in_, sem, r=(), w=()):
+        order(q, r, w, ())
+        cnt[sem] = cnt.get(sem, 0) + 16
+        Q[q].dma_start(out, in_).then_inc(T.sem[sem], 16)
+        note((sem, cnt[sem]), r, w, ())
+
+    v, a = g.vector, g.scalar
+
+    def ts(out, in0, s1, s2, o0, o1, r, w, b=()):
+        if o1 is None:
+            op("V", lambda: v.tensor_scalar(out, in0, s1, None, o0), r, w, b)
+        else:
+            op("V", lambda: v.tensor_scalar(out, in0, s1, s2, o0, o1), r, w, b)
+
+    def tt(out, in0, in1, o, r, w, b=()):
+        op("V", lambda: v.tensor_tensor(out, in0, in1, o), r, w, b)
+
+    def cp(out, in_, r, w, b=()):
+        op("V", lambda: v.tensor_copy(out, in_), r, w, b)
+
+    def ms(out, c, w, b=()):
+        op("V", lambda: v.memset(out, c), (), w, b)
+
+    def act(out, in_, f, r, w, b=(), bias=0.0, scale=1.0, acc=None):
+        op("A", lambda: a.activation(out, in_, f, bias=bias, scale=scale, accum_out=acc), r, w, b)
+
+    def mm(out, lhsT, rhs, start, stop, r, w, b):
+        op("P", lambda: g.tensor.matmul(out, lhsT, rhs, start, stop), r, w, [b])
+
+    def iota(out, pat, base, cm, w, fl=True):
+        if fl:
+            op("G", lambda: g.iota(out, pat, base, cm, allow_small_or_imprecise_dtypes=True), (), w)
+        else:
+            op("G", lambda: g.iota(out, pat, base, cm), (), w)
+
+    def code(out, in_, r, w, b=(), scaled=False):
+        act(out, in_, F.Exp, r, w, b, bias=-EMPTY / 32.0, scale=(1.0 / 32 / 4096 if scaled else 1.0 / 32))
+
+    NTw, MTw, XTw = T.NT[:, 0:W], T.MT[:, 0:W], T.XT[:, 0:W]
+
+    dma("S", T.NM[:, 0:512], T.nm[:, 0:512], "ln0", w=["NM0"])
+    dma("A", T.NM[:, 512:1024], T.nm[:, 512:1024], "ln1", w=["NM1"])
+    dma("S", T.NM[:, 1024:W], T.nm[:, 1024:W], "ln2", w=["NM2"])
+    dma("A", T.W32[:], T.w[:], "lw", w=["W32"])
+    dma("S", XTw, T.x[:], "lx", w=["XT"])
+    dma("A", T.Z0[:], T.z[:], "lz", w=["Z0"])
+    dma("S", T.TH[:], T.th[:], "lt", w=["TH"])
+
+    iota(T.PI[:], [[0, 2]], 0, 1, ["PI"], False)
+    iota(T.CI[:], [[1, 128]], 0, 0, ["CI"])
+    iota(T.IO[:], [[1, W]], 0, 0, ["IO"])
+    iota(T.GI[:], [[1, 8], [0, 16]], 0, 0, ["GI"])
+    iota(T.KI[:], [[0, 16], [1, 16]], 0, 0, ["KI"])
+    iota(T.IA[:], [[1, 272]], 128, -1, ["IA"], False)
+    pf, pm, pg = T.PF[:, 0:1], T.PF[:, 1:2], T.PF[:, 2:3]
+    ms(T.ONE[:], 1.0, ["ONE"])
+    ms(T.O32[:], 0, ["O32"])
+    ms(T.HT[:], 0.0, ["HT"])
+    ms(T.OLF[:], 0.0, ["OLF"])
+    ms(T.CK[0:1, :], -17 * U, ["CK"])
+    ms(T.MS[:], 4096.0, ["MSf"])
+    ts(T.PJ[:, 0:1], T.PI[:, 0:1], 15, None, A.bitwise_and, None, ["PI"], ["PJ0"])
+    ts(T.PJ[:, 1:2], T.PI[:, 0:1], 4, None, A.logical_shift_right, None, ["PI"], ["PJ1"])
+    cp(pf, T.PI[:, 0:1], ["PI"], ["pf"])
+    cp(T.PF[:, 1:3], T.PJ[:], ["PJ0", "PJ1"], ["pm"])
+    ts(T.ID[:], T.CI[:], pf, None, A.is_equal, None, ["CI", "pf"], ["ID"])
+    for name, c in (("W1", 1.0), ("W2", 2 * U), ("Wm", -U), ("Wp", U), ("Wf", 1.0 / 16), ("Wt", U / 16), ("BOh", 1.0)):
+        ts(T[name][:], T.CI[:, 0:8], pg, c, A.is_equal, A.mult, ["CI", "pm"], [name])
+    cp(T.Ih[:], T.ID[:], ["ID"], ["Ih"])
+    cp(T.REP[:], T.CI[:, 0:16], ["CI"], ["REP"])
+    ts(T.TRI[:], T.CI[:, 0:16], pm, 15.0, A.add, A.is_gt, ["CI", "pm"], ["TRI"])
+    ts(T.LL[:], T.CI[:, 0:12], 16.0, pm, A.mult, A.add, ["CI", "pm"], ["LL"])
+    ts(T.T1[:, 0:1], pm, 1.5, None, A.add, None, ["pm"], ["T10"])
+    ts(T.BA[:], T.LL[:], 8.0, 1536.0, A.mult, A.add, ["LL"], ["BA"])
+    ts(T.BB[:], T.LL[:], 16.0, 1024.0, A.mult, A.add, ["LL"], ["BB"])
+    tt(T.T1[:, 1:2], T.T1[:, 0:1], T.T1[:, 0:1], A.mult, ["T10"], ["T11"])
+    tt(T.DF[:], T.BA[:], T.BB[:], A.max, ["BA", "BB"], ["DF"])
+    ts(T.T1[:, 2:3], T.T1[:, 1:2], 8.0, pm, A.mult, A.add, ["T11", "pm"], ["T12"])
+    ts(T.C1[:], T.LL[:], -1.0 / 256, 0.875, A.mult, A.add, ["LL"], ["C1"])
+    ts(T.C2[:], T.LL[:], -1.0 / 256, 1.0 / 512, A.mult, A.add, ["LL"], ["C2"])
+    ts(T.END[:, 0:1], T.T1[:, 2:3], 2.0, float(EL - 1), A.subtract, A.min, ["T12"], ["END"])
+    for name, c, n in (("If1", -370 * U, H), ("Ib", 1.0, 128), ("nI", -1.0, 128), ("I15", 1536.0, H), ("IMa", 2560 * 4096.0, H),
+                       ("IMb", -4096.0, H), ("If2", -18 * U, H)):
+        act(T[name][0:n, :], T.ID[0:n, 0:n], F.Copy, ["ID"], [name], scale=c)
+    code(T.IC[:], T.IO[:], ["IO"], ["IC"])
+
+    banks = ["PX0", "PX1", "PH"]
+    magic = 1.5 * 2.0 ** 35
+    for j in range(3):
+        c = slice(512 * j, 512 * j + 512)
+        ts(T[banks[j]][:], T.NM[:, c], magic, magic, A.add, A.subtract, ["NM%d" % j], ["M4%d" % j], [banks[j]])
+        tt(T.NT[:, c], T.NM[:, c], T[banks[j]][:], A.subtract, ["NM%d" % j, "M4%d" % j], ["NT%d" % j], [banks[j]])
+        act(T.FT[:, c], T[banks[j]][:], F.Relu, ["M4%d" % j], ["FT%d" % j], [banks[j]], bias=-(NONE - 1) * 2.0 ** 22, scale=1024.0)
+        if j == 0:
+            ts(T.BOX[:], T.GI[:], pg, -U, A.is_equal, A.mult, ["GI", "pm"], ["BOX"])
+            ts(T.CR[0:1, :], T.KI[0:1, :], 2048.0, None, A.mult, None, ["KI"], ["CR"])
+    lastw["NT"] = lastw["NT2"]
+    cp(T.WI[:], T.W32[:], ["W32"], ["WI"])
+
+    def kview(buf, c, k):
+        return buf[:, 1536 * c + k:1536 * c + 1536:16]
+
+    def kslot(buf, c, k, n=1):
+        s = (16 * c + k) * H
+        return buf[:, s:s + n * H]
+
+    def kcols(P, c, k):
+        return P[0:H, 128 * c + k:128 * c + 128:16]
+
+    def eq_half(c, col, ok, ks):
+        for k in ks:
+            tt(kslot(T.EQ, c, k), kview(T.NG, c, k), T.PA[:, col + H * c:col + H * c + H], A.is_equal,
+               ["NG%d" % c, ok], ["EQ%d_%d" % (c, k)], ["PA"])
+            mm(kcols(T.PC, c, k), kslot(T.EQ, c, k), T.W1[:], True, True, ["EQ%d_%d" % (c, k), "W1"], ["PC%d" % c], "PC")
+
+    def flag(c):
+        cs = slice(128 * c, 128 * c + 128)
+        act(T.FL[0:H, cs], T.PC[0:H, cs], F.Sign, ["PC%d" % c], ["FL%d" % c], ["PC"])
+
+    def weigh(c, I, stop):
+        cs = slice(128 * c, 128 * c + 128)
+        mm(T.PD[0:H, cs], T[I][0:H, :], T.FL[0:H, cs], False, stop, [I, "FL%d" % c], ["PD"], "PD")
+
+    def pick(col, fallback):
+        op("V", lambda: v.tensor_tensor_scan(T.SC[0:H, :], T.RS[0:H, :], T.PD[0:H, 0:256], 0.0, A.add, A.min), ["RS", "PD"], ["SC"], ["PD"])
+        if fallback:
+            tt(T.S32[0:H, :], T.SC[0:H, 15:256:16], T.PL[0:H, 32:48], A.min, ["SC", "FB"], ["S32"], ["PL"])
+        else:
+            cp(T.S32[0:H, :], T.SC[0:H, 15:256:16], ["SC"], ["S32"])
+        ts(T.O32[0:H, :], T.S32[0:H, :], 2047, None, A.bitwise_and, None, ["S32"], ["O32"])
+        tt(T.OA[:], T.O32[:, 0:16].indirect(T.REP[:, 0:16]), T.RR[:, 0:256], A.mult, ["O32", "REP", "RR"], ["OA"])
+        for c in range(2):
+            mm(T.PL[:, col + 6 * c:col + 6 * c + 6], T.OA[0:H, 128 * c:128 * c + 128], T.BOh[0:H, 0:6], True, True,
+               ["OA", "BOh"], ["PL%d" % col], "PL")
+
+    def first_cmp(js):
+        for j in js:
+            ts(T.EE[:, SEG[j]:SEG[j + 1]], T.OC[:, 16 * j + 31:14:-1], T.OCL[:, j:j + 1], T.DL[:, j:j + 1], A.is_equal, A.mult,
+               ["OC", "OCv", "OCL", "DL"], ["EE%d" % j])
+
+    def first_cnt(js):
+        for j in js:
+            n = 16 * j + 16
+            act(T.JK[:, SEG[j]:SEG[j] + n], T.PX0[:, 0:n], F.Sign, ["CB", "BA"], ["AC%d" % j], ["PX0"], bias=T.BA[:, j:j + 1],
+                acc=T.AC[:, j:j + 1])
+            act(T.JK[:, EL + SEG[j]:EL + SEG[j] + n], T.PX0[:, 0:n], F.Sign, ["CB", "BB"], ["BC%d" % j], ["PX0"], bias=T.BB[:, j:j + 1],
+                acc=T.BC[:, j:j + 1])
+
+    def x_update(t):
+        zo = T["ZO%d" % t]
+        tt(T.DX[:], T.PA[:, 0:L], zo[:], A.subtract, ["zP", "ZO%d" % t], ["DX"], ["PA"])
+        ts(T.CL[:], T.DX[:], -2.0, 2.0, A.max, A.min, ["DX"], ["CL"])
+        tt(T.CM[:], T.CL[:], T.PM[:, 0:L], A.mult, ["CL", "miss"], ["CM"], ["PM"])
+        tt(T.XT[:, 0:4096].indirect(T.OFO[:, 0:12]), zo[:], T.CM[:], A.add, ["ZO%d" % t, "CM", "OFO"], ["XT"])
+
+    sent = [0]
+
+    def send(t, buf, land, sem):
+        src, via, dst = route(T, topo, rank, t)
+        need("G", [lastw[buf]])
+        sent[0] += put(g, T, topo, src, dst if via is None else via, T[land][:], T[buf][:], sem)
+
+    def arrival(t):
+        src, via, dst = route(T, topo, (rank - 1 - t % (NR - 1)) % NR, t)
+        n = len(topo.engines(src if via is None else via, dst))
+        lastw["ZL%d" % t] = ("za%d" % t, n)
+        lastw["WL%d" % t] = ("wa%d" % t, n)
+
+    for t in range(RO):
+        last = t == RO - 1
+        wk, zk = ("WI", "Z0") if t == 0 else ("WL%d" % (t - 1), "ZL%d" % (t - 1))
+        wl, z = T[wk][:, 0:12], T[zk]
+        if t == 0:
+            ts(T.E16[:], T.NM[:, 0:W].indirect(wl), 1.0 / 4096, None, A.mult, None, ["NM0", "NM1", "NM2", wk], ["E16"])
+        else:
+            ts(T.E16[:], MTw.indirect(wl), 1.0 / 4096, float(NONE), A.mult, A.min, ["MT", wk], ["E16"])
+        code(T.NG[:, 0:1536], NTw.indirect(T.E16[:, 0:H]), ["NT", "E16"], ["NG0"])
+        if t == 0:
+            ms(T.XT[:, NONE:W], 39.0, ["XT"])
+            for j in range(3):
+                c = slice(512 * j, 512 * j + 512)
+                tt(T.MT[:, c], T.FT[:, c], T[banks[j]][:], A.add, ["FT%d" % j, "M4%d" % j], ["MT%d" % j], [banks[j]])
+            lastw["MT"] = lastw["MT2"]
+            ts(T.ZT[:, 0:H], z[:, 0:H], 8.0, None, A.add, None, [zk], ["ZT0"])
+            ms(T.ZT[:, H:L], 8.0, ["ZT1"])
+        else:
+            x_update(t - 1)
+        act(T.XG[:, 16 * XS:1536], XTw.indirect(T.E16[:, XS:H]), F.Copy, ["XT", "E16"], ["XGa"])
+        act(T.XG[:, 1536:3072], XTw.indirect(T.E16[:, H:L]), F.Copy, ["XT", "E16"], ["XG1"])
+        code(T.NG[:, 1536:3072], NTw.indirect(T.E16[:, H:L]), ["NT", "E16"], ["NG1"])
+        cp(T.WC[:], T.IC[:, 0:W].indirect(wl), ["IC", wk], ["WC"])
+        cp(T.PA[:, 0:L], z[:], [zk], ["zP"], ["PA"])
+        cp(T.PA[:, L:2 * L], T.WC[:], ["WC"], ["wP"], ["PA"])
+        cp(T.XG[:, 0:16 * XS], XTw.indirect(T.E16[:, 0:XS]), ["XT", "E16"], ["XG0"])
+        ts(T.EF[:], MTw.indirect(wl), 1.0 / 4096, float(NONE), A.mult, A.min, ["MT", wk], ["EF"])
+        mm(T.PD[0:H, 0:256], T.ONE[0:1, 0:H], T.CR[0:1, :], True, False, ["ONE", "CR"], ["PD"], "PD")
+        for c in range(2):
+            mm(T.PD[0:H, 128 * c:128 * c + 128], T.ZT[:, H * c:H * c + H], T.BOX[:], False, False, ["ZT%d" % c, "BOX"], ["PD"], "PD")
+        mm(T.PD[0:H, 128:256], T.EF[:, H:L], T.Ih[:], False, False, ["EF", "Ih"], ["PD"], "PD")
+        xk = ["XG0", "XGa"]
+        for k in range(16):
+            mm(kcols(T.PD, 0, k), kview(T.XG, 0, k), T.Wm[:], False, False, xk + ["Wm"], ["PD"], "PD")
+        eq_half(0, L, "wP", range(16))
+
+        def diff(q):
+            P = "PX%d" % (q % 2)
+            for k in range(4):
+                o = T[P][:, H * k:H * k + H]
+                mm(o, T.Ib[:], kview(T.XG, 1, 4 * q + k), True, False, ["Ib", "XG1"], [P], P)
+                mm(o, T.nI[:], z[:, H:L], False, True, ["nI", zk], [P], P)
+
+        def absd(q):
+            P = "PX%d" % (q % 2)
+            act(kslot(T.MX, 1, 4 * q, 4), T[P][:, 0:4 * H], F.Abs, [P], ["AB%d" % q], [P])
+
+        def maxes(ks):
+            for k in ks:
+                tt(kslot(T.MX, 0, k), kview(T.XG, 0, k), T.PA[:, 0:H], A.max, xk + ["zP"], ["MX%d" % k], ["PA"])
+                mm(kcols(T.PD, 0, k), kslot(T.MX, 0, k), T.W2[:], False, False, ["MX%d" % k, "W2"], ["PD"], "PD")
+
+        def sums(q):
+            for k in range(4 * q, 4 * q + 4):
+                mm(kcols(T.PD, 1, k), kslot(T.MX, 1, k), T.Wp[:], False, False, ["AB%d" % q, "Wp"], ["PD"], "PD")
+
+        if t == 0:
+            ts(T.IA[:], T.IA[:], 15, None, A.bitwise_and, None, ["IA"], ["IA"])
+            ts(T.RS[:], T.KI[:], 0.0, 1e8, A.is_equal, A.mult, ["KI"], ["RS"])
+            ts(T.RR[:], T.IA[:], 0.0, None, A.is_equal, None, ["IA"], ["RR"])
+        diff(0)
+        maxes(range(8))
+        diff(1)
+        maxes(range(8, 16))
+        mm(T.PD[0:H, 0:128], T.EF[:, 0:H], T.Ih[:], False, False, ["EF", "Ih"], ["PD"], "PD")
+        flag(0)
+        absd(0)
+        absd(1)
+        diff(2)
+        eq_half(1, L, "wP", range(4))
+        diff(3)
+        absd(2)
+        absd(3)
+        sums(0)
+        eq_half(1, L, "wP", range(4, 8))
+        sums(1)
+        weigh(0, "If1", False)
+        eq_half(1, L, "wP", range(8, 12))
+        sums(2)
+        eq_half(1, L, "wP", range(12, 14))
+        sums(3)
+        eq_half(1, L, "wP", range(14, 16))
+        flag(1)
+        weigh(1, "If1", True)
+        act(T.WB[:], T.IO[:, 0:W].indirect(wl), F.Copy, ["IO", wk], ["WB"])
+        if t == 0:
+            act(T.LR[0:1, :], T.IO[0:1, 0:L], F.Copy, ["IO"], ["LR"], scale=1.0 / 256)
+            act(T.DL[:], T.DF[:], F.Copy, ["DF"], ["DL"])
+            for j in range(12):
+                act(T.MS[:, SEG[j]:SEG[j] + 16], T.TRI[:], F.Copy, ["TRI", "MSf"], ["MS%d" % j], scale=4096.0)
+            lastw["MS"] = lastw["MS11"]
+        pick(0, False)
+        cp(T.OL[:], T.PL[:, 0:12], ["PL0"], ["OL"], ["PL"])
+        ol = T.OL[:, 0:12]
+        cp(T.U16[:], NTw.indirect(ol), ["NT", "OL"], ["U16"])
+        code(T.OCL[:], T.PL[:, 0:12], ["PL0"], ["OCL"], ["PL"])
+        code(T.NG[:, 0:1536], MTw.indirect(T.U16[:, 0:H]), ["MT", "U16"], ["NG0"], scaled=True)
+        act(T.NO[:], NTw.indirect(ol), F.Copy, ["NT", "OL"], ["NO"])
+        code(T.NG[:, 1536:3072], MTw.indirect(T.U16[:, H:L]), ["MT", "U16"], ["NG1"], scaled=True)
+        if last:
+            ms(T.XT[:, NONE:W], 255.0, ["XT"])
+            cp(T["ZO%d" % t][:], XTw.indirect(ol), ["XT", "OL"], ["ZO%d" % t])
+        else:
+            ts(T["ZO%d" % t][:], XTw.indirect(ol), 31.0, None, A.min, None, ["XT", "OL"], ["ZO%d" % t])
+        send(t, "ZO%d" % t, "ZL%d" % t, "za%d" % t)
+        if t > 0:
+            op("V", lambda: v.tensor_reduce(T.SS[:, 0:1], T.PM[:, 400:416], AxisListType.X, A.add), ["wins"], ["SS0"], ["PM"])
+        cp(T.OC[:, 16:208], T.IC[:, 0:W].indirect(ol), ["IC", "OL"], ["OC"])
+        if t > 0:
+            cp(T.SI[:, 0:1], T.SS[:, 0:1], ["SS0"], ["SI"])
+        cp(T.WLF[:], wl, [wk], ["WLF"])
+        if t > 0:
+            ts(T.SI[:, 1:2], T.SI[:, 0:1], 31, None, A.bitwise_and, None, ["SI"], ["SJ"])
+        cp(T.PA[:, 2 * L:3 * L], T.OC[:, 16:208], ["OC"], ["oP"], ["PA"])
+        if t > 0:
+            ts(T.SS[:, 1:2], T.SI[:, 1:2], U, None, A.mult, None, ["SJ"], ["SS1"])
+        cp(T.OLF[:, 0:12], T.PL[:, 0:12], ["PL0"], ["OLF"], ["PL"])
+        if t > 0:
+            ts(T.THR[0:H, :], T.TH0[0:H, :], T.SS[0:H, 1:2], None, A.add, None, ["TH0", "SS1"], ["THR"])
+        mm(T.PD[0:H, 0:256], T.ONE[0:1, 0:H], T.CR[0:1, :], True, False, ["ONE", "CR"], ["PD"], "PD")
+        mm(T.PX0[:, 0:L], T.ID[:], T.WB[:], True, False, ["ID", "WB"], ["CB"], "PX0")
+        mm(T.PX0[:, 0:L], T.ONE[0:1, :], T.LR[0:1, :], False, True, ["ONE", "LR"], ["CB"], "PX0")
+        if t == 0:
+            cp(T.OC[:, 15:16], T.IC[:, NONE:W], ["IC"], ["OCv"])
+            cp(T.T1[:, 3:4], T.TH[:], ["TH"], ["T13"])
+            ts(T.THB[:], T.ONE[:, 0:H], T.T1[:, 3:4], None, A.mult, None, ["ONE", "T13"], ["THB"])
+            for c in range(2):
+                mm(T.PL[0:H, 64 + 8 * c:72 + 8 * c], T.THB[:], T.Wt[:], True, True, ["THB", "Wt"], ["PLt"], "PL")
+        tt(T.DN[:], NTw.indirect(ol), T.WB[:], A.subtract, ["NT", "OL", "WB"], ["DN"])
+        if t == 0:
+            ts(T.TH0[0:H, :], T.PL[0:H, 64:80], -498 * U, None, A.add, None, ["PLt"], ["TH0"], ["PL"])
+        mm(T.PL[0:H, 32:48], T.ONE[0:1, 0:H], T.CK[0:1, :], True, False, ["ONE", "CK"], ["FB"], "PL")
+        for c in range(2):
+            mm(T.PL[0:H, 32 + 8 * c:40 + 8 * c], T.WB[:, H * c:H * c + H], T.Wf[:], False, c == 1, ["WB", "Wf"], ["FB"], "PL")
+        thk = "TH0" if t == 0 else "THR"
+        tt(T.BA[:], T.C1[:], T.WLF[:], A.subtract, ["C1", "WLF"], ["BA"])
+        tt(T.BB[:], T.C2[:], T.WLF[:], A.subtract, ["C2", "WLF"], ["BB"])
+        tt(T.HT[0:H, :], T.SC[0:H, 15:256:16], T[thk][0:H, :], A.is_lt, ["SC", thk], ["HT"])
+        first_cmp(range(2))
+        for k in range(16):
+            mm(kcols(T.PD, 0, k), kview(T.NG, 0, k), T.Wm[:], False, False, ["NG0", "Wm"], ["PD"], "PD")
+        eq_half(0, 2 * L, "oP", range(8))
+        for c in range(2):
+            mm(T.PD[0:H, 128 * c:128 * c + 128], T.NO[:, H * c:H * c + H], T.ID[:], False, False, ["NO", "ID"], ["PD"], "PD")
+        eq_half(0, 2 * L, "oP", range(8, 16))
+        first_cmp(range(2, 7))
+        flag(0)
+        for k in range(16):
+            mm(kcols(T.PD, 1, k), kview(T.NG, 1, k), T.Wm[:], False, False, ["NG1", "Wm"], ["PD"], "PD")
+        weigh(0, "If2", False)
+        act(T.HA[:], T.HT[:, 0:16].indirect(T.REP[:, 0:16]), F.Copy, ["HT", "REP"], ["HA"])
+        eq_half(1, 2 * L, "oP", range(16))
+        code(T.EC[:], MTw.indirect(wl), ["MT", wk], ["EC"], scaled=True)
+        act(T.E4[:], MTw.indirect(wl), F.Copy, ["MT", wk], ["E4"])
+        first_cnt(range(2))
+        flag(1)
+        weigh(1, "If2", True)
+        first_cnt(range(2, 12))
+        act(T.DA[:], T.DN[:], F.Abs, ["DN"], ["DA"], scale=2048.0)
+        for c in range(2):
+            ha, cs = T.HA[0:H, 128 * c:128 * c + 128], slice(H * c, H * c + H)
+            mm(T.PH[:, cs], ha, T.I15[0:H, :], True, False, ["HA", "I15"], ["hitN"], "PH")
+            mm(T.PH[:, cs], ha, T.nI[0:H, 0:H], False, True, ["HA", "nI"], ["hitN"], "PH")
+        pick(16, True)
+        for c in range(2):
+            ha, cs = T.HA[0:H, 128 * c:128 * c + 128], slice(H * c, H * c + H)
+            cs2 = slice(L + H * c, L + H * c + H)
+            mm(T.PH[:, cs2], ha, T.IMa[0:H, :], True, False, ["HA", "IMa"], ["hitM"], "PH")
+            mm(T.PH[:, cs2], ha, T.IMb[0:H, :], False, True, ["HA", "IMb"], ["hitM"], "PH")
+            if not last:
+                mm(T.PM[:, cs], T.ONE[0:H, :], T.Ib[0:H, 0:H], True, False, ["ONE", "Ib"], ["miss"], "PM")
+                mm(T.PM[:, cs], ha, T.nI[0:H, 0:H], False, True, ["HA", "nI"], ["miss"], "PM")
+        if not last:
+            mm(T.PM[:, 400:416], T.ONE[0:H, :], T.HT[0:H, :], True, True, ["ONE", "HT"], ["wins"], "PM")
+        cp(T["WO%d" % t][:], T.PL[:, 16:28], ["PL16"], ["WO%d" % t], ["PL"])
+        send(t, "WO%d" % t, "WL%d" % t, "wa%d" % t)
+        arrival(t)
+        first_cmp(range(7, 12))
+        tt(T.Q[:], T.EC[:], T.PA[:, 2 * L:3 * L], A.not_equal, ["EC", "oP"], ["Q"], ["PA"])
+        op("V", lambda: v.tensor_tensor_scan(T.ES[:], T.EE[:], T.MS[:], 0.0, A.max, A.min), ["EE%d" % j for j in range(12)] + ["MS"], ["ES"])
+        tt(T.AM[:], T.Q[:], T.PH[:, L:2 * L], A.mult, ["Q", "hitM"], ["AM"], ["PH"])
+        tt(T.G1[:], T.AC[:], T.BC[:], A.is_gt, ["AC%d" % j for j in range(12)] + ["BC%d" % j for j in range(12)], ["G1"])
+        tt(T.OF[:], T.ES[:, 0:EL].indirect(T.END[:, 0:1]), T.OLF[:], A.max, ["ES", "END", "OLF"], ["OF"])
+        tt(T.G1[:], T.G1[:], T.DF[:], A.mult, ["G1", "DF"], ["G1"])
+        cp(T.OFO[:], T.OF[:, 0:12], ["OF"], ["OFO"])
+        tt(T.G1[:], T.G1[:], T.WLF[:], A.max, ["G1", "WLF"], ["G1"])
+        tt(T.PM[:, L:2 * L], T.RR[:, t:t + L], T.PH[:, 0:L], A.is_gt, ["RR", "hitN"], ["PMt"], ["PM", "PH"])
+        cp(T.OFW[:], T.G1[:], ["G1"], ["OFW"])
+        tt(T.PM[:, L:2 * L], T.DN[:], T.PM[:, L:2 * L], A.mult, ["DN", "PMt"], ["PMt"], ["PM"])
+        tt(T.MT[:, 0:4096].indirect(T.OFW[:, 0:12]), T.E4[:], T.AM[:], A.max, ["E4", "AM", "OFW"], ["MT"])
+        if last:
+            fb = ["PD", "PC", "PX1"]
+            top = NONE * 4096.0
+            for j in range(3):
+                c = slice(512 * j, 512 * j + 512)
+                act(T[fb[j]][:], T.MT[:, c], F.Relu, ["MT"], [fb[j]], [fb[j]], bias=top, scale=-1.0)
+                act(T[fb[j]][:], T[fb[j]][:], F.Identity, [fb[j]], [fb[j]], [fb[j]], bias=top, scale=-1.0)
+        else:
+            zn, nk = T["ZL%d" % t], "ZL%d" % t
+            act(T.ZR[:, 0:H], zn[:, 0:H], F.Relu, [nk], ["ZR0"], bias=23.0, scale=-1.0)
+            act(T.ZR[:, H:L], zn[:, H:L], F.Sign, [nk], ["ZR1"], bias=31.0, scale=-1.0)
+            act(T.ZT[:, 0:H], T.ZR[:, 0:H], F.Identity, ["ZR0"], ["ZT0"], bias=31.0, scale=-1.0)
+            act(T.ZT[:, H:L], T.ZR[:, H:L], F.Copy, ["ZR1"], ["ZT1"], scale=8.0)
+        tt(T.T3[:], T.NO[:], T.PM[:, L:2 * L], A.subtract, ["NO", "PMt"], ["T3"], ["PM"])
+        tt(T.AN[:], T.DA[:], T.PH[:, 0:L], A.min, ["DA", "hitN"], ["AN"], ["PH"])
+        tt(T.NT[:, 0:4096].indirect(T.OFO[:, 0:12]), T.T3[:], T.AN[:], A.max, ["T3", "AN", "OFO"], ["NT"])
+
+    fb = ["PD", "PC", "PX1"]
+    dma("S", T.yz[:], T["ZL%d" % (RO - 1)][:], "st", r=["ZL%d" % (RO - 1)])
+    for j in range(3):
+        c = slice(512 * j, 512 * j + 512)
+        tt(T.OUT[:, c], T.NT[:, c], T[fb[j]][:], A.add, ["NT", fb[j]], ["OUT%d" % j], [fb[j]])
+        dma("S", T.ynm[:, c], T.OUT[:, c], "st", r=["OUT%d" % j])
+    dma("A", T.yw[:], T["WL%d" % (RO - 1)][:], "st", r=["WL%d" % (RO - 1)])
+    need("G", list(cnt.items()) + [("sent", sent[0])])

@@ -4,10 +4,10 @@ W, L, RO, NR = 1536, 192, 4, 6
 NONE = W - 1
 EMPTY = 2559
 H = 96
-XS = 64
 SEG = [8 * a * (a + 1) + a for a in range(13)]
 EL = SEG[12]
 U = 32768.0
+REPS = (("PA", 0), ("PL", 128))
 
 f32, bf, f16, i32, u16 = "float32", "bfloat16", "float16", "int32", "uint16"
 SCRATCH = {}
@@ -36,8 +36,7 @@ for _t in range(RO):
     SCRATCH["ZL%d" % _t] = ("sbuf", [128, L], bf)
     SCRATCH["WO%d" % _t] = ("sbuf", [128, 12], u16 if _t < RO - 1 else f32)
     SCRATCH["WL%d" % _t] = ("sbuf", [128, 12], u16 if _t < RO - 1 else f32)
-SCRATCH["PA"] = ("psum", [128, 1024], bf)
-for _n in ["PD", "PC", "PX0", "PX1", "PL", "PM", "PH"]:
+for _n in ["PA", "PD", "PC", "PX0", "PX1", "PL", "PM", "PH"]:
     SCRATCH[_n] = ("psum", [128, 512], f32)
 
 SEMAPHORES = (["sV", "sA", "sP", "sG", "sent", "lw", "lz", "lt", "lx", "ln0", "ln1", "ln2", "st"]
@@ -211,6 +210,7 @@ def rank_program(g, core, T, topo):
                        ("IMb", -4096.0, H), ("If2", -18 * U, H)):
         act(T[name][0:n, :], T.ID[0:n, 0:n], F.Copy, ["ID"], [name], scale=c)
     code(T.IC[:], T.IO[:], ["IO"], ["IC"])
+    act(T.LR[0:1, :], T.IO[0:1, 0:L], F.Copy, ["IO"], ["LR"], scale=1.0 / 256)
 
     banks = ["PX0", "PX1", "PH"]
     magic = 1.5 * 2.0 ** 35
@@ -235,11 +235,19 @@ def rank_program(g, core, T, topo):
     def kcols(P, c, k):
         return P[0:H, 128 * c + k:128 * c + 128:16]
 
-    def eq_half(c, col, ok, ks):
-        for k in ks:
-            tt(kslot(T.EQ, c, k), kview(T.NG, c, k), T.PA[:, col + H * c:col + H * c + H], A.is_equal,
-               ["NG%d" % c, ok], ["EQ%d_%d" % (c, k)], ["PA"])
-            mm(kcols(T.PC, c, k), kslot(T.EQ, c, k), T.W1[:], True, True, ["EQ%d_%d" % (c, k), "W1"], ["PC%d" % c], "PC")
+    def four(src, col, k, c):
+        P, o = REPS[c]
+        for e in range(4):
+            mm(T[P][:, o + e:o + 4 * H:4], T.Ib[:], src[:, col + H * c:col + H * c + H], True, True, ["Ib", k], ["cP%d" % c], P)
+
+    def eq_half(c, js):
+        P, o = REPS[c]
+        for j in js:
+            s = (4 * c + j) * 4 * H
+            tt(T.EQ[:, s:s + 4 * H], T.NG[:, 1536 * c + j:1536 * c + 1536:4], T[P][:, o:o + 4 * H], A.is_equal,
+               ["NG%d" % c, "cP%d" % c], ["EQ%d_%d" % (c, j)], [P])
+            for e in range(4):
+                mm(kcols(T.PC, c, j + 4 * e), T.EQ[:, s + e:s + 4 * H:4], T.W1[:], True, True, ["EQ%d_%d" % (c, j), "W1"], ["PC%d" % c], "PC")
 
     def flag(c):
         cs = slice(128 * c, 128 * c + 128)
@@ -274,12 +282,13 @@ def rank_program(g, core, T, topo):
             act(T.JK[:, EL + SEG[j]:EL + SEG[j] + n], T.PX0[:, 0:n], F.Sign, ["CB", "BB"], ["BC%d" % j], ["PX0"], bias=T.BB[:, j:j + 1],
                 acc=T.BC[:, j:j + 1])
 
-    def x_update(t):
-        zo = T["ZO%d" % t]
-        tt(T.DX[:], T.PA[:, 0:L], zo[:], A.subtract, ["zP", "ZO%d" % t], ["DX"], ["PA"])
+    def x_step(t, z, zk):
+        tt(T.DX[:], z[:], T["ZO%d" % t][:], A.subtract, [zk, "ZO%d" % t], ["DX"])
         ts(T.CL[:], T.DX[:], -2.0, 2.0, A.max, A.min, ["DX"], ["CL"])
         tt(T.CM[:], T.CL[:], T.PM[:, 0:L], A.mult, ["CL", "miss"], ["CM"], ["PM"])
-        tt(T.XT[:, 0:4096].indirect(T.OFO[:, 0:12]), zo[:], T.CM[:], A.add, ["ZO%d" % t, "CM", "OFO"], ["XT"])
+
+    def x_update(t):
+        tt(T.XT[:, 0:4096].indirect(T.OFO[:, 0:12]), T["ZO%d" % t][:], T.CM[:], A.add, ["ZO%d" % t, "CM", "OFO"], ["XT"])
 
     sent = [0]
 
@@ -313,22 +322,22 @@ def rank_program(g, core, T, topo):
             ms(T.ZT[:, H:L], 8.0, ["ZT1"])
         else:
             x_update(t - 1)
-        act(T.XG[:, 16 * XS:1536], XTw.indirect(T.E16[:, XS:H]), F.Copy, ["XT", "E16"], ["XGa"])
         act(T.XG[:, 1536:3072], XTw.indirect(T.E16[:, H:L]), F.Copy, ["XT", "E16"], ["XG1"])
         code(T.NG[:, 1536:3072], NTw.indirect(T.E16[:, H:L]), ["NT", "E16"], ["NG1"])
         cp(T.WC[:], T.IC[:, 0:W].indirect(wl), ["IC", wk], ["WC"])
-        cp(T.PA[:, 0:L], z[:], [zk], ["zP"], ["PA"])
-        cp(T.PA[:, L:2 * L], T.WC[:], ["WC"], ["wP"], ["PA"])
-        cp(T.XG[:, 0:16 * XS], XTw.indirect(T.E16[:, 0:XS]), ["XT", "E16"], ["XG0"])
+        for e in range(2):
+            mm(T.PM[:, L + e:2 * L:2], T.Ib[:], z[:, 0:H], True, True, ["Ib", zk], ["PMt"], "PM")
+        four(T.WC, 0, "WC", 0)
+        four(T.WC, 0, "WC", 1)
+        cp(T.XG[:, 0:1536], XTw.indirect(T.E16[:, 0:H]), ["XT", "E16"], ["XG0"])
         ts(T.EF[:], MTw.indirect(wl), 1.0 / 4096, float(NONE), A.mult, A.min, ["MT", wk], ["EF"])
         mm(T.PD[0:H, 0:256], T.ONE[0:1, 0:H], T.CR[0:1, :], True, False, ["ONE", "CR"], ["PD"], "PD")
         for c in range(2):
             mm(T.PD[0:H, 128 * c:128 * c + 128], T.ZT[:, H * c:H * c + H], T.BOX[:], False, False, ["ZT%d" % c, "BOX"], ["PD"], "PD")
-        mm(T.PD[0:H, 128:256], T.EF[:, H:L], T.Ih[:], False, False, ["EF", "Ih"], ["PD"], "PD")
-        xk = ["XG0", "XGa"]
         for k in range(16):
-            mm(kcols(T.PD, 0, k), kview(T.XG, 0, k), T.Wm[:], False, False, xk + ["Wm"], ["PD"], "PD")
-        eq_half(0, L, "wP", range(16))
+            mm(kcols(T.PD, 0, k), kview(T.XG, 0, k), T.Wm[:], False, False, ["XG0", "Wm"], ["PD"], "PD")
+        mm(T.PD[0:H, 128:256], T.EF[:, H:L], T.Ih[:], False, False, ["EF", "Ih"], ["PD"], "PD")
+        eq_half(0, range(4))
 
         def diff(q):
             P = "PX%d" % (q % 2)
@@ -341,10 +350,12 @@ def rank_program(g, core, T, topo):
             P = "PX%d" % (q % 2)
             act(kslot(T.MX, 1, 4 * q, 4), T[P][:, 0:4 * H], F.Abs, [P], ["AB%d" % q], [P])
 
-        def maxes(ks):
-            for k in ks:
-                tt(kslot(T.MX, 0, k), kview(T.XG, 0, k), T.PA[:, 0:H], A.max, xk + ["zP"], ["MX%d" % k], ["PA"])
-                mm(kcols(T.PD, 0, k), kslot(T.MX, 0, k), T.W2[:], False, False, ["MX%d" % k, "W2"], ["PD"], "PD")
+        def maxes(js):
+            for j in js:
+                s = j * L
+                tt(T.MX[:, s:s + L], T.XG[:, j:1536:8], T.PM[:, L:2 * L], A.max, ["XG0", "PMt"], ["MX%d" % j], ["PM"])
+                for e in range(2):
+                    mm(kcols(T.PD, 0, j + 8 * e), T.MX[:, s + e:s + L:2], T.W2[:], False, False, ["MX%d" % j, "W2"], ["PD"], "PD")
 
         def sums(q):
             for k in range(4 * q, 4 * q + 4):
@@ -355,32 +366,43 @@ def rank_program(g, core, T, topo):
             ts(T.RS[:], T.KI[:], 0.0, 1e8, A.is_equal, A.mult, ["KI"], ["RS"])
             ts(T.RR[:], T.IA[:], 0.0, None, A.is_equal, None, ["IA"], ["RR"])
         diff(0)
-        maxes(range(8))
         diff(1)
-        maxes(range(8, 16))
-        mm(T.PD[0:H, 0:128], T.EF[:, 0:H], T.Ih[:], False, False, ["EF", "Ih"], ["PD"], "PD")
-        flag(0)
         absd(0)
         absd(1)
+        maxes(range(3))
         diff(2)
-        eq_half(1, L, "wP", range(4))
+        flag(0)
+        maxes(range(3, 6))
         diff(3)
         absd(2)
         absd(3)
+        maxes(range(6, 8))
+        mm(T.PD[0:H, 0:128], T.EF[:, 0:H], T.Ih[:], False, False, ["EF", "Ih"], ["PD"], "PD")
+        act(T.WB[:], T.IO[:, 0:W].indirect(wl), F.Copy, ["IO", wk], ["WB"])
         sums(0)
-        eq_half(1, L, "wP", range(4, 8))
+        eq_half(1, range(1))
         sums(1)
         weigh(0, "If1", False)
-        eq_half(1, L, "wP", range(8, 12))
+        eq_half(1, range(1, 2))
         sums(2)
-        eq_half(1, L, "wP", range(12, 14))
+        eq_half(1, range(2, 3))
         sums(3)
-        eq_half(1, L, "wP", range(14, 16))
+        eq_half(1, range(3, 4))
         flag(1)
         weigh(1, "If1", True)
-        act(T.WB[:], T.IO[:, 0:W].indirect(wl), F.Copy, ["IO", wk], ["WB"])
-        if t == 0:
-            act(T.LR[0:1, :], T.IO[0:1, 0:L], F.Copy, ["IO"], ["LR"], scale=1.0 / 256)
+        mm(T.PX0[:, 0:L], T.ID[:], T.WB[:], True, False, ["ID", "WB"], ["CB"], "PX0")
+        mm(T.PX0[:, 0:L], T.ONE[0:1, :], T.LR[0:1, :], False, True, ["ONE", "LR"], ["CB"], "PX0")
+        cp(T.WLF[:], wl, [wk], ["WLF"])
+        if t > 0:
+            op("V", lambda: v.tensor_reduce(T.SS[:, 0:1], T.PM[:, 400:416], AxisListType.X, A.add), ["wins"], ["SS0"], ["PM"])
+        tt(T.BA[:], T.C1[:], T.WLF[:], A.subtract, ["C1", "WLF"], ["BA"])
+        if t > 0:
+            cp(T.SI[:, 0:1], T.SS[:, 0:1], ["SS0"], ["SI"])
+        tt(T.BB[:], T.C2[:], T.WLF[:], A.subtract, ["C2", "WLF"], ["BB"])
+        if t > 0:
+            ts(T.SI[:, 1:2], T.SI[:, 0:1], 31, None, A.bitwise_and, None, ["SI"], ["SJ"])
+            first_cnt(range(5))
+        else:
             act(T.DL[:], T.DF[:], F.Copy, ["DF"], ["DL"])
             for j in range(12):
                 act(T.MS[:, SEG[j]:SEG[j] + 16], T.TRI[:], F.Copy, ["TRI", "MSf"], ["MS%d" % j], scale=4096.0)
@@ -391,7 +413,6 @@ def rank_program(g, core, T, topo):
         cp(T.U16[:], NTw.indirect(ol), ["NT", "OL"], ["U16"])
         code(T.OCL[:], T.PL[:, 0:12], ["PL0"], ["OCL"], ["PL"])
         code(T.NG[:, 0:1536], MTw.indirect(T.U16[:, 0:H]), ["MT", "U16"], ["NG0"], scaled=True)
-        act(T.NO[:], NTw.indirect(ol), F.Copy, ["NT", "OL"], ["NO"])
         code(T.NG[:, 1536:3072], MTw.indirect(T.U16[:, H:L]), ["MT", "U16"], ["NG1"], scaled=True)
         if last:
             ms(T.XT[:, NONE:W], 255.0, ["XT"])
@@ -399,23 +420,13 @@ def rank_program(g, core, T, topo):
         else:
             ts(T["ZO%d" % t][:], XTw.indirect(ol), 31.0, None, A.min, None, ["XT", "OL"], ["ZO%d" % t])
         send(t, "ZO%d" % t, "ZL%d" % t, "za%d" % t)
-        if t > 0:
-            op("V", lambda: v.tensor_reduce(T.SS[:, 0:1], T.PM[:, 400:416], AxisListType.X, A.add), ["wins"], ["SS0"], ["PM"])
+        cp(T.OLF[:, 0:12], T.PL[:, 0:12], ["PL0"], ["OLF"], ["PL"])
         cp(T.OC[:, 16:208], T.IC[:, 0:W].indirect(ol), ["IC", "OL"], ["OC"])
-        if t > 0:
-            cp(T.SI[:, 0:1], T.SS[:, 0:1], ["SS0"], ["SI"])
-        cp(T.WLF[:], wl, [wk], ["WLF"])
-        if t > 0:
-            ts(T.SI[:, 1:2], T.SI[:, 0:1], 31, None, A.bitwise_and, None, ["SI"], ["SJ"])
-        cp(T.PA[:, 2 * L:3 * L], T.OC[:, 16:208], ["OC"], ["oP"], ["PA"])
+        four(T.OC, 16, "OC", 0)
+        four(T.OC, 16, "OC", 1)
         if t > 0:
             ts(T.SS[:, 1:2], T.SI[:, 1:2], U, None, A.mult, None, ["SJ"], ["SS1"])
-        cp(T.OLF[:, 0:12], T.PL[:, 0:12], ["PL0"], ["OLF"], ["PL"])
-        if t > 0:
-            ts(T.THR[0:H, :], T.TH0[0:H, :], T.SS[0:H, 1:2], None, A.add, None, ["TH0", "SS1"], ["THR"])
         mm(T.PD[0:H, 0:256], T.ONE[0:1, 0:H], T.CR[0:1, :], True, False, ["ONE", "CR"], ["PD"], "PD")
-        mm(T.PX0[:, 0:L], T.ID[:], T.WB[:], True, False, ["ID", "WB"], ["CB"], "PX0")
-        mm(T.PX0[:, 0:L], T.ONE[0:1, :], T.LR[0:1, :], False, True, ["ONE", "LR"], ["CB"], "PX0")
         if t == 0:
             cp(T.OC[:, 15:16], T.IC[:, NONE:W], ["IC"], ["OCv"])
             cp(T.T1[:, 3:4], T.TH[:], ["TH"], ["T13"])
@@ -425,34 +436,36 @@ def rank_program(g, core, T, topo):
         tt(T.DN[:], NTw.indirect(ol), T.WB[:], A.subtract, ["NT", "OL", "WB"], ["DN"])
         if t == 0:
             ts(T.TH0[0:H, :], T.PL[0:H, 64:80], -498 * U, None, A.add, None, ["PLt"], ["TH0"], ["PL"])
+        else:
+            ts(T.THR[0:H, :], T.TH0[0:H, :], T.SS[0:H, 1:2], None, A.add, None, ["TH0", "SS1"], ["THR"])
         mm(T.PL[0:H, 32:48], T.ONE[0:1, 0:H], T.CK[0:1, :], True, False, ["ONE", "CK"], ["FB"], "PL")
         for c in range(2):
             mm(T.PL[0:H, 32 + 8 * c:40 + 8 * c], T.WB[:, H * c:H * c + H], T.Wf[:], False, c == 1, ["WB", "Wf"], ["FB"], "PL")
         thk = "TH0" if t == 0 else "THR"
-        tt(T.BA[:], T.C1[:], T.WLF[:], A.subtract, ["C1", "WLF"], ["BA"])
-        tt(T.BB[:], T.C2[:], T.WLF[:], A.subtract, ["C2", "WLF"], ["BB"])
+        first_cmp(range(1))
         tt(T.HT[0:H, :], T.SC[0:H, 15:256:16], T[thk][0:H, :], A.is_lt, ["SC", thk], ["HT"])
-        first_cmp(range(2))
+        first_cmp(range(1, 8))
         for k in range(16):
             mm(kcols(T.PD, 0, k), kview(T.NG, 0, k), T.Wm[:], False, False, ["NG0", "Wm"], ["PD"], "PD")
-        eq_half(0, 2 * L, "oP", range(8))
-        for c in range(2):
-            mm(T.PD[0:H, 128 * c:128 * c + 128], T.NO[:, H * c:H * c + H], T.ID[:], False, False, ["NO", "ID"], ["PD"], "PD")
-        eq_half(0, 2 * L, "oP", range(8, 16))
-        first_cmp(range(2, 7))
+        eq_half(0, range(4))
+        first_cmp(range(8, 12))
         flag(0)
         for k in range(16):
             mm(kcols(T.PD, 1, k), kview(T.NG, 1, k), T.Wm[:], False, False, ["NG1", "Wm"], ["PD"], "PD")
         weigh(0, "If2", False)
+        act(T.NO[:], NTw.indirect(ol), F.Copy, ["NT", "OL"], ["NO"])
         act(T.HA[:], T.HT[:, 0:16].indirect(T.REP[:, 0:16]), F.Copy, ["HT", "REP"], ["HA"])
-        eq_half(1, 2 * L, "oP", range(16))
+        eq_half(1, range(1))
+        for c in range(2):
+            mm(T.PD[0:H, 128 * c:128 * c + 128], T.NO[:, H * c:H * c + H], T.ID[:], False, False, ["NO", "ID"], ["PD"], "PD")
+        eq_half(1, range(1, 4))
         code(T.EC[:], MTw.indirect(wl), ["MT", wk], ["EC"], scaled=True)
-        act(T.E4[:], MTw.indirect(wl), F.Copy, ["MT", wk], ["E4"])
-        first_cnt(range(2))
         flag(1)
         weigh(1, "If2", True)
-        first_cnt(range(2, 12))
+        act(T.E4[:], MTw.indirect(wl), F.Copy, ["MT", wk], ["E4"])
+        first_cnt(range(5 if t > 0 else 0, 12))
         act(T.DA[:], T.DN[:], F.Abs, ["DN"], ["DA"], scale=2048.0)
+        op("V", lambda: v.tensor_tensor_scan(T.ES[:], T.EE[:], T.MS[:], 0.0, A.max, A.min), ["EE%d" % j for j in range(12)] + ["MS"], ["ES"])
         for c in range(2):
             ha, cs = T.HA[0:H, 128 * c:128 * c + 128], slice(H * c, H * c + H)
             mm(T.PH[:, cs], ha, T.I15[0:H, :], True, False, ["HA", "I15"], ["hitN"], "PH")
@@ -468,21 +481,21 @@ def rank_program(g, core, T, topo):
                 mm(T.PM[:, cs], ha, T.nI[0:H, 0:H], False, True, ["HA", "nI"], ["miss"], "PM")
         if not last:
             mm(T.PM[:, 400:416], T.ONE[0:H, :], T.HT[0:H, :], True, True, ["ONE", "HT"], ["wins"], "PM")
+        tt(T.OF[:], T.ES[:, 0:EL].indirect(T.END[:, 0:1]), T.OLF[:], A.max, ["ES", "END", "OLF"], ["OF"])
         cp(T["WO%d" % t][:], T.PL[:, 16:28], ["PL16"], ["WO%d" % t], ["PL"])
         send(t, "WO%d" % t, "WL%d" % t, "wa%d" % t)
         arrival(t)
-        first_cmp(range(7, 12))
-        tt(T.Q[:], T.EC[:], T.PA[:, 2 * L:3 * L], A.not_equal, ["EC", "oP"], ["Q"], ["PA"])
-        op("V", lambda: v.tensor_tensor_scan(T.ES[:], T.EE[:], T.MS[:], 0.0, A.max, A.min), ["EE%d" % j for j in range(12)] + ["MS"], ["ES"])
-        tt(T.AM[:], T.Q[:], T.PH[:, L:2 * L], A.mult, ["Q", "hitM"], ["AM"], ["PH"])
-        tt(T.G1[:], T.AC[:], T.BC[:], A.is_gt, ["AC%d" % j for j in range(12)] + ["BC%d" % j for j in range(12)], ["G1"])
-        tt(T.OF[:], T.ES[:, 0:EL].indirect(T.END[:, 0:1]), T.OLF[:], A.max, ["ES", "END", "OLF"], ["OF"])
-        tt(T.G1[:], T.G1[:], T.DF[:], A.mult, ["G1", "DF"], ["G1"])
+        tt(T.Q[:], T.EC[:], T.OC[:, 16:208], A.not_equal, ["EC", "OC"], ["Q"])
         cp(T.OFO[:], T.OF[:, 0:12], ["OF"], ["OFO"])
-        tt(T.G1[:], T.G1[:], T.WLF[:], A.max, ["G1", "WLF"], ["G1"])
+        tt(T.AM[:], T.Q[:], T.PH[:, L:2 * L], A.mult, ["Q", "hitM"], ["AM"], ["PH"])
         tt(T.PM[:, L:2 * L], T.RR[:, t:t + L], T.PH[:, 0:L], A.is_gt, ["RR", "hitN"], ["PMt"], ["PM", "PH"])
-        cp(T.OFW[:], T.G1[:], ["G1"], ["OFW"])
+        tt(T.G1[:], T.AC[:], T.BC[:], A.is_gt, ["AC%d" % j for j in range(12)] + ["BC%d" % j for j in range(12)], ["G1"])
         tt(T.PM[:, L:2 * L], T.DN[:], T.PM[:, L:2 * L], A.mult, ["DN", "PMt"], ["PMt"], ["PM"])
+        tt(T.G1[:], T.G1[:], T.DF[:], A.mult, ["G1", "DF"], ["G1"])
+        tt(T.T3[:], T.NO[:], T.PM[:, L:2 * L], A.subtract, ["NO", "PMt"], ["T3"], ["PM"])
+        tt(T.G1[:], T.G1[:], T.WLF[:], A.max, ["G1", "WLF"], ["G1"])
+        tt(T.AN[:], T.DA[:], T.PH[:, 0:L], A.min, ["DA", "hitN"], ["AN"], ["PH"])
+        cp(T.OFW[:], T.G1[:], ["G1"], ["OFW"])
         tt(T.MT[:, 0:4096].indirect(T.OFW[:, 0:12]), T.E4[:], T.AM[:], A.max, ["E4", "AM", "OFW"], ["MT"])
         if last:
             fb = ["PD", "PC", "PX1"]
@@ -497,9 +510,9 @@ def rank_program(g, core, T, topo):
             act(T.ZR[:, H:L], zn[:, H:L], F.Sign, [nk], ["ZR1"], bias=31.0, scale=-1.0)
             act(T.ZT[:, 0:H], T.ZR[:, 0:H], F.Identity, ["ZR0"], ["ZT0"], bias=31.0, scale=-1.0)
             act(T.ZT[:, H:L], T.ZR[:, H:L], F.Copy, ["ZR1"], ["ZT1"], scale=8.0)
-        tt(T.T3[:], T.NO[:], T.PM[:, L:2 * L], A.subtract, ["NO", "PMt"], ["T3"], ["PM"])
-        tt(T.AN[:], T.DA[:], T.PH[:, 0:L], A.min, ["DA", "hitN"], ["AN"], ["PH"])
         tt(T.NT[:, 0:4096].indirect(T.OFO[:, 0:12]), T.T3[:], T.AN[:], A.max, ["T3", "AN", "OFO"], ["NT"])
+        if not last:
+            x_step(t, z, zk)
 
     fb = ["PD", "PC", "PX1"]
     dma("S", T.yz[:], T["ZL%d" % (RO - 1)][:], "st", r=["ZL%d" % (RO - 1)])

@@ -2,45 +2,59 @@ from concourse.mybir import AluOpType as A, AxisListType, ActivationFunctionType
 
 W, L, RO, NR = 1536, 192, 4, 6
 NONE = W - 1
-EMPTY = 2559
 H = 96
-SEG = [8 * a * (a + 1) + a for a in range(13)]
-EL = SEG[12]
+TOP = 2047
+OFF = 4096.0 * TOP
+JUNK, DUMP = 1536, 1600
+PAD = 8
 U = 32768.0
-REPS = (("PA", 0), ("PL", 128))
+BIG = 2.0 ** 99
+SLOPE = 23.0 / 512
+WIDE = 2048
 
 f32, bf, f16, i32, u16 = "float32", "bfloat16", "float16", "int32", "uint16"
 SCRATCH = {}
 for _n, _c, _d in [
-    ("NM", W, i32), ("NT", 4096, f32), ("MT", 4096, f32), ("XT", 4096, bf), ("FT", W, f32), ("OUT", W, f32),
-    ("IO", W, f32), ("IC", W, bf), ("NG", 3072, bf), ("XG", 3072, bf), ("MX", 3072, bf), ("EQ", 3072, bf),
-    ("W32", 12, i32), ("TH", 1, i32), ("Z0", L, bf), ("WI", 12, u16),
-    ("IA", 272, i32), ("RR", 272, f32), ("PI", 2, i32), ("PJ", 2, i32), ("PF", 4, f32),
-    ("CI", 128, f32), ("KI", 256, f32), ("GI", 128, f32), ("RS", 256, f32), ("CR", 256, bf), ("CK", 16, bf), ("LR", L, bf),
-    ("ONE", 128, bf), ("ID", 128, f32), ("Ih", 128, f16), ("Ib", 128, bf), ("nI", 128, bf), ("I15", H, bf), ("IMa", H, bf),
-    ("IMb", H, bf), ("If1", H, bf), ("If2", H, bf), ("BOX", 128, bf), ("W1", 8, bf), ("W2", 8, bf), ("Wm", 8, bf),
-    ("Wp", 8, bf), ("Wf", 8, f32), ("Wt", 8, bf), ("BOh", 8, f16), ("REP", 16, u16), ("END", 2, u16), ("LL", 12, f32),
-    ("DF", 12, f32), ("C1", 12, f32), ("C2", 12, f32), ("BA", 12, f32), ("BB", 12, f32),
-    ("AC", 12, f32), ("BC", 12, f32), ("JK", 2 * EL, bf), ("G1", 12, f32),
-    ("DL", 12, bf), ("TRI", 16, f32), ("MS", EL, bf), ("T1", 4, f32), ("THB", H, bf), ("TH0", 16, f32), ("THR", 16, f32),
-    ("E16", L, u16), ("U16", L, u16), ("EF", L, f16), ("WC", L, bf), ("OC", 208, bf), ("ZT", L, bf), ("ZR", L, bf),
-    ("FL", 256, bf), ("SC", 256, f32), ("S32", 16, i32), ("O32", 16, i32), ("OA", 256, f16), ("OL", 12, u16),
-    ("OLF", 16, f32), ("WLF", 12, f32), ("OCL", 12, bf), ("HT", 16, bf), ("HA", 256, bf), ("WB", L, f32),
-    ("EE", EL, bf), ("ES", EL, bf), ("OF", 16, f32), ("OFO", 12, u16), ("OFW", 12, u16),
-    ("E4", L, f32), ("EC", L, bf), ("NO", L, f32), ("DN", L, f32), ("DA", L, f32), ("Q", L, bf), ("AM", L, f32), ("AN", L, f32),
-    ("T3", L, f32), ("DX", L, bf), ("CL", L, bf), ("CM", L, bf), ("SS", 2, f32), ("SI", 2, i32),
+    ("NM", W, i32), ("NT", WIDE, f32), ("MT", WIDE + PAD, f32), ("XT", WIDE, bf), ("FT", W, f32), ("OUT", W, f32),
+    ("IO", WIDE, f32), ("NG", 3072, bf), ("MG", 3072, bf), ("XG", 3072, bf), ("MX", 3072, bf), ("EQ", 3072, bf),
+    ("W32", 12, i32), ("TH", 1, i32), ("Z0", L, bf), ("WI", 16, u16),
+    ("IA", 208, i32), ("RN", 208, bf), ("PI", 2, i32), ("PJ", 4, i32), ("PF", 4, f32),
+    ("CI", 128, f32), ("KI", 128, f32), ("GI", 128, f32), ("RS", 128, f32), ("CR", 128, bf), ("CK", 8, f32), ("ZERO", 32, bf),
+    ("ONE", 128, bf), ("ONF", 128, f32), ("UF", 128, f32), ("HLF", 2, bf),
+    ("ID", 128, f32), ("Ih", 128, f16), ("Ib", 128, bf), ("nI", 128, bf), ("IB", H, bf),
+    ("If1", H, bf), ("If2", H, bf), ("BOX", 128, bf), ("W1", 8, bf), ("W2", 8, bf), ("Wm", 8, bf),
+    ("Wp", 8, bf), ("Wf", 8, f32), ("Wt", 8, bf), ("EXB", 128, bf), ("EXN", 128, bf), ("SEL", 240, f16), ("SI", 16, f32),
+    ("P2", H, f32), ("HF", H + 12, f32), ("TP", H, f32),
+    ("CV", 12, u16), ("CF", 12, f32), ("BI", 48, f32), ("MK", 48, f32), ("MD", L, f32), ("WT", 12, bf),
+    ("TC", 32, f32), ("T1", 8, f32), ("THB", H, bf), ("TH0", 16, f32), ("TH1", 16, f32), ("THR", 16, f32),
+    ("E16", L, u16), ("U16", L, u16), ("EF", L, f16), ("UH", L, f16), ("WC", L, bf), ("OC", L, bf), ("ZR", L, bf),
+    ("FL", 256, bf), ("SC", 256, f32), ("S32", 16, i32), ("O32", 16, i32), ("OA", 96, f16), ("OL", 12, u16),
+    ("IDL", 24, f32), ("CL2", 24, bf), ("MS", 16, bf), ("HR", L, bf), ("WIN", 2, f32), ("WB", L, f32), ("OB", L, f32),
+    ("EE", 18 * H, bf), ("FF", 32, bf), ("OD", L, f16), ("OF", 24, f32), ("OFU", 24, u16),
+    ("DN", L, f32), ("KN", L, f32), ("Q", L, f32), ("CL", L, bf), ("CM", L, bf), ("SS", 2, f32),
 ]:
     SCRATCH[_n] = ("sbuf", [128, _c], _d)
 for _t in range(RO):
     SCRATCH["ZO%d" % _t] = ("sbuf", [128, L], bf)
     SCRATCH["ZL%d" % _t] = ("sbuf", [128, L], bf)
-    SCRATCH["WO%d" % _t] = ("sbuf", [128, 12], u16 if _t < RO - 1 else f32)
+    SCRATCH["WO%d" % _t] = ("sbuf", [128, 16], u16 if _t < RO - 1 else f32)
     SCRATCH["WL%d" % _t] = ("sbuf", [128, 12], u16 if _t < RO - 1 else f32)
-for _n in ["PA", "PD", "PC", "PX0", "PX1", "PL", "PM", "PH"]:
+for _n in ["PD0", "PD1", "PC", "CB0", "CB1", "PX0", "PX1", "PS"]:
     SCRATCH[_n] = ("psum", [128, 512], f32)
 
 SEMAPHORES = (["sV", "sA", "sP", "sG", "sent", "lw", "lz", "lt", "lx", "ln0", "ln1", "ln2", "st"]
-              + ["za%d" % t for t in range(RO)] + ["wa%d" % t for t in range(RO)])
+              + ["%s%d" % (s, t) for t in range(RO) for s in ("za", "wa", "wb")])
+PIECES = (("za", "Z", 0, L, 0), ("wa", "W", 0, 6, 0), ("wb", "W", 6, 12, 8))
+SENDS = (0, 1, 2)
+
+ORDER = """
+load wc0 kpow e0 tabN +intw1 +od +cutN2 +loww1 sameo1 +out0 kx +putX samew0 diffb absN0 kkeys ef1 +cl eqN0d +cutN1 +listw1 +kn oc0 gX0 +of listo1 gap1
+diffa sameo2 flagN0 scano0 tabM0 gap0 +thr +cm fourz open0 e1 gap2 fourw1 fourw0 eqN0c +wo1 tabM1 +send2 gN0 +ofu +absN2 +cutM0 diffc maxd wc1 wb zr
+maxb +cutM2 ef0 gX1 eqN0a dx +cutM1 idw gN1 +out1 putN maxc kpick +outw eqN0b maxa tabM2 +ss addE0 clw diffd open1 sumX listo0 absb eqN1c intw0 absN1
+absa into0 eqN1b sameo0 putM lowo0 zo eqN1d ol0 into1 eqN1a miss1 u0 addE1 samew1 absd samew2 sameo4 outz loww0 rows lowo1 absc flagN1 ob0 kth scano1
+ido0 gM0 back0 samew3 openS flagM0 samew4 ol1 ob1 kdump oc1 fouro0 ido1 miss0 uh0 sumM0 samew5 fouro1 u1 eqM0a eqM0c send1 cutN0 eqM0d clo back1 uh1
+sameo3 gM1 eqM0b sumM1 hit eqM1b eqM1c scanw0 sameo5 scanw1 listw0 eqM1d eqM1a wo0 krow q dn flagM1 ff out2 send0
+""".split()
 
 
 def route(T, topo, r, t):
@@ -67,9 +81,11 @@ def relay_program(g, core, T, topo):
             if via != core:
                 continue
             n = len(topo.engines(src, core))
-            for buf, sem in (("ZL%d" % t, "za%d" % t), ("WL%d" % t, "wa%d" % t)):
-                g.wait_ge(T.sem[sem], n)
-                sent += put(g, T, topo, core, dst, T[buf][:], T[buf][:], sem)
+            for p in SENDS:
+                sem, buf, lo, hi, _ = PIECES[p]
+                ap = T["%sL%d" % (buf, t)][:, lo:hi]
+                g.wait_ge(T.sem["%s%d" % (sem, t)], n)
+                sent += put(g, T, topo, core, dst, ap, ap, "%s%d" % (sem, t))
     if sent:
         g.wait_ge(T.sem.sent, sent)
 
@@ -80,56 +96,80 @@ def rank_program(g, core, T, topo):
         relay_program(g, core, T, topo)
         return
     Q = {"V": g.vector, "A": g.scalar, "P": g.tensor, "G": g, "S": g.sync}
-    cnt = {}
-    waited = {q: {} for q in Q}
-    lastw, readers, bank = {}, {}, {}
+    calls = []
+    lastw, readers = {}, {}
+    now = [0, ""]
+    sent = [0]
 
-    def need(q, toks):
-        best = {}
-        for s, n in toks:
-            best[s] = max(best.get(s, 0), n)
-        for s, n in best.items():
-            if waited[q].get(s, 0) < n:
-                Q[q].wait_ge(T.sem[s], n)
-                waited[q][s] = n
+    def step(name):
+        now[1] = name
 
-    def order(q, r, w, b):
-        own = "s" + q
-        toks = []
+    def record(q, fn, sem, inc, r, w, b=(), after=()):
+        pre = set(after)
         for k in r:
-            if k in lastw:
-                toks.append(lastw[k])
+            pre.add(lastw[k])
         for k in w:
             if k in lastw:
-                toks.append(lastw[k])
-            toks.extend(readers.get(k, {}).items())
-        for k in b:
-            toks.extend((s, n) for s, n in bank.get(k, {}).items() if s != own)
-        if q == "P":
-            toks = [x for x in toks if x[0] != own]
-        need(q, toks)
-
-    def note(tok, r, w, b):
+                pre.add(lastw[k])
+            pre.update(readers.get(k, ()))
+        me = len(calls)
+        calls.append((q, fn, sem, inc, tuple(b), tuple(now), sorted(pre)))
         for k in r:
-            readers.setdefault(k, {})[tok[0]] = tok[1]
+            readers.setdefault(k, []).append(me)
         for k in w:
-            lastw[k] = tok
-            readers[k] = {}
-        for k in b:
-            bank.setdefault(k, {})[tok[0]] = tok[1]
+            lastw[k] = me
+            readers[k] = []
+        return me
 
-    def op(q, fn, r=(), w=(), b=()):
-        order(q, r, w, b)
-        s = "s" + q
-        cnt[s] = cnt.get(s, 0) + 1
-        fn().then_inc(T.sem[s], 1)
-        note((s, cnt[s]), r, w, b)
+    def op(q, fn, r=(), w=(), b=(), after=()):
+        return record(q, fn, "s" + q, 1, r, w, b, after)
 
     def dma(q, out, in_, sem, r=(), w=()):
-        order(q, r, w, ())
-        cnt[sem] = cnt.get(sem, 0) + 16
-        Q[q].dma_start(out, in_).then_inc(T.sem[sem], 16)
-        note((sem, cnt[sem]), r, w, ())
+        record(q, lambda: Q[q].dma_start(out, in_), sem, 16, r, w)
+
+    def issue():
+        place = {name.lstrip("+"): i + len(ORDER) * name.count("+") for i, name in enumerate(ORDER)}
+        nxt = [[] for _ in calls]
+        for i, c in enumerate(calls):
+            for p in c[6]:
+                nxt[p].append(i)
+        left = [len(c[6]) for c in calls]
+        turn = [(c[5][0] * len(ORDER) + place.get(c[5][1], 0), i) for i, c in enumerate(calls)]
+        ready = [i for i in range(len(calls)) if not left[i]]
+        cnt, tok, bank = {}, {}, {}
+        waited = {q: {} for q in Q}
+        while ready:
+            i = min(ready, key=lambda j: turn[j])
+            ready.remove(i)
+            q, fn, sem, inc, banks_, _, pre = calls[i]
+            for j in nxt[i]:
+                left[j] -= 1
+                if not left[j]:
+                    ready.append(j)
+            if q == "R":
+                tok[i] = (sem, inc)
+                continue
+            toks = [tok[p] for p in pre if tok[p]] + [x for k in banks_ for x in bank.get(k, {}).items() if x[0] != sem]
+            most = {}
+            for sm, m in toks:
+                if not (q == "P" and sm == sem):
+                    most[sm] = max(most.get(sm, 0), m)
+            for sm, m in most.items():
+                if waited[q].get(sm, 0) < m:
+                    Q[q].wait_ge(T.sem[sm], m)
+                    waited[q][sm] = m
+            if sem is None:
+                fn()
+                tok[i] = None
+                continue
+            cnt[sem] = cnt.get(sem, 0) + inc
+            fn().then_inc(T.sem[sem], inc)
+            tok[i] = (sem, cnt[sem])
+            for k in banks_:
+                bank.setdefault(k, {})[sem] = cnt[sem]
+        for sm, m in list(cnt.items()) + [("sent", sent[0])]:
+            if waited["G"].get(sm, 0) < m:
+                g.wait_ge(T.sem[sm], m)
 
     v, a = g.vector, g.scalar
 
@@ -148,11 +188,23 @@ def rank_program(g, core, T, topo):
     def ms(out, c, w, b=()):
         op("V", lambda: v.memset(out, c), (), w, b)
 
+    def scan(out, d0, d1, first_, o0, o1, r, w, b=()):
+        op("V", lambda: v.tensor_tensor_scan(out, d0, d1, first_, o0, o1), r, w, b)
+
+    def total(out, in_, r, w):
+        op("V", lambda: v.tensor_reduce(out, in_, AxisListType.X, A.add), r, w)
+
     def act(out, in_, f, r, w, b=(), bias=0.0, scale=1.0, acc=None):
         op("A", lambda: a.activation(out, in_, f, bias=bias, scale=scale, accum_out=acc), r, w, b)
 
-    def mm(out, lhsT, rhs, start, stop, r, w, b):
-        op("P", lambda: g.tensor.matmul(out, lhsT, rhs, start, stop), r, w, [b])
+    def mm(out, lhsT, rhs, start, stop, r, w, b, after=()):
+        if start and stop:
+            r = list(r) + ["shut" + b] if "shut" + b in lastw else r
+        elif start or stop:
+            w = list(w) + ["open" + b, "shut" + b]
+        else:
+            r, w = list(r) + ["open" + b], []
+        return op("P", lambda: g.tensor.matmul(out, lhsT, rhs, start, stop), r, w, [b], after)
 
     def iota(out, pat, base, cm, w, fl=True):
         if fl:
@@ -160,365 +212,380 @@ def rank_program(g, core, T, topo):
         else:
             op("G", lambda: g.iota(out, pat, base, cm), (), w)
 
-    def code(out, in_, r, w, b=(), scaled=False):
-        act(out, in_, F.Exp, r, w, b, bias=-EMPTY / 32.0, scale=(1.0 / 32 / 4096 if scaled else 1.0 / 32))
+    def mcode(out, in_, r, w):
+        act(out, in_, F.Sigmoid, r, w, bias=7.0, scale=SLOPE / 4096)
 
-    NTw, MTw, XTw = T.NT[:, 0:W], T.MT[:, 0:W], T.XT[:, 0:W]
+    def ncode(out, in_, r, w, off=OFF):
+        act(out, in_, F.Sigmoid, r, w, bias=-off / 32 - 80.0, scale=1.0 / 32)
 
+    NTw, MTw, XTw, IOw = T.NT[:, 0:WIDE], T.MT[:, PAD:PAD + WIDE], T.XT[:, 0:WIDE], T.IO[:, 0:WIDE]
+
+    def hs(c, n=H):
+        return slice(n * c, n * c + n)
+
+    step("load")
     dma("S", T.NM[:, 0:512], T.nm[:, 0:512], "ln0", w=["NM0"])
     dma("A", T.NM[:, 512:1024], T.nm[:, 512:1024], "ln1", w=["NM1"])
     dma("S", T.NM[:, 1024:W], T.nm[:, 1024:W], "ln2", w=["NM2"])
     dma("A", T.W32[:], T.w[:], "lw", w=["W32"])
-    dma("S", XTw, T.x[:], "lx", w=["XT"])
+    dma("S", T.XT[:, 0:W], T.x[:], "lx", w=["XT"])
     dma("A", T.Z0[:], T.z[:], "lz", w=["Z0"])
     dma("S", T.TH[:], T.th[:], "lt", w=["TH"])
 
     iota(T.PI[:], [[0, 2]], 0, 1, ["PI"], False)
     iota(T.CI[:], [[1, 128]], 0, 0, ["CI"])
-    iota(T.IO[:], [[1, W]], 0, 0, ["IO"])
+    iota(T.IO[:, 0:W], [[1, W]], 0, 0, ["IO"])
+    iota(T.NT[:, W:WIDE], [[0, WIDE - W]], int(NONE + OFF), 0, ["NTt"])
     iota(T.GI[:], [[1, 8], [0, 16]], 0, 0, ["GI"])
-    iota(T.KI[:], [[0, 16], [1, 16]], 0, 0, ["KI"])
-    iota(T.IA[:], [[1, 272]], 128, -1, ["IA"], False)
-    pf, pm, pg = T.PF[:, 0:1], T.PF[:, 1:2], T.PF[:, 2:3]
+    iota(T.KI[:], [[0, 8], [1, 16]], 0, 0, ["KI"])
+    iota(T.MT[:, PAD + W:PAD + WIDE], [[0, WIDE - W]], 0, 0, ["MTu"])
+    iota(T.BI[:], [[1, 6], [0, 8]], 0, 0, ["BI"])
+    iota(T.CF[:], [[8, 4], [0, 3]], 0, 0, ["CF"])
+    iota(T.IA[:], [[1, 208]], 128, -1, ["IA"], False)
+    iota(T.EE[:], [[0, 18 * H]], 0, 0, ["EEz"])
+    pf, pm, pg, p8 = T.PF[:, 0:1], T.PF[:, 1:2], T.PF[:, 2:3], T.PF[:, 3:4]
+    ms(T.IO[:, W:WIDE], float(JUNK), ["IOt"])
+    ms(T.XT[:, W:WIDE], 39.0, ["XTt"])
     ms(T.ONE[:], 1.0, ["ONE"])
-    ms(T.O32[:], 0, ["O32"])
-    ms(T.HT[:], 0.0, ["HT"])
-    ms(T.OLF[:], 0.0, ["OLF"])
-    ms(T.CK[0:1, :], -17 * U, ["CK"])
-    ms(T.MS[:], 4096.0, ["MSf"])
+    ms(T.O32[:], 0, ["O320", "O321"])
+    ms(T.FF[:], 0.0, ["FF"])
+    ms(T.ZERO[0:1, :], 0.0, ["ZERO"])
+    ms(T.CK[0:1, :], PAD - OFF - 17 * U, ["CK"])
+    ms(T.ONF[0:1, :], 1.0, ["ONF"])
+    ms(T.UF[0:8, :], U, ["UF"])
+    ms(T.HLF[0:1, :], -15.5 * U, ["HLF"])
+    ms(T.MT[:, 0:PAD], 0.0, ["MTt"])
+    ms(T.CR[0:2, :], -496 * U, ["CR"])
+    ms(T.SEL[:], 0.0, ["SEL"])
+    ms(T.HF[:, 0:H], 0.5, ["HFa"])
+    ms(T.HF[:, H:H + 12], 2.0 ** -16, ["HFb"])
     ts(T.PJ[:, 0:1], T.PI[:, 0:1], 15, None, A.bitwise_and, None, ["PI"], ["PJ0"])
     ts(T.PJ[:, 1:2], T.PI[:, 0:1], 4, None, A.logical_shift_right, None, ["PI"], ["PJ1"])
+    ts(T.PJ[:, 2:3], T.PI[:, 0:1], 7, None, A.bitwise_and, None, ["PI"], ["PJ2"])
     cp(pf, T.PI[:, 0:1], ["PI"], ["pf"])
-    cp(T.PF[:, 1:3], T.PJ[:], ["PJ0", "PJ1"], ["pm"])
+    cp(T.PF[:, 1:4], T.PJ[:, 0:3], ["PJ0", "PJ1", "PJ2"], ["pm"])
     ts(T.ID[:], T.CI[:], pf, None, A.is_equal, None, ["CI", "pf"], ["ID"])
-    for name, c in (("W1", 1.0), ("W2", 2 * U), ("Wm", -U), ("Wp", U), ("Wf", 1.0 / 16), ("Wt", U / 16), ("BOh", 1.0)):
+    for name, c in (("W1", 1.0), ("W2", 2 * U), ("Wm", -U), ("Wp", U), ("Wt", U / 16)):
         ts(T[name][:], T.CI[:, 0:8], pg, c, A.is_equal, A.mult, ["CI", "pm"], [name])
+    cp(T.Wf[:], T.ID[:, 0:128:16], ["ID"], ["Wf"])
     cp(T.Ih[:], T.ID[:], ["ID"], ["Ih"])
-    cp(T.REP[:], T.CI[:, 0:16], ["CI"], ["REP"])
-    ts(T.TRI[:], T.CI[:, 0:16], pm, 15.0, A.add, A.is_gt, ["CI", "pm"], ["TRI"])
-    ts(T.LL[:], T.CI[:, 0:12], 16.0, pm, A.mult, A.add, ["CI", "pm"], ["LL"])
-    ts(T.T1[:, 0:1], pm, 1.5, None, A.add, None, ["pm"], ["T10"])
-    ts(T.BA[:], T.LL[:], 8.0, 1536.0, A.mult, A.add, ["LL"], ["BA"])
-    ts(T.BB[:], T.LL[:], 16.0, 1024.0, A.mult, A.add, ["LL"], ["BB"])
-    tt(T.T1[:, 1:2], T.T1[:, 0:1], T.T1[:, 0:1], A.mult, ["T10"], ["T11"])
-    tt(T.DF[:], T.BA[:], T.BB[:], A.max, ["BA", "BB"], ["DF"])
-    ts(T.T1[:, 2:3], T.T1[:, 1:2], 8.0, pm, A.mult, A.add, ["T11", "pm"], ["T12"])
-    ts(T.C1[:], T.LL[:], -1.0 / 256, 0.875, A.mult, A.add, ["LL"], ["C1"])
-    ts(T.C2[:], T.LL[:], -1.0 / 256, 1.0 / 512, A.mult, A.add, ["LL"], ["C2"])
-    ts(T.END[:, 0:1], T.T1[:, 2:3], 2.0, float(EL - 1), A.subtract, A.min, ["T12"], ["END"])
-    for name, c, n in (("If1", -370 * U, H), ("Ib", 1.0, 128), ("nI", -1.0, 128), ("I15", 1536.0, H), ("IMa", 2560 * 4096.0, H),
-                       ("IMb", -4096.0, H), ("If2", -18 * U, H)):
+    ts(T.SI[:], T.CI[:, 0:16], pm, None, A.is_equal, None, ["CI", "pm"], ["SI"])
+    cp(T.SEL[:, 112:128], T.SI[:], ["SI"], ["SEL"])
+    for name, c, n in (("Ib", 1.0, 128), ("nI", -1.0, 128), ("If1", -370 * U, H), ("If2", -18 * U, H), ("IB", BIG, H)):
         act(T[name][0:n, :], T.ID[0:n, 0:n], F.Copy, ["ID"], [name], scale=c)
-    code(T.IC[:], T.IO[:], ["IO"], ["IC"])
-    act(T.LR[0:1, :], T.IO[0:1, 0:L], F.Copy, ["IO"], ["LR"], scale=1.0 / 256)
+    cp(T.WI[:, 0:12], T.W32[:], ["W32"], ["WI_0", "WI_1"])
 
-    banks = ["PX0", "PX1", "PH"]
+    banks = ["PX0", "PX1", "PS"]
+    whole = [["PX0", "miss"], ["PX1", "dx", "wins"], ["PS", "PO"]]
     magic = 1.5 * 2.0 ** 35
+    gap = float(TOP - NONE)
     for j in range(3):
-        c = slice(512 * j, 512 * j + 512)
-        ts(T[banks[j]][:], T.NM[:, c], magic, magic, A.add, A.subtract, ["NM%d" % j], ["M4%d" % j], [banks[j]])
-        tt(T.NT[:, c], T.NM[:, c], T[banks[j]][:], A.subtract, ["NM%d" % j, "M4%d" % j], ["NT%d" % j], [banks[j]])
-        act(T.FT[:, c], T[banks[j]][:], F.Relu, ["M4%d" % j], ["FT%d" % j], [banks[j]], bias=-(NONE - 1) * 2.0 ** 22, scale=1024.0)
-        if j == 0:
-            ts(T.BOX[:], T.GI[:], pg, -U, A.is_equal, A.mult, ["GI", "pm"], ["BOX"])
-            ts(T.CR[0:1, :], T.KI[0:1, :], 2048.0, None, A.mult, None, ["KI"], ["CR"])
-    lastw["NT"] = lastw["NT2"]
-    cp(T.WI[:], T.W32[:], ["W32"], ["WI"])
+        c = hs(j, 512)
+        step("tabN")
+        ts(T[banks[j]][:], T.NM[:, c], magic, magic + OFF, A.add, A.subtract, ["NM%d" % j], whole[j], [banks[j]])
+        tt(T.NT[:, c], T.NM[:, c], T[banks[j]][:], A.subtract, ["NM%d" % j] + whole[j], ["NT"], [banks[j]])
+        step("gap%d" % j)
+        act(T.FT[:, c], T[banks[j]][:], F.Relu, whole[j], ["FT%d" % j], [banks[j]], bias=(gap + 1) * gap * 4096, scale=gap)
+        step("tabM%d" % j)
+        tt(T.MT[:, PAD + 512 * j:PAD + 512 * j + 512], T.FT[:, c], T[banks[j]][:], A.add, ["FT%d" % j, "MTt", "MTu"] + whole[j], ["MT"], [banks[j]])
+    step("kx")
+    ms(T.XT[:, NONE:W], 39.0, ["XT"])
+    step("kkeys")
+    ts(T.BOX[:], T.GI[:], pg, U, A.is_equal, A.mult, ["GI", "pm"], ["BOX"])
+    ts(T.CR[0:1, :], T.KI[0:1, :], 2048.0, None, A.mult, None, ["KI"], ["CR"])
+    step("kpick")
+    ts(T.RS[:], T.KI[:], 0.0, 1e8, A.is_equal, A.mult, ["KI"], ["RS"])
+    ts(T.CV[:], T.CF[:], p8, None, A.add, None, ["CF", "pm"], ["CV"])
+    ts(T.MK[:], T.BI[:], pg, None, A.is_equal, None, ["BI", "pm"], ["MK"])
+    step("kpow")
+    scan(T.P2[:], T.HF[:, 0:H], T.ONE[:, 0:H], 2.0 ** 97, A.mult, A.mult, ["HFa", "ONE"], ["P2"])
+    tt(T.TP[:, 0:16], T.P2[:, 0:16], T.SI[:], A.mult, ["P2", "SI"], ["TP"])
+    total(T.T1[:, 4:5], T.TP[:, 0:16], ["TP"], ["T14"])
+    tt(T.TP[:], T.P2[:], T.ID[:, 0:H], A.mult, ["P2", "ID"], ["TP"])
+    ts(T.T1[:, 5:6], T.T1[:, 4:5], 65536.0, None, A.mult, None, ["T14"], ["T15"])
+    total(T.T1[:, 2:3], T.TP[:], ["TP"], ["T12"])
+    scan(T.WT[:], T.HF[:, H:H + 12], T.ONE[:, 0:12], T.T1[:, 5:6], A.mult, A.mult, ["HFb", "ONE", "T15"], ["WT"])
+    step("kth")
+    cp(T.T1[:, 3:4], T.TH[:], ["TH"], ["T13"])
+    ts(T.THB[:], T.ONE[:, 0:H], T.T1[:, 3:4], None, A.mult, None, ["ONE", "T13"], ["THB"])
+    for c in range(2):
+        mm(T.PC[0:H, 256 + 8 * c:264 + 8 * c], T.THB[:], T.Wt[:], True, True, ["THB", "Wt"], ["PLt"], "PC")
+    ts(T.TH0[0:H, :], T.PC[0:H, 256:272], -498 * U, None, A.add, None, ["PLt"], ["TH0"], ["PC"])
+    ts(T.TH1[0:H, :], T.PC[0:H, 256:272], -482.5 * U, None, A.add, None, ["PLt"], ["TH1"], ["PC"])
+    step("krow")
+    ts(T.IA[:], T.IA[:], 15, None, A.bitwise_and, None, ["IA"], ["IA"])
+    ts(T.RN[:], T.IA[:], 0.0, None, A.not_equal, None, ["IA"], ["RN"])
+    ts(T.EXB[0:8, :], T.GI[0:8, :], T.PF[0:8, 0:1], 4096.0, A.is_equal, A.mult, ["GI", "pf"], ["EXB"])
+    ts(T.EXN[0:8, :], T.GI[0:8, :], T.PF[0:8, 0:1], -1.0, A.is_equal, A.mult, ["GI", "pf"], ["EXN"])
+    step("kdump")
+    for c in range(2):
+        ts(T.T1[:, c:c + 1], pf, float(DUMP + H * c), None, A.add, None, ["pf"], ["T1%d" % c])
+    for c in range(2):
+        for lst in range(2):
+            s = 2 * lst + c
+            ts(T.MD[:, hs(s, 48)], T.MK[:], T.T1[:, c:c + 1], None, A.mult, None, ["MK", "T1%d" % c], ["MD%d" % s])
+            ts(T.TC[0:H, hs(s, 8)], T.ONE[0:H, 0:8], T.T1[0:H, 2:3], 2.5 * 2.0 ** (-H * c), A.mult, A.mult, ["ONE", "T12"], ["TC%d" % s])
+    four_ = ["0", "1", "2", "3"]
 
     def kview(buf, c, k):
         return buf[:, 1536 * c + k:1536 * c + 1536:16]
 
-    def kslot(buf, c, k, n=1):
-        s = (16 * c + k) * H
-        return buf[:, s:s + n * H]
+    def kcols(P, k, o=0):
+        return P[0:H, o + k:o + 128:16]
 
-    def kcols(P, c, k):
-        return P[0:H, 128 * c + k:128 * c + 128:16]
-
-    def four(src, col, k, c):
-        P, o = REPS[c]
+    def four(src, key, c, bank_):
         for e in range(4):
-            mm(T[P][:, o + e:o + 4 * H:4], T.Ib[:], src[:, col + H * c:col + H * c + H], True, True, ["Ib", k], ["cP%d" % c], P)
+            mm(T[bank_][:, e:4 * H:4], T.Ib[:], src[:, hs(c)], True, True, ["Ib", key], [bank_], bank_)
 
-    def eq_half(c, js):
-        P, o = REPS[c]
-        for j in js:
+    def eq(G, c, I):
+        P = "CB%d" % c
+        for j in range(4):
+            step("eq%s%d%s" % (G[0], c, "abcd"[j]))
             s = (4 * c + j) * 4 * H
-            tt(T.EQ[:, s:s + 4 * H], T.NG[:, 1536 * c + j:1536 * c + 1536:4], T[P][:, o:o + 4 * H], A.is_equal,
-               ["NG%d" % c, "cP%d" % c], ["EQ%d_%d" % (c, j)], [P])
+            tt(T.EQ[:, s:s + 4 * H], T[G][:, 1536 * c + j:1536 * c + 1536:4], T[P][:, 0:4 * H], A.is_equal,
+               ["%s%d" % (G, c), P], ["EQ%d_%d" % (c, j)], [P])
             for e in range(4):
-                mm(kcols(T.PC, c, j + 4 * e), T.EQ[:, s + e:s + 4 * H:4], T.W1[:], True, True, ["EQ%d_%d" % (c, j), "W1"], ["PC%d" % c], "PC")
+                mm(kcols(T.PC, j + 4 * e, 128 * c), T.EQ[:, s + e:s + 4 * H:4], T.W1[:], True, True, ["EQ%d_%d" % (c, j), "W1"], ["PC%d%d" % (c, j)], "PC")
+        step("flag%s%d" % (G[0], c))
+        cs, P = hs(c, 128), "PD%d" % c
+        act(T.FL[0:H, cs], T.PC[0:H, cs], F.Sign, ["PC%d%d" % (c, j) for j in range(4)], ["FL%d" % c], ["PC"])
+        mm(T[P][0:H, 0:128], T[I][0:H, :], T.FL[0:H, cs], False, True, [I, "FL%d" % c], [P], P)
 
-    def flag(c):
-        cs = slice(128 * c, 128 * c + 128)
-        act(T.FL[0:H, cs], T.PC[0:H, cs], F.Sign, ["PC%d" % c], ["FL%d" % c], ["PC"])
+    def keys_open(c, rows):
+        P = "PD%d" % c
+        mm(T[P][0:H, 0:128], T.ONE[0:rows, 0:H], T.CR[0:rows, :], True, False, ["ONE", "CR"], [P], P)
 
-    def weigh(c, I, stop):
-        cs = slice(128 * c, 128 * c + 128)
-        mm(T.PD[0:H, cs], T[I][0:H, :], T.FL[0:H, cs], False, stop, [I, "FL%d" % c], ["PD"], "PD")
+    def keys_add(c, src, key, rhs, after=()):
+        P = "PD%d" % c
+        return mm(T[P][0:H, 0:128], src[:, hs(c)], T[rhs][:], False, False, [key, rhs], [P], P, after)
 
-    def pick(col, fallback):
-        op("V", lambda: v.tensor_tensor_scan(T.SC[0:H, :], T.RS[0:H, :], T.PD[0:H, 0:256], 0.0, A.add, A.min), ["RS", "PD"], ["SC"], ["PD"])
-        if fallback:
-            tt(T.S32[0:H, :], T.SC[0:H, 15:256:16], T.PL[0:H, 32:48], A.min, ["SC", "FB"], ["S32"], ["PL"])
+    def keys_sum(c, view, key, rhs, ks=range(16)):
+        P = "PD%d" % c
+        return [mm(kcols(T[P], k), view(k), T[rhs][:], False, False, [key, rhs], [P], P) for k in ks]
+
+    def to_list(out, src, lo, hi, key, w, P):
+        for gg in range(8):
+            mm(out, T.SEL[0:H, 112 - 16 * gg:240 - 16 * gg], src[0:H, lo + gg:hi:8], gg == 0, gg == 7, [key, "SEL"], [w], P)
+
+    def pick(c, tag):
+        P, cs, g8 = "PD%d" % c, hs(c, 128), hs(c, 8)
+        step("scan" + tag)
+        scan(T.SC[0:H, cs], T.RS[0:H, :], T[P][0:H, 0:128], 0.0, A.add, A.min, ["RS", P], ["SC%d" % c], [P])
+        step("int" + tag)
+        least = T.SC[0:H, 128 * c + 15:128 * c + 128:16]
+        if tag[0] == "w":
+            tt(T.S32[0:H, g8], least, T[P][0:H, 144:152], A.min, ["SC%d" % c, "FB%d" % c], ["S32%d" % c], [P])
         else:
-            cp(T.S32[0:H, :], T.SC[0:H, 15:256:16], ["SC"], ["S32"])
-        ts(T.O32[0:H, :], T.S32[0:H, :], 2047, None, A.bitwise_and, None, ["S32"], ["O32"])
-        tt(T.OA[:], T.O32[:, 0:16].indirect(T.REP[:, 0:16]), T.RR[:, 0:256], A.mult, ["O32", "REP", "RR"], ["OA"])
-        for c in range(2):
-            mm(T.PL[:, col + 6 * c:col + 6 * c + 6], T.OA[0:H, 128 * c:128 * c + 128], T.BOh[0:H, 0:6], True, True,
-               ["OA", "BOh"], ["PL%d" % col], "PL")
+            cp(T.S32[0:H, g8], least, ["SC%d" % c], ["S32%d" % c])
+        step("low" + tag)
+        ts(T.O32[0:H, g8], T.S32[0:H, g8], 2047, None, A.bitwise_and, None, ["S32%d" % c], ["O32%d" % c])
+        step("list" + tag)
+        tt(T.OA[:, hs(c, 48)], T.O32[:, g8].indirect(T.CV[:, 0:3]), T.MK[:], A.mult, ["O32%d" % c, "CV", "MK"], ["OA%d" % c])
+        to_list(T[P][:, 128:134], T.OA, 48 * c, 48 * c + 48, "OA%d" % c, "PL%d" % c, P)
 
-    def first_cmp(js):
-        for j in js:
-            ts(T.EE[:, SEG[j]:SEG[j + 1]], T.OC[:, 16 * j + 31:14:-1], T.OCL[:, j:j + 1], T.DL[:, j:j + 1], A.is_equal, A.mult,
-               ["OC", "OCv", "OCL", "DL"], ["EE%d" % j])
+    def first(src, keys, lst):
+        for b in range(12):
+            step("same%s%d" % ("ow"[lst], b // 2))
+            lo, s0 = 16 * b, (2 * b if b < 6 else 5 + b) * H
+            ts(T.EE[:, s0 + lo:s0 + L], src[:, lo:L], T.CL2[:, 12 * lst + b:12 * lst + b + 1], T.WT[:, b:b + 1], A.is_equal, A.mult,
+               keys + ["WT", "EEz"], ["EE%d" % b])
+            for c in range(0 if b < 6 else 1, 2):
+                o = 16 * lst + 8 * c
+                mm(T.PS[0:H, o:o + 8], T.EE[:, s0 + H * c:s0 + H * c + H], T.W1[:], False, lst == 0 and b == 11, ["EE%d" % b, "W1"], ["PS"], "PS")
 
-    def first_cnt(js):
-        for j in js:
-            n = 16 * j + 16
-            act(T.JK[:, SEG[j]:SEG[j] + n], T.PX0[:, 0:n], F.Sign, ["CB", "BA"], ["AC%d" % j], ["PX0"], bias=T.BA[:, j:j + 1],
-                acc=T.AC[:, j:j + 1])
-            act(T.JK[:, EL + SEG[j]:EL + SEG[j] + n], T.PX0[:, 0:n], F.Sign, ["CB", "BB"], ["BC%d" % j], ["PX0"], bias=T.BB[:, j:j + 1],
-                acc=T.BC[:, j:j + 1])
-
-    def x_step(t, z, zk):
-        tt(T.DX[:], z[:], T["ZO%d" % t][:], A.subtract, [zk, "ZO%d" % t], ["DX"])
-        ts(T.CL[:], T.DX[:], -2.0, 2.0, A.max, A.min, ["DX"], ["CL"])
-        tt(T.CM[:], T.CL[:], T.PM[:, 0:L], A.mult, ["CL", "miss"], ["CM"], ["PM"])
-
-    def x_update(t):
-        tt(T.XT[:, 0:4096].indirect(T.OFO[:, 0:12]), T["ZO%d" % t][:], T.CM[:], A.add, ["ZO%d" % t, "CM", "OFO"], ["XT"])
-
-    sent = [0]
-
-    def send(t, buf, land, sem):
+    def send(t, p, key):
+        sem, buf, lo, hi, o = PIECES[p]
+        name = "%s%d" % (sem, t)
         src, via, dst = route(T, topo, rank, t)
-        need("G", [lastw[buf]])
-        sent[0] += put(g, T, topo, src, dst if via is None else via, T[land][:], T[buf][:], sem)
-
-    def arrival(t):
-        src, via, dst = route(T, topo, (rank - 1 - t % (NR - 1)) % NR, t)
-        n = len(topo.engines(src if via is None else via, dst))
-        lastw["ZL%d" % t] = ("za%d" % t, n)
-        lastw["WL%d" % t] = ("wa%d" % t, n)
+        to = dst if via is None else via
+        sent[0] += len(topo.engines(src, to))
+        step("send%d" % p)
+        me = record("G", lambda: put(g, T, topo, src, to, T["%sL%d" % (buf, t)][:, lo:hi], T["%sO%d" % (buf, t)][:, o:o + hi - lo], name),
+                    None, 0, [key], ["sends"])
+        far, relay, here = route(T, topo, (rank - 1 - t % (NR - 1)) % NR, t)
+        record("R", None, name, len(topo.engines(far if relay is None else relay, here)), [], [("ZL%d", "WL%d_0", "WL%d_1")[p] % t], (), [me])
 
     for t in range(RO):
+        now[0] = t
         last = t == RO - 1
         wk, zk = ("WI", "Z0") if t == 0 else ("WL%d" % (t - 1), "ZL%d" % (t - 1))
         wl, z = T[wk][:, 0:12], T[zk]
-        if t == 0:
-            ts(T.E16[:], T.NM[:, 0:W].indirect(wl), 1.0 / 4096, None, A.mult, None, ["NM0", "NM1", "NM2", wk], ["E16"])
-        else:
-            ts(T.E16[:], MTw.indirect(wl), 1.0 / 4096, float(NONE), A.mult, A.min, ["MT", wk], ["E16"])
-        code(T.NG[:, 0:1536], NTw.indirect(T.E16[:, 0:H]), ["NT", "E16"], ["NG0"])
-        if t == 0:
-            ms(T.XT[:, NONE:W], 39.0, ["XT"])
-            for j in range(3):
-                c = slice(512 * j, 512 * j + 512)
-                tt(T.MT[:, c], T.FT[:, c], T[banks[j]][:], A.add, ["FT%d" % j, "M4%d" % j], ["MT%d" % j], [banks[j]])
-            lastw["MT"] = lastw["MT2"]
-            ts(T.ZT[:, 0:H], z[:, 0:H], 8.0, None, A.add, None, [zk], ["ZT0"])
-            ms(T.ZT[:, H:L], 8.0, ["ZT1"])
-        else:
-            x_update(t - 1)
-        act(T.XG[:, 1536:3072], XTw.indirect(T.E16[:, H:L]), F.Copy, ["XT", "E16"], ["XG1"])
-        code(T.NG[:, 1536:3072], NTw.indirect(T.E16[:, H:L]), ["NT", "E16"], ["NG1"])
-        cp(T.WC[:], T.IC[:, 0:W].indirect(wl), ["IC", wk], ["WC"])
-        for e in range(2):
-            mm(T.PM[:, L + e:2 * L:2], T.Ib[:], z[:, 0:H], True, True, ["Ib", zk], ["PMt"], "PM")
-        four(T.WC, 0, "WC", 0)
-        four(T.WC, 0, "WC", 1)
-        cp(T.XG[:, 0:1536], XTw.indirect(T.E16[:, 0:H]), ["XT", "E16"], ["XG0"])
-        ts(T.EF[:], MTw.indirect(wl), 1.0 / 4096, float(NONE), A.mult, A.min, ["MT", wk], ["EF"])
-        mm(T.PD[0:H, 0:256], T.ONE[0:1, 0:H], T.CR[0:1, :], True, False, ["ONE", "CR"], ["PD"], "PD")
+        wks = [wk + "_0", wk + "_1"]
+        ZO, zo = T["ZO%d" % t], "ZO%d" % t
+        step("zr")
+        act(T.ZR[:], z[:], F.Relu, [zk], ["ZR"], bias=23.0, scale=-1.0)
+        step("wb")
+        act(T.WB[:], IOw.indirect(wl), F.Identity, ["IO", "IOt"] + wks, ["WB"], bias=OFF)
+        step("idw")
+        cp(T.IDL[:, 12:24], wl, wks, ["IDw"])
+        step("clw")
+        ncode(T.CL2[:, 12:24], T.IDL[:, 12:24], ["IDw"], ["CLw"], off=0.0)
         for c in range(2):
-            mm(T.PD[0:H, 128 * c:128 * c + 128], T.ZT[:, H * c:H * c + H], T.BOX[:], False, False, ["ZT%d" % c, "BOX"], ["PD"], "PD")
-        for k in range(16):
-            mm(kcols(T.PD, 0, k), kview(T.XG, 0, k), T.Wm[:], False, False, ["XG0", "Wm"], ["PD"], "PD")
-        mm(T.PD[0:H, 128:256], T.EF[:, H:L], T.Ih[:], False, False, ["EF", "Ih"], ["PD"], "PD")
-        eq_half(0, range(4))
-
-        def diff(q):
-            P = "PX%d" % (q % 2)
-            for k in range(4):
-                o = T[P][:, H * k:H * k + H]
-                mm(o, T.Ib[:], kview(T.XG, 1, 4 * q + k), True, False, ["Ib", "XG1"], [P], P)
-                mm(o, T.nI[:], z[:, H:L], False, True, ["nI", zk], [P], P)
-
-        def absd(q):
-            P = "PX%d" % (q % 2)
-            act(kslot(T.MX, 1, 4 * q, 4), T[P][:, 0:4 * H], F.Abs, [P], ["AB%d" % q], [P])
-
-        def maxes(js):
-            for j in js:
-                s = j * L
-                tt(T.MX[:, s:s + L], T.XG[:, j:1536:8], T.PM[:, L:2 * L], A.max, ["XG0", "PMt"], ["MX%d" % j], ["PM"])
-                for e in range(2):
-                    mm(kcols(T.PD, 0, j + 8 * e), T.MX[:, s + e:s + L:2], T.W2[:], False, False, ["MX%d" % j, "W2"], ["PD"], "PD")
-
-        def sums(q):
-            for k in range(4 * q, 4 * q + 4):
-                mm(kcols(T.PD, 1, k), kslot(T.MX, 1, k), T.Wp[:], False, False, ["AB%d" % q, "Wp"], ["PD"], "PD")
-
-        if t == 0:
-            ts(T.IA[:], T.IA[:], 15, None, A.bitwise_and, None, ["IA"], ["IA"])
-            ts(T.RS[:], T.KI[:], 0.0, 1e8, A.is_equal, A.mult, ["KI"], ["RS"])
-            ts(T.RR[:], T.IA[:], 0.0, None, A.is_equal, None, ["IA"], ["RR"])
-        diff(0)
-        diff(1)
-        absd(0)
-        absd(1)
-        maxes(range(3))
-        diff(2)
-        flag(0)
-        maxes(range(3, 6))
-        diff(3)
-        absd(2)
-        absd(3)
-        maxes(range(6, 8))
-        mm(T.PD[0:H, 0:128], T.EF[:, 0:H], T.Ih[:], False, False, ["EF", "Ih"], ["PD"], "PD")
-        act(T.WB[:], T.IO[:, 0:W].indirect(wl), F.Copy, ["IO", wk], ["WB"])
-        sums(0)
-        eq_half(1, range(1))
-        sums(1)
-        weigh(0, "If1", False)
-        eq_half(1, range(1, 2))
-        sums(2)
-        eq_half(1, range(2, 3))
-        sums(3)
-        eq_half(1, range(3, 4))
-        flag(1)
-        weigh(1, "If1", True)
-        mm(T.PX0[:, 0:L], T.ID[:], T.WB[:], True, False, ["ID", "WB"], ["CB"], "PX0")
-        mm(T.PX0[:, 0:L], T.ONE[0:1, :], T.LR[0:1, :], False, True, ["ONE", "LR"], ["CB"], "PX0")
-        cp(T.WLF[:], wl, [wk], ["WLF"])
-        if t > 0:
-            op("V", lambda: v.tensor_reduce(T.SS[:, 0:1], T.PM[:, 400:416], AxisListType.X, A.add), ["wins"], ["SS0"], ["PM"])
-        tt(T.BA[:], T.C1[:], T.WLF[:], A.subtract, ["C1", "WLF"], ["BA"])
-        if t > 0:
-            cp(T.SI[:, 0:1], T.SS[:, 0:1], ["SS0"], ["SI"])
-        tt(T.BB[:], T.C2[:], T.WLF[:], A.subtract, ["C2", "WLF"], ["BB"])
-        if t > 0:
-            ts(T.SI[:, 1:2], T.SI[:, 0:1], 31, None, A.bitwise_and, None, ["SI"], ["SJ"])
-            first_cnt(range(5))
-        else:
-            act(T.DL[:], T.DF[:], F.Copy, ["DF"], ["DL"])
-            for j in range(12):
-                act(T.MS[:, SEG[j]:SEG[j] + 16], T.TRI[:], F.Copy, ["TRI", "MSf"], ["MS%d" % j], scale=4096.0)
-            lastw["MS"] = lastw["MS11"]
-        pick(0, False)
-        cp(T.OL[:], T.PL[:, 0:12], ["PL0"], ["OL"], ["PL"])
-        ol = T.OL[:, 0:12]
-        cp(T.U16[:], NTw.indirect(ol), ["NT", "OL"], ["U16"])
-        code(T.OCL[:], T.PL[:, 0:12], ["PL0"], ["OCL"], ["PL"])
-        code(T.NG[:, 0:1536], MTw.indirect(T.U16[:, 0:H]), ["MT", "U16"], ["NG0"], scaled=True)
-        code(T.NG[:, 1536:3072], MTw.indirect(T.U16[:, H:L]), ["MT", "U16"], ["NG1"], scaled=True)
+            wc, k, P = T[wk][:, hs(c, 6)], wks[c], "PD%d" % c
+            step("e%d" % c)
+            if t == 0:
+                ts(T.E16[:, hs(c)], T.NM[:, 0:W].indirect(wc), 1.0 / 4096, None, A.mult, None, ["NM0", "NM1", "NM2", k], ["E16%d" % c])
+            else:
+                ts(T.E16[:, hs(c)], MTw.indirect(wc), 1.0 / 4096, float(TOP), A.mult, A.add, ["MT", k], ["E16%d" % c])
+            step("wc%d" % c)
+            ncode(T.WC[:, hs(c)], IOw.indirect(wc), ["IO", "IOt", k], ["WC%d" % c], off=0.0)
+            step("gN%d" % c)
+            ncode(T.NG[:, hs(c, 1536)], NTw.indirect(T.E16[:, hs(c)]), ["NT", "NTt", "E16%d" % c], ["NG%d" % c])
+            step("gX%d" % c)
+            if c == 0:
+                cp(T.XG[:, hs(c, 1536)], XTw.indirect(T.E16[:, hs(c)]), ["XT", "XTt", "E16%d" % c], ["XG%d" % c])
+            else:
+                act(T.XG[:, hs(c, 1536)], XTw.indirect(T.E16[:, hs(c)]), F.Copy, ["XT", "XTt", "E16%d" % c], ["XG%d" % c])
+            step("open%d" % c)
+            keys_open(c, 2)
+            wide = [keys_add(c, T.ZR, "ZR", "BOX")]
+            if c == 0:
+                step("fourz")
+                four(z, zk, 0, "CB1")
+                step("sumX")
+                wide += keys_sum(0, lambda k_: kview(T.XG, 0, k_), "XG0", "Wm")
+                for j in range(4):
+                    step("max" + "abcd"[j])
+                    s = j * 4 * H
+                    tt(T.MX[:, s:s + 4 * H], T.XG[:, j:1536:4], T.CB1[:, 0:4 * H], A.max, ["XG0", "CB1"], ["MX%d" % j], ["CB1"])
+                    for e in range(4):
+                        wide.append(mm(kcols(T.PD0, j + 4 * e), T.MX[:, s + e:s + 4 * H:4], T.W2[:], False, False, ["MX%d" % j, "W2"], [P], P))
+            else:
+                wide.append(keys_add(1, z, zk, "BOX"))
+                for q in range(4):
+                    X, keys = "PX%d" % (q % 2), whole[q % 2][0:2]
+                    step("diff" + "abcd"[q])
+                    for e in range(4):
+                        o = T[X][:, H * e:H * e + H]
+                        mm(o, T.Ib[:], kview(T.XG, 1, 4 * q + e), True, False, ["Ib", "XG1"], keys, X)
+                        mm(o, T.nI[:], z[:, H:L], False, True, ["nI", zk], keys, X)
+                    step("abs" + "abcd"[q])
+                    s = 1536 + 4 * H * q
+                    act(T.MX[:, s:s + 4 * H], T[X][:, 0:4 * H], F.Abs, keys, ["AB%d" % q], [X])
+                    keys_sum(1, lambda k_: T.MX[:, 1536 + H * k_:1536 + H * k_ + H], "AB%d" % q, "Wp", range(4 * q, 4 * q + 4))
+            step("ef%d" % c)
+            if t == 0:
+                ts(T.EF[:, hs(c)], MTw.indirect(wc), 1.0 / 4096, float(TOP), A.mult, A.add, ["MT", k], ["EF%d" % c])
+            else:
+                cp(T.EF[:, hs(c)], T.E16[:, hs(c)], ["E16%d" % c], ["EF%d" % c])
+            step("addE%d" % c)
+            keys_add(c, T.EF, "EF%d" % c, "Ih", wide)
+            step("fourw%d" % c)
+            four(T.WC, "WC%d" % c, c, "CB%d" % c)
+            eq("NG", c, "If1")
+            pick(c, "o%d" % c)
+            ol, k = T.OL[:, hs(c, 6)], "OL%d" % c
+            step("ol%d" % c)
+            cp(ol, T[P][:, 128:134], ["PL%d" % c], [k], [P])
+            step("u%d" % c)
+            ts(T.U16[:, hs(c)], NTw.indirect(ol), PAD - OFF, float(NONE + PAD), A.add, A.min, ["NT", k], ["U16%d" % c])
+            step("ob%d" % c)
+            act(T.OB[:, hs(c)], IOw.indirect(ol), F.Identity, ["IO", "IOt", k], ["OB%d" % c], bias=-OFF, scale=4096.0)
+            step("oc%d" % c)
+            mcode(T.OC[:, hs(c)], T.OB[:, hs(c)], ["OB%d" % c], ["OC%d" % c])
+            step("ido%d" % c)
+            ts(T.IDL[:, hs(c, 6)], T[P][:, 128:134], float(JUNK), None, A.min, None, ["PL%d" % c], ["IDo%d" % c], [P])
+            step("miss%d" % c)
+            thk = "TH0" if t == 0 else "THR"
+            tt(T.MS[0:H, hs(c, 8)], T.SC[0:H, 128 * c + 15:128 * c + 128:16], T[thk][0:H, hs(c, 8)], A.is_ge, ["SC%d" % c, thk], ["MS%d" % c])
+        ol, olk = T.OL[:, 0:12], ["OL0", "OL1"]
+        step("zo")
         if last:
-            ms(T.XT[:, NONE:W], 255.0, ["XT"])
-            cp(T["ZO%d" % t][:], XTw.indirect(ol), ["XT", "OL"], ["ZO%d" % t])
+            ms(T.XT[:, TOP:TOP + 1], 255.0, ["XT"])
+            cp(ZO[:], XTw.indirect(ol), ["XT"] + olk, [zo])
         else:
-            ts(T["ZO%d" % t][:], XTw.indirect(ol), 31.0, None, A.min, None, ["XT", "OL"], ["ZO%d" % t])
-        send(t, "ZO%d" % t, "ZL%d" % t, "za%d" % t)
-        cp(T.OLF[:, 0:12], T.PL[:, 0:12], ["PL0"], ["OLF"], ["PL"])
-        cp(T.OC[:, 16:208], T.IC[:, 0:W].indirect(ol), ["IC", "OL"], ["OC"])
-        four(T.OC, 16, "OC", 0)
-        four(T.OC, 16, "OC", 1)
-        if t > 0:
-            ts(T.SS[:, 1:2], T.SI[:, 1:2], U, None, A.mult, None, ["SJ"], ["SS1"])
-        mm(T.PD[0:H, 0:256], T.ONE[0:1, 0:H], T.CR[0:1, :], True, False, ["ONE", "CR"], ["PD"], "PD")
-        if t == 0:
-            cp(T.OC[:, 15:16], T.IC[:, NONE:W], ["IC"], ["OCv"])
-            cp(T.T1[:, 3:4], T.TH[:], ["TH"], ["T13"])
-            ts(T.THB[:], T.ONE[:, 0:H], T.T1[:, 3:4], None, A.mult, None, ["ONE", "T13"], ["THB"])
+            ts(ZO[:], XTw.indirect(ol), 31.0, None, A.min, None, ["XT"] + olk, [zo])
+        for c in range(2):
+            P = "PD%d" % c
+            step("gM%d" % c)
+            mcode(T.MG[:, hs(c, 1536)], T.MT[:, 0:WIDE].indirect(T.U16[:, hs(c)]), ["MT", "U16%d" % c], ["MG%d" % c])
+            step("back%d" % c)
+            mm(T[P][0:H, 144:152], T.ONF[0:1, 0:H], T.CK[0:1, :], True, False, ["ONF", "CK"], ["FB%d" % c], P)
+            mm(T[P][0:H, 144:152], T.WB[:, hs(c)], T.Wf[:], False, True, ["WB", "Wf"], ["FB%d" % c], P)
+            keys_open(c, 1)
+            step("fouro%d" % c)
+            four(T.OC, "OC%d" % c, c, "CB%d" % c)
+            step("uh%d" % c)
+            cp(T.UH[:, hs(c)], T.U16[:, hs(c)], ["U16%d" % c], ["UH%d" % c])
+            keys_add(c, T.UH, "UH%d" % c, "Ih")
+            step("sumM%d" % c)
+            keys_sum(c, lambda k_: kview(T.MG, c, k_), "MG%d" % c, "Wm")
+            eq("MG", c, "If2")
+            pick(c, "w%d" % c)
+            step("wo%d" % c)
+            ts(T["WO%d" % t][:, 8 * c:8 * c + 6], T[P][:, 128:134], float(PAD), None, A.subtract, None, ["PL%d" % c], ["WO%d_%d" % (t, c)], [P])
+        for p in SENDS:
+            send(t, p, (zo, "WO%d_0" % t, "WO%d_1" % t)[p])
+        step("openS")
+        mm(T.PS[0:H, 0:32], T.ONE[0:1, 0:H], T.ZERO[0:1, :], True, False, ["ONE", "ZERO"], ["PS"], "PS")
+        first(T.WC, ["WC0", "WC1", "CLw"], 1)
+        step("clo")
+        act(T.CL2[:, 0:12], T.IDL[:, 0:12], F.Sigmoid, ["IDo0", "IDo1"], ["CLo"], bias=7.0 - TOP * SLOPE, scale=SLOPE)
+        step("rows")
+        for c in range(2):
+            mm(T.PS[0:H, 16 + 8 * c:24 + 8 * c], T.IB[0:H, :], T.MS[0:H, hs(c, 8)], False, False, ["IB", "MS%d" % c], ["PS"], "PS")
+            mm(T.PX1[0:8, hs(c)], T.MS[0:H, hs(c, 8)], T.Ib[0:H, 0:H], True, True, ["Ib", "MS%d" % c], ["PX1"], "PX1")
+        first(T.OC, ["OC0", "OC1", "CLo"], 0)
+        step("hit")
+        act(T.HR[0:8, :], T.PX1[0:8, 0:L], F.Identity, ["PX1"], ["HR", "WIN"], ["PX1"], bias=1.0, scale=-1.0, acc=T.WIN[0:8, 0:1])
+        mm(T.PX0[:, 0:L], T.EXB[0:8, :], T.HR[0:8, :], True, False, ["EXB", "HR"], ["PX0"], "PX0")
+        mm(T.PX0[:, 0:L], T.Ib[:], T.RN[:, t:t + L], False, True, ["Ib", "RN"], ["PX0"], "PX0")
+        if not last:
             for c in range(2):
-                mm(T.PL[0:H, 64 + 8 * c:72 + 8 * c], T.THB[:], T.Wt[:], True, True, ["THB", "Wt"], ["PLt"], "PL")
-        tt(T.DN[:], NTw.indirect(ol), T.WB[:], A.subtract, ["NT", "OL", "WB"], ["DN"])
-        if t == 0:
-            ts(T.TH0[0:H, :], T.PL[0:H, 64:80], -498 * U, None, A.add, None, ["PLt"], ["TH0"], ["PL"])
-        else:
-            ts(T.THR[0:H, :], T.TH0[0:H, :], T.SS[0:H, 1:2], None, A.add, None, ["TH0", "SS1"], ["THR"])
-        mm(T.PL[0:H, 32:48], T.ONE[0:1, 0:H], T.CK[0:1, :], True, False, ["ONE", "CK"], ["FB"], "PL")
-        for c in range(2):
-            mm(T.PL[0:H, 32 + 8 * c:40 + 8 * c], T.WB[:, H * c:H * c + H], T.Wf[:], False, c == 1, ["WB", "Wf"], ["FB"], "PL")
-        thk = "TH0" if t == 0 else "THR"
-        first_cmp(range(1))
-        tt(T.HT[0:H, :], T.SC[0:H, 15:256:16], T[thk][0:H, :], A.is_lt, ["SC", thk], ["HT"])
-        first_cmp(range(1, 8))
-        for k in range(16):
-            mm(kcols(T.PD, 0, k), kview(T.NG, 0, k), T.Wm[:], False, False, ["NG0", "Wm"], ["PD"], "PD")
-        eq_half(0, range(4))
-        first_cmp(range(8, 12))
-        flag(0)
-        for k in range(16):
-            mm(kcols(T.PD, 1, k), kview(T.NG, 1, k), T.Wm[:], False, False, ["NG1", "Wm"], ["PD"], "PD")
-        weigh(0, "If2", False)
-        act(T.NO[:], NTw.indirect(ol), F.Copy, ["NT", "OL"], ["NO"])
-        act(T.HA[:], T.HT[:, 0:16].indirect(T.REP[:, 0:16]), F.Copy, ["HT", "REP"], ["HA"])
-        eq_half(1, range(1))
-        for c in range(2):
-            mm(T.PD[0:H, 128 * c:128 * c + 128], T.NO[:, H * c:H * c + H], T.ID[:], False, False, ["NO", "ID"], ["PD"], "PD")
-        eq_half(1, range(1, 4))
-        code(T.EC[:], MTw.indirect(wl), ["MT", wk], ["EC"], scaled=True)
-        flag(1)
-        weigh(1, "If2", True)
-        act(T.E4[:], MTw.indirect(wl), F.Copy, ["MT", wk], ["E4"])
-        first_cnt(range(5 if t > 0 else 0, 12))
-        act(T.DA[:], T.DN[:], F.Abs, ["DN"], ["DA"], scale=2048.0)
-        op("V", lambda: v.tensor_tensor_scan(T.ES[:], T.EE[:], T.MS[:], 0.0, A.max, A.min), ["EE%d" % j for j in range(12)] + ["MS"], ["ES"])
-        for c in range(2):
-            ha, cs = T.HA[0:H, 128 * c:128 * c + 128], slice(H * c, H * c + H)
-            mm(T.PH[:, cs], ha, T.I15[0:H, :], True, False, ["HA", "I15"], ["hitN"], "PH")
-            mm(T.PH[:, cs], ha, T.nI[0:H, 0:H], False, True, ["HA", "nI"], ["hitN"], "PH")
-        pick(16, True)
-        for c in range(2):
-            ha, cs = T.HA[0:H, 128 * c:128 * c + 128], slice(H * c, H * c + H)
-            cs2 = slice(L + H * c, L + H * c + H)
-            mm(T.PH[:, cs2], ha, T.IMa[0:H, :], True, False, ["HA", "IMa"], ["hitM"], "PH")
-            mm(T.PH[:, cs2], ha, T.IMb[0:H, :], False, True, ["HA", "IMb"], ["hitM"], "PH")
-            if not last:
-                mm(T.PM[:, cs], T.ONE[0:H, :], T.Ib[0:H, 0:H], True, False, ["ONE", "Ib"], ["miss"], "PM")
-                mm(T.PM[:, cs], ha, T.nI[0:H, 0:H], False, True, ["HA", "nI"], ["miss"], "PM")
+                o = T.PX0[:, L + H * c:L + H * c + H]
+                mm(o, T.ONE[0:1, :], T.ONE[0:1, 0:H], True, False, ["ONE"], ["miss"], "PX0")
+                mm(o, T.EXN[0:8, :], T.HR[0:8, hs(c)], False, True, ["EXN", "HR"], ["miss"], "PX0")
+            mm(T.PX1[:, 400:401], T.UF[0:8, :], T.WIN[0:8, 0:1], True, False, ["UF", "WIN"], ["wins"], "PX1")
+            mm(T.PX1[:, 400:401], T.ONE[0:1, :], T.HLF[0:1, 0:1], False, True, ["ONE", "HLF"], ["wins"], "PX1")
+            step("dx")
+            mm(T.PX1[:, L:2 * L], T.Ib[:], z[:], True, False, ["Ib", zk], ["dx"], "PX1")
+            mm(T.PX1[:, L:2 * L], T.nI[:], ZO[:], False, True, ["nI", zo], ["dx"], "PX1")
+        step("dn")
+        tt(T.DN[:], NTw.indirect(ol), T.WB[:], A.subtract, ["NT", "WB"] + olk, ["DN"])
+        step("q")
+        tt(T.Q[:], MTw.indirect(wl), T.OB[:], A.is_equal, ["MT", "OB0", "OB1"] + wks, ["Q"])
+        step("kn")
+        tt(T.KN[:], T.DN[:], T.PX0[:, 0:L], A.mult, ["DN", "PX0"], ["KN"], ["PX0"])
+        step("ff")
+        tt(T.FF[0:H, :], T.PS[0:H, 0:32], T.TC[0:H, :], A.is_ge, ["PS"] + ["TC" + s for s in four_], ["FF"], ["PS"])
+        step("od")
+        tt(T.OD[:], T.FF[:, 0:32].indirect(T.CV[:, 0:12]), T.MD[:], A.mult, ["FF", "CV"] + ["MD" + s for s in four_], ["OD"])
+        to_list(T.PS[:, 32:56], T.OD, 0, L, "OD", "PO", "PS")
+        step("of")
+        tt(T.OF[:], T.IDL[:], T.PS[:, 32:56], A.max, ["IDo0", "IDo1", "IDw", "PO"], ["OF"], ["PS"])
+        step("ofu")
+        cp(T.OFU[:], T.OF[:], ["OF"], ["OFU"])
+        step("putN")
+        tt(NTw.indirect(T.OFU[:, 0:12]), T.WB[:], T.KN[:], A.add, ["WB", "KN", "OFU"], ["NT"])
+        step("putM")
+        tt(MTw.indirect(T.OFU[:, 12:24]), T.OB[:], T.Q[:], A.mult, ["OB0", "OB1", "Q", "OFU"], ["MT"])
         if not last:
-            mm(T.PM[:, 400:416], T.ONE[0:H, :], T.HT[0:H, :], True, True, ["ONE", "HT"], ["wins"], "PM")
-        tt(T.OF[:], T.ES[:, 0:EL].indirect(T.END[:, 0:1]), T.OLF[:], A.max, ["ES", "END", "OLF"], ["OF"])
-        cp(T["WO%d" % t][:], T.PL[:, 16:28], ["PL16"], ["WO%d" % t], ["PL"])
-        send(t, "WO%d" % t, "WL%d" % t, "wa%d" % t)
-        arrival(t)
-        tt(T.Q[:], T.EC[:], T.OC[:, 16:208], A.not_equal, ["EC", "OC"], ["Q"])
-        cp(T.OFO[:], T.OF[:, 0:12], ["OF"], ["OFO"])
-        tt(T.AM[:], T.Q[:], T.PH[:, L:2 * L], A.mult, ["Q", "hitM"], ["AM"], ["PH"])
-        tt(T.PM[:, L:2 * L], T.RR[:, t:t + L], T.PH[:, 0:L], A.is_gt, ["RR", "hitN"], ["PMt"], ["PM", "PH"])
-        tt(T.G1[:], T.AC[:], T.BC[:], A.is_gt, ["AC%d" % j for j in range(12)] + ["BC%d" % j for j in range(12)], ["G1"])
-        tt(T.PM[:, L:2 * L], T.DN[:], T.PM[:, L:2 * L], A.mult, ["DN", "PMt"], ["PMt"], ["PM"])
-        tt(T.G1[:], T.G1[:], T.DF[:], A.mult, ["G1", "DF"], ["G1"])
-        tt(T.T3[:], T.NO[:], T.PM[:, L:2 * L], A.subtract, ["NO", "PMt"], ["T3"], ["PM"])
-        tt(T.G1[:], T.G1[:], T.WLF[:], A.max, ["G1", "WLF"], ["G1"])
-        tt(T.AN[:], T.DA[:], T.PH[:, 0:L], A.min, ["DA", "hitN"], ["AN"], ["PH"])
-        cp(T.OFW[:], T.G1[:], ["G1"], ["OFW"])
-        tt(T.MT[:, 0:4096].indirect(T.OFW[:, 0:12]), T.E4[:], T.AM[:], A.max, ["E4", "AM", "OFW"], ["MT"])
-        if last:
-            fb = ["PD", "PC", "PX1"]
-            top = NONE * 4096.0
-            for j in range(3):
-                c = slice(512 * j, 512 * j + 512)
-                act(T[fb[j]][:], T.MT[:, c], F.Relu, ["MT"], [fb[j]], [fb[j]], bias=top, scale=-1.0)
-                act(T[fb[j]][:], T[fb[j]][:], F.Identity, [fb[j]], [fb[j]], [fb[j]], bias=top, scale=-1.0)
-        else:
-            zn, nk = T["ZL%d" % t], "ZL%d" % t
-            act(T.ZR[:, 0:H], zn[:, 0:H], F.Relu, [nk], ["ZR0"], bias=23.0, scale=-1.0)
-            act(T.ZR[:, H:L], zn[:, H:L], F.Sign, [nk], ["ZR1"], bias=31.0, scale=-1.0)
-            act(T.ZT[:, 0:H], T.ZR[:, 0:H], F.Identity, ["ZR0"], ["ZT0"], bias=31.0, scale=-1.0)
-            act(T.ZT[:, H:L], T.ZR[:, H:L], F.Copy, ["ZR1"], ["ZT1"], scale=8.0)
-        tt(T.NT[:, 0:4096].indirect(T.OFO[:, 0:12]), T.T3[:], T.AN[:], A.max, ["T3", "AN", "OFO"], ["NT"])
-        if not last:
-            x_step(t, z, zk)
+            step("cl")
+            ts(T.CL[:], T.PX1[:, L:2 * L], -2.0, 2.0, A.max, A.min, ["dx"], ["CL"], ["PX1"])
+            step("cm")
+            tt(T.CM[:], T.CL[:], T.PX0[:, L:2 * L], A.mult, ["CL", "miss"], ["CM"], ["PX0"])
+            step("putX")
+            tt(XTw.indirect(T.OFU[:, 0:12]), ZO[:], T.CM[:], A.add, [zo, "CM", "OFU"], ["XT"])
+            step("ss")
+            ts(T.SS[:, 0:1], T.PX1[:, 400:401], 1.5 * 2.0 ** 43, 1.5 * 2.0 ** 43, A.add, A.subtract, ["wins"], ["SS"], ["PX1"])
+            step("thr")
+            ts(T.THR[0:H, :], T.TH1[0:H, :], T.PX1[0:H, 400:401], T.SS[0:H, 0:1], A.add, A.subtract, ["TH1", "wins", "SS"], ["THR"], ["PX1"])
 
-    fb = ["PD", "PC", "PX1"]
-    dma("S", T.yz[:], T["ZL%d" % (RO - 1)][:], "st", r=["ZL%d" % (RO - 1)])
+    t = RO - 1
+    top = NONE * 4096.0
+    step("outz")
+    dma("S", T.yz[:], T["ZL%d" % t][:], "st", r=["ZL%d" % t])
     for j in range(3):
-        c = slice(512 * j, 512 * j + 512)
-        tt(T.OUT[:, c], T.NT[:, c], T[fb[j]][:], A.add, ["NT", fb[j]], ["OUT%d" % j], [fb[j]])
+        c = hs(j, 512)
+        step("absN%d" % j)
+        act(T.FT[:, c], T.NT[:, c], F.Abs, ["NT"], ["FT%d" % j], bias=-OFF)
+        step("cutN%d" % j)
+        ts(T.FT[:, c], T.FT[:, c], float(NONE), top, A.min, A.add, ["FT%d" % j], ["FT%d" % j])
+        step("cutM%d" % j)
+        act(T[banks[j]][:], T.MT[:, PAD + 512 * j:PAD + 512 * j + 512], F.Relu, ["MT"], whole[j], [banks[j]], bias=top - OFF, scale=-1.0)
+        step("out%d" % j)
+        tt(T.OUT[:, c], T.FT[:, c], T[banks[j]][:], A.subtract, ["FT%d" % j, banks[j]], ["OUT%d" % j], [banks[j]])
         dma("S", T.ynm[:, c], T.OUT[:, c], "st", r=["OUT%d" % j])
-    dma("A", T.yw[:], T["WL%d" % (RO - 1)][:], "st", r=["WL%d" % (RO - 1)])
-    need("G", list(cnt.items()) + [("sent", sent[0])])
+    step("outw")
+    dma("A", T.yw[:], T["WL%d" % t][:], "st", r=["WL%d_0" % t, "WL%d_1" % t])
+    issue()

@@ -11,27 +11,33 @@ U = 32768.0
 BIG = 2.0 ** 99
 SLOPE = 23.0 / 512
 WIDE = 2048
+FIN = 1
+VFLAGS = ("M0",)
+EARLY = ("e0 e1 wc0 wc1 gN0 gN1 gX0 gX1 zr0 zr1 wb0 wb1 open0 open1 fourw0 fourw1 eqN0a eqN0b eqN0c eqN0d maxa maxb maxc maxd fourz sumX ef0 ef1 "
+         "addE0 addE1 flagN0 idw scano0 lowo0 listo0").split()
+LATE = ("dn ff od kn of ofu q putN putM no sb hit zo1 eqM1a eqM1b eqM1c eqM1d flagM1 scanw1 intw1 loww1 listw1 wo1 sumM1 gM1 scanw0 intw0 loww0 listw0 wo0 "
+        "sameo0 sameo1 sameo2 sameo3 sameo4 sameo5").split()
 
 f32, bf, f16, i32, u16 = "float32", "bfloat16", "float16", "int32", "uint16"
 SCRATCH = {}
 for _n, _c, _d in [
     ("NM", W, i32), ("NT", WIDE, f32), ("MT", WIDE + PAD, f32), ("XT", WIDE, bf), ("FT", W, f32), ("OUT", W, f32),
-    ("IO", WIDE, f32), ("NG", 3072, bf), ("MG", 3072, bf), ("XG", 3072, bf), ("MX", 3072, bf), ("EQ", 3072, bf),
+    ("IO", W, f32), ("NG", 3072, bf), ("MG", 3072, bf), ("XG", 3072, bf), ("MX", 3072, bf), ("EQ", 3072, bf),
     ("W32", 12, i32), ("TH", 1, i32), ("Z0", L, bf), ("WI", 16, u16),
-    ("IA", 208, i32), ("RN", 208, bf), ("PI", 2, i32), ("PJ", 4, i32), ("PF", 4, f32),
-    ("CI", 128, f32), ("KI", 128, f32), ("GI", 128, f32), ("RS", 128, f32), ("CR", 128, bf), ("CK", 8, f32), ("ZERO", 32, bf),
-    ("ONE", 128, bf), ("ONF", 128, f32), ("UF", 128, f32), ("HLF", 2, bf),
-    ("ID", 128, f32), ("Ih", 128, f16), ("Ib", 128, bf), ("nI", 128, bf), ("IB", H, bf),
-    ("If1", H, bf), ("If2", H, bf), ("BOX", 128, bf), ("W1", 8, bf), ("W2", 8, bf), ("Wm", 8, bf),
-    ("Wp", 8, bf), ("Wf", 8, f32), ("Wt", 8, bf), ("EXB", 128, bf), ("EXN", 128, bf), ("SEL", 240, f16), ("SI", 16, f32),
+    ("RP", 24, u16), ("RN", 208, bf), ("PJ", 8, i32), ("PF", 4, f32),
+    ("CI", 128, f32), ("KI", 128, f32), ("RS", 128, f32), ("CR", 128, bf), ("CK", 8, f32),
+    ("ONE", 128, bf), ("ONF", H, f32), ("UF", 128, f32), ("HLF", 2, bf), ("ZB", H, bf),
+    ("ID", 128, f32), ("Ih", 128, f16), ("Ib", 128, bf), ("nI", 128, bf), ("IB", H, bf), ("nF", 128, f32), ("Iq", 128, f32),
+    ("If1", H, bf), ("If2", H, bf), ("BOX", 128, bf), ("BX8", 128, bf), ("W1", 8, bf), ("W2", 8, bf), ("Wm", 8, bf),
+    ("Wp", 8, bf), ("Wf", 8, f32), ("Wt", 8, bf), ("EXB", 128, bf), ("EXN", 128, bf), ("EX2", 128, bf), ("SEL", 240, f16), ("SI", 16, f32),
     ("P2", H, f32), ("HF", H + 12, f32), ("TP", H, f32),
-    ("CV", 12, u16), ("CF", 12, f32), ("BI", 48, f32), ("MK", 48, f32), ("MD", L, f32), ("WT", 12, bf),
+    ("CV", 12, u16), ("BI", 60, f32), ("MK", 48, f32), ("MD", L, f32), ("WT", 12, bf),
     ("TC", 32, f32), ("T1", 8, f32), ("THB", H, bf), ("TH0", 16, f32), ("TH1", 16, f32), ("THR", 16, f32),
     ("E16", L, u16), ("U16", L, u16), ("EF", L, f16), ("UH", L, f16), ("WC", L, bf), ("OC", L, bf), ("ZR", L, bf),
-    ("FL", 256, bf), ("SC", 256, f32), ("S32", 16, i32), ("O32", 16, i32), ("OA", 96, f16), ("OL", 12, u16),
+    ("FL", 256, bf), ("SC", 256, i32), ("S32", 16, i32), ("O32", 16, i32), ("OA", 96, f16), ("OL", 12, u16),
     ("IDL", 24, f32), ("CL2", 24, bf), ("MS", 16, bf), ("HR", L, bf), ("WIN", 2, f32), ("WB", L, f32), ("OB", L, f32),
     ("EE", 18 * H, bf), ("FF", 32, bf), ("OD", L, f16), ("OF", 24, f32), ("OFU", 24, u16),
-    ("DN", L, f32), ("KN", L, f32), ("Q", L, f32), ("CL", L, bf), ("CM", L, bf), ("SS", 2, f32),
+    ("DN", L, f32), ("SB", L, bf), ("KN", L, f32), ("Q", L, f32), ("CL", L, bf), ("CM", L, bf), ("XN", L, bf),
 ]:
     SCRATCH[_n] = ("sbuf", [128, _c], _d)
 for _t in range(RO):
@@ -43,17 +49,20 @@ for _n in ["PD0", "PD1", "PC", "CB0", "CB1", "PX0", "PX1", "PS"]:
     SCRATCH[_n] = ("psum", [128, 512], f32)
 
 SEMAPHORES = (["sV", "sA", "sP", "sG", "sent", "lw", "lz", "lt", "lx", "ln0", "ln1", "ln2", "st"]
-              + ["%s%d" % (s, t) for t in range(RO) for s in ("za", "wa", "wb")])
-PIECES = (("za", "Z", 0, L, 0), ("wa", "W", 0, 6, 0), ("wb", "W", 6, 12, 8))
-SENDS = (0, 1, 2)
+              + ["%s%d" % (s, t) for t in range(RO) for s in ("za", "wa", "zb", "wb")])
+PIECES = (("za", "Z", 0, H, 0), ("wa", "W", 0, 6, 0), ("zb", "Z", H, L, H), ("wb", "W", 6, 12, 8))
 
 ORDER = """
-load wc0 kpow e0 tabN +intw1 +od +cutN2 +loww1 sameo1 +out0 kx +putX samew0 diffb absN0 kkeys ef1 +cl eqN0d +cutN1 +listw1 +kn oc0 gX0 +of listo1 gap1
-diffa sameo2 flagN0 scano0 tabM0 gap0 +thr +cm fourz open0 e1 gap2 fourw1 fourw0 eqN0c +wo1 tabM1 +send2 gN0 +ofu +absN2 +cutM0 diffc maxd wc1 wb zr
-maxb +cutM2 ef0 gX1 eqN0a dx +cutM1 idw gN1 +out1 putN maxc kpick +outw eqN0b maxa tabM2 +ss addE0 clw diffd open1 sumX listo0 absb eqN1c intw0 absN1
-absa into0 eqN1b sameo0 putM lowo0 zo eqN1d ol0 into1 eqN1a miss1 u0 addE1 samew1 absd samew2 sameo4 outz loww0 rows lowo1 absc flagN1 ob0 kth scano1
-ido0 gM0 back0 samew3 openS flagM0 samew4 ol1 ob1 kdump oc1 fouro0 ido1 miss0 uh0 sumM0 samew5 fouro1 u1 eqM0a eqM0c send1 cutN0 eqM0d clo back1 uh1
-sameo3 gM1 eqM0b sumM1 hit eqM1b eqM1c scanw0 sameo5 scanw1 listw0 eqM1d eqM1a wo0 krow q dn flagM1 ff out2 send0
+load kx kpow idw_ tabY2 e1_ tabY1 e0_ tabY0 tabN2 tabN0 maxb_ +out0b tabN1 maxd_ gX0_ tabM0 eqN0a_ maxa_ gap0 wb0_ wc0_ +listw1 gN0_ +out0a gX1_
+fourz_ fourw0_ sumX_ eqN0b_ open0_ eqN0d_ eqN0c_ zr1_ open1_ gap2 wc1 gap1 gN0 ef0_ kpick flagN0_ wc1_ +kn flagN0 gM0 zr0_ wb0 +outw addE0_ zr0 ef1_
+openS e1 +putM gN1_ +cm fourw1_ +cl fourz +wo1 tabM2 +putN open0 wc0 diff1c +putX e0 maxc_ tabM1 gX0 +send3 fourw0 eqN0b zr1 eqN0a diff1d sumX maxd
+eqN0d gX1 eqN0c addE0 gN1 diff1b maxb scano0_ lowo0 maxc maxa ef0 +ss idw open1 ef1 diff1a fourw1 scano0 addE1 listo0 abs1b lowo0_ wb1_ kdump listo0_
+wb1 eqN1a addE1_ abs1a clw eqN1d ol0 eqN1b eqN1c abs1d oc0 zo0 samew0 abs1c flagN1 u0 +thr kth scano1 fouro0 samew2 back0 lowo1 samew5 miss listo1
+samew4 samew1 clo0 samew3 ob1 oc1 gM1 ol1 rows sumM0 hit clo1 eqM0c ob0 u1 eqM0a eqM0b addU0 eqM0d sameo2' fouro1 sameo5 addU1 uh sameo1' sameo4'
+sameo3 flagM0 sameo0' of' dn' sameo3' sameo5' scanw0' ff' gM1' qd back1 eqM1d' intw0' hit' od' sameo0 no' sameo4 loww0' eqM1b' send0 scanw0 sameo1
+flagM1' x255 intw0 listw0' ido1 ido0 zo1' q' sb' ofu' eqM1c' eqM1a' kn' wo0' sumM1 scanw1' zo1 cutM2 putN' sumM1' sameo2 dn loww0 eqM1d absN2 absN1
+cutM1 dx eqM1c eqM1a eqM1b ff intw1' listw0 flagM1 od wo0 send1 absN0 putM' cutM0 cutN0 loww1' listw1' out1a cutN2 no wo1' out2b out2a send2 out1b
+loww1 cutN1 scanw1 outz sb of intw1 q ofu
 """.split()
 
 
@@ -81,8 +90,7 @@ def relay_program(g, core, T, topo):
             if via != core:
                 continue
             n = len(topo.engines(src, core))
-            for p in SENDS:
-                sem, buf, lo, hi, _ = PIECES[p]
+            for sem, buf, lo, hi, _ in PIECES:
                 ap = T["%sL%d" % (buf, t)][:, lo:hi]
                 g.wait_ge(T.sem["%s%d" % (sem, t)], n)
                 sent += put(g, T, topo, core, dst, ap, ap, "%s%d" % (sem, t))
@@ -102,7 +110,7 @@ def rank_program(g, core, T, topo):
     sent = [0]
 
     def step(name):
-        now[1] = name
+        now[1] = name + "'" * (now[0] == RO - 1 and name in LATE) + "_" * (now[0] == 0 and name in EARLY)
 
     def record(q, fn, sem, inc, r, w, b=(), after=()):
         pre = set(after)
@@ -134,7 +142,7 @@ def rank_program(g, core, T, topo):
             for p in c[6]:
                 nxt[p].append(i)
         left = [len(c[6]) for c in calls]
-        turn = [(c[5][0] * len(ORDER) + place.get(c[5][1], 0), i) for i, c in enumerate(calls)]
+        turn = [(c[5][0] * len(ORDER) + place[c[5][1]], i) for i, c in enumerate(calls)]
         ready = [i for i in range(len(calls)) if not left[i]]
         cnt, tok, bank = {}, {}, {}
         waited = {q: {} for q in Q}
@@ -215,10 +223,13 @@ def rank_program(g, core, T, topo):
     def mcode(out, in_, r, w):
         act(out, in_, F.Sigmoid, r, w, bias=7.0, scale=SLOPE / 4096)
 
+    def ocode(out, in_, r, w, b=()):
+        act(out, in_, F.Sigmoid, r, w, b, bias=7.0 - TOP * SLOPE, scale=SLOPE)
+
     def ncode(out, in_, r, w, off=OFF):
         act(out, in_, F.Sigmoid, r, w, bias=-off / 32 - 80.0, scale=1.0 / 32)
 
-    NTw, MTw, XTw, IOw = T.NT[:, 0:WIDE], T.MT[:, PAD:PAD + WIDE], T.XT[:, 0:WIDE], T.IO[:, 0:WIDE]
+    NTw, MTw, XTw, IOw = T.NT[:, 0:WIDE], T.MT[:, PAD:PAD + WIDE], T.XT[:, 0:WIDE], T.IO[:, 0:W]
 
     def hs(c, n=H):
         return slice(n * c, n * c + n)
@@ -229,74 +240,83 @@ def rank_program(g, core, T, topo):
     dma("S", T.NM[:, 1024:W], T.nm[:, 1024:W], "ln2", w=["NM2"])
     dma("A", T.W32[:], T.w[:], "lw", w=["W32"])
     dma("S", T.XT[:, 0:W], T.x[:], "lx", w=["XT"])
-    dma("A", T.Z0[:], T.z[:], "lz", w=["Z0"])
+    dma("S", T.Z0[:], T.z[:], "lz", w=["Z0"])
     dma("S", T.TH[:], T.th[:], "lt", w=["TH"])
 
-    iota(T.PI[:], [[0, 2]], 0, 1, ["PI"], False)
+    iota(T.PJ[:, 4:6], [[0, 2]], 0, 1, ["PI"], False)
     iota(T.CI[:], [[1, 128]], 0, 0, ["CI"])
-    iota(T.IO[:, 0:W], [[1, W]], 0, 0, ["IO"])
-    iota(T.NT[:, W:WIDE], [[0, WIDE - W]], int(NONE + OFF), 0, ["NTt"])
-    iota(T.GI[:], [[1, 8], [0, 16]], 0, 0, ["GI"])
     iota(T.KI[:], [[0, 8], [1, 16]], 0, 0, ["KI"])
+    iota(T.BI[:, 0:48], [[1, 6], [0, 8]], 0, 0, ["BI"])
+    iota(T.BI[:, 48:60], [[8, 4], [0, 3]], 0, 0, ["CF"])
+    iota(T.IO[:, 0:NONE], [[1, NONE]], 0, 0, ["IO"])
+    iota(T.NT[:, W:WIDE], [[0, WIDE - W]], int(NONE + OFF), 0, ["NTt"])
     iota(T.MT[:, PAD + W:PAD + WIDE], [[0, WIDE - W]], 0, 0, ["MTu"])
-    iota(T.BI[:], [[1, 6], [0, 8]], 0, 0, ["BI"])
-    iota(T.CF[:], [[8, 4], [0, 3]], 0, 0, ["CF"])
-    iota(T.IA[:], [[1, 208]], 128, -1, ["IA"], False)
+    iota(T.O32[:], [[0, 16]], 0, 0, ["O320", "O321"], False)
+    iota(T.FF[:], [[0, 32]], 0, 0, ["FF"])
+    iota(T.UF[0:8, :], [[0, 128]], int(U), 0, ["UF"])
+    iota(T.HLF[0:1, :], [[0, 2]], int(-15.5 * U), 0, ["HLF"])
+    iota(T.MT[:, 0:PAD], [[0, PAD]], 0, 0, ["MTt"])
+    iota(T.ZB[0:1, :], [[0, H]], 0, 0, ["ZB"])
+    iota(T.ONF[0:1, :], [[0, H]], 1, 0, ["ONF"])
+    iota(T.CK[0:1, :], [[0, 8]], int(PAD - OFF - 17 * U), 0, ["CK"])
     iota(T.EE[:], [[0, 18 * H]], 0, 0, ["EEz"])
-    pf, pm, pg, p8 = T.PF[:, 0:1], T.PF[:, 1:2], T.PF[:, 2:3], T.PF[:, 3:4]
-    ms(T.IO[:, W:WIDE], float(JUNK), ["IOt"])
-    ms(T.XT[:, W:WIDE], 39.0, ["XTt"])
-    ms(T.ONE[:], 1.0, ["ONE"])
-    ms(T.O32[:], 0, ["O320", "O321"])
-    ms(T.FF[:], 0.0, ["FF"])
-    ms(T.ZERO[0:1, :], 0.0, ["ZERO"])
-    ms(T.CK[0:1, :], PAD - OFF - 17 * U, ["CK"])
-    ms(T.ONF[0:1, :], 1.0, ["ONF"])
-    ms(T.UF[0:8, :], U, ["UF"])
-    ms(T.HLF[0:1, :], -15.5 * U, ["HLF"])
-    ms(T.MT[:, 0:PAD], 0.0, ["MTt"])
-    ms(T.CR[0:2, :], -496 * U, ["CR"])
+    pi, pf, pm, pg, p8 = T.PJ[:, 4:5], T.PF[:, 0:1], T.PF[:, 1:2], T.PF[:, 2:3], T.PF[:, 3:4]
+    ms(T.IO[:, NONE:W], float(JUNK), ["IOt"])
+    ms(T.XT[:, W:WIDE], -8.0, ["XTt"])
+    act(T.ONE[:], T.CI[:], F.Sigmoid, ["CI"], ["ONE"], bias=30.0)
     ms(T.SEL[:], 0.0, ["SEL"])
     ms(T.HF[:, 0:H], 0.5, ["HFa"])
     ms(T.HF[:, H:H + 12], 2.0 ** -16, ["HFb"])
-    ts(T.PJ[:, 0:1], T.PI[:, 0:1], 15, None, A.bitwise_and, None, ["PI"], ["PJ0"])
-    ts(T.PJ[:, 1:2], T.PI[:, 0:1], 4, None, A.logical_shift_right, None, ["PI"], ["PJ1"])
-    ts(T.PJ[:, 2:3], T.PI[:, 0:1], 7, None, A.bitwise_and, None, ["PI"], ["PJ2"])
-    cp(pf, T.PI[:, 0:1], ["PI"], ["pf"])
+    ts(T.PJ[:, 0:1], pi, 15, None, A.bitwise_and, None, ["PI"], ["PJ0"])
+    ts(T.PJ[:, 1:2], pi, 4, None, A.logical_shift_right, None, ["PI"], ["PJ1"])
+    ts(T.PJ[:, 2:3], pi, 7, None, A.bitwise_and, None, ["PI"], ["PJ2"])
+    cp(pf, pi, ["PI"], ["pf"])
     cp(T.PF[:, 1:4], T.PJ[:, 0:3], ["PJ0", "PJ1", "PJ2"], ["pm"])
     ts(T.ID[:], T.CI[:], pf, None, A.is_equal, None, ["CI", "pf"], ["ID"])
-    for name, c in (("W1", 1.0), ("W2", 2 * U), ("Wm", -U), ("Wp", U), ("Wt", U / 16)):
-        ts(T[name][:], T.CI[:, 0:8], pg, c, A.is_equal, A.mult, ["CI", "pm"], [name])
+    ts(T.W1[:], T.CI[:, 0:8], pg, None, A.is_equal, None, ["CI", "pm"], ["W1"])
     cp(T.Wf[:], T.ID[:, 0:128:16], ["ID"], ["Wf"])
     cp(T.Ih[:], T.ID[:], ["ID"], ["Ih"])
     ts(T.SI[:], T.CI[:, 0:16], pm, None, A.is_equal, None, ["CI", "pm"], ["SI"])
     cp(T.SEL[:, 112:128], T.SI[:], ["SI"], ["SEL"])
-    for name, c, n in (("Ib", 1.0, 128), ("nI", -1.0, 128), ("If1", -370 * U, H), ("If2", -18 * U, H), ("IB", BIG, H)):
+    cp(T.RP[:, 0:8], T.CI[:, 0:8], ["CI"], ["RPa"])
+    ts(T.RP[:, 8:24], T.ONE[:, 0:16], pm, None, A.mult, None, ["ONE", "pm"], ["RPb"])
+    for name, c in (("W2", 2 * U), ("Wm", -U), ("Wp", U), ("Wt", U / 16)):
+        act(T[name][:], T.W1[:], F.Copy, ["W1"], [name], scale=c)
+    for name, c, n in (("Ib", 1.0, 128), ("nI", -1.0, 128), ("If1", -370 * U, H), ("If2", -18 * U, H), ("IB", BIG, H), ("nF", -1.0, 128),
+                       ("Iq", -1.0 / 4096, 128)):
         act(T[name][0:n, :], T.ID[0:n, 0:n], F.Copy, ["ID"], [name], scale=c)
+    act(T.BOX[:], T.W1[:, 0:8].indirect(T.RP[:, 0:8]), F.Copy, ["W1", "RPa"], ["BOX"], scale=-U)
+    act(T.BX8[:], T.BOX[:], F.Copy, ["BOX"], ["BX8"], scale=8.0)
+    act(T.EXB[:], T.ID[:, 0:8].indirect(T.RP[:, 0:8]), F.Copy, ["ID", "RPa"], ["EXB"], scale=4096.0)
+    act(T.EXN[:], T.EXB[:], F.Copy, ["EXB"], ["EXN"], scale=64.0 / 4096)
+    act(T.EX2[:], T.EXB[:], F.Copy, ["EXB"], ["EX2"], scale=-2.0 / 4096)
+    act(T.RN[:], T.SI[:, 0:16].indirect(T.RP[:, 8:21]), F.Identity, ["SI", "RPb"], ["RN"], bias=1.0, scale=-1.0)
+    act(T.CR[0:1, :], T.KI[0:1, :], F.Copy, ["KI"], ["CR"], scale=2048.0)
+    act(T.RS[0:H, :], T.KI[0:H, :], F.Relu, ["KI"], ["RS"], bias=1e8, scale=-1e8)
     cp(T.WI[:, 0:12], T.W32[:], ["W32"], ["WI_0", "WI_1"])
 
     banks = ["PX0", "PX1", "PS"]
-    whole = [["PX0", "miss"], ["PX1", "dx", "wins"], ["PS", "PO"]]
+    whole = [["PX0", "xn"], ["PX1", "dx", "wins"], ["PS", "PO"]]
     magic = 1.5 * 2.0 ** 35
     gap = float(TOP - NONE)
     for j in range(3):
         c = hs(j, 512)
-        step("tabN")
+        step("tabY%d" % j)
         ts(T[banks[j]][:], T.NM[:, c], magic, magic + OFF, A.add, A.subtract, ["NM%d" % j], whole[j], [banks[j]])
-        tt(T.NT[:, c], T.NM[:, c], T[banks[j]][:], A.subtract, ["NM%d" % j] + whole[j], ["NT"], [banks[j]])
+        step("tabN%d" % j)
+        tt(T.NT[:, c], T.NM[:, c], T[banks[j]][:], A.subtract, ["NM%d" % j] + whole[j], ["NT%d" % j] + ["NT"] * (j == 2), [banks[j]])
         step("gap%d" % j)
         act(T.FT[:, c], T[banks[j]][:], F.Relu, whole[j], ["FT%d" % j], [banks[j]], bias=(gap + 1) * gap * 4096, scale=gap)
         step("tabM%d" % j)
-        tt(T.MT[:, PAD + 512 * j:PAD + 512 * j + 512], T.FT[:, c], T[banks[j]][:], A.add, ["FT%d" % j, "MTt", "MTu"] + whole[j], ["MT"], [banks[j]])
+        tt(T.MT[:, PAD + 512 * j:PAD + 512 * j + 512], T.FT[:, c], T[banks[j]][:], A.add, ["FT%d" % j] + whole[j],
+           ["MT%d" % j] + ["MT"] * (j == 2), [banks[j]])
     step("kx")
-    ms(T.XT[:, NONE:W], 39.0, ["XT"])
-    step("kkeys")
-    ts(T.BOX[:], T.GI[:], pg, U, A.is_equal, A.mult, ["GI", "pm"], ["BOX"])
-    ts(T.CR[0:1, :], T.KI[0:1, :], 2048.0, None, A.mult, None, ["KI"], ["CR"])
+    act(T.XT[:, 0:W], T.XT[:, 0:W], F.Identity, ["XT"], ["XT"], bias=31.0, scale=-1.0)
+    act(T.XT[:, NONE:W], T.ONE[:, 0:1], F.Copy, ["ONE"], ["XT"], scale=-8.0)
+    act(T.Z0[:], T.Z0[:], F.Identity, ["Z0"], ["Z0_0", "Z0_1"], bias=31.0, scale=-1.0)
     step("kpick")
-    ts(T.RS[:], T.KI[:], 0.0, 1e8, A.is_equal, A.mult, ["KI"], ["RS"])
-    ts(T.CV[:], T.CF[:], p8, None, A.add, None, ["CF", "pm"], ["CV"])
-    ts(T.MK[:], T.BI[:], pg, None, A.is_equal, None, ["BI", "pm"], ["MK"])
+    ts(T.CV[:], T.BI[:, 48:60], p8, None, A.add, None, ["CF", "pm"], ["CV"])
+    ts(T.MK[:], T.BI[:, 0:48], pg, None, A.is_equal, None, ["BI", "pm"], ["MK"])
     step("kpow")
     scan(T.P2[:], T.HF[:, 0:H], T.ONE[:, 0:H], 2.0 ** 97, A.mult, A.mult, ["HFa", "ONE"], ["P2"])
     tt(T.TP[:, 0:16], T.P2[:, 0:16], T.SI[:], A.mult, ["P2", "SI"], ["TP"])
@@ -312,20 +332,15 @@ def rank_program(g, core, T, topo):
         mm(T.PC[0:H, 256 + 8 * c:264 + 8 * c], T.THB[:], T.Wt[:], True, True, ["THB", "Wt"], ["PLt"], "PC")
     ts(T.TH0[0:H, :], T.PC[0:H, 256:272], -498 * U, None, A.add, None, ["PLt"], ["TH0"], ["PC"])
     ts(T.TH1[0:H, :], T.PC[0:H, 256:272], -482.5 * U, None, A.add, None, ["PLt"], ["TH1"], ["PC"])
-    step("krow")
-    ts(T.IA[:], T.IA[:], 15, None, A.bitwise_and, None, ["IA"], ["IA"])
-    ts(T.RN[:], T.IA[:], 0.0, None, A.not_equal, None, ["IA"], ["RN"])
-    ts(T.EXB[0:8, :], T.GI[0:8, :], T.PF[0:8, 0:1], 4096.0, A.is_equal, A.mult, ["GI", "pf"], ["EXB"])
-    ts(T.EXN[0:8, :], T.GI[0:8, :], T.PF[0:8, 0:1], -1.0, A.is_equal, A.mult, ["GI", "pf"], ["EXN"])
     step("kdump")
     for c in range(2):
         ts(T.T1[:, c:c + 1], pf, float(DUMP + H * c), None, A.add, None, ["pf"], ["T1%d" % c])
+        ts(T.T1[:, 6 + c:7 + c], T.T1[:, 2:3], 2.5 * 2.0 ** (-H * c), None, A.mult, None, ["T12"], ["T1%d" % (6 + c)])
     for c in range(2):
         for lst in range(2):
             s = 2 * lst + c
-            ts(T.MD[:, hs(s, 48)], T.MK[:], T.T1[:, c:c + 1], None, A.mult, None, ["MK", "T1%d" % c], ["MD%d" % s])
-            ts(T.TC[0:H, hs(s, 8)], T.ONE[0:H, 0:8], T.T1[0:H, 2:3], 2.5 * 2.0 ** (-H * c), A.mult, A.mult, ["ONE", "T12"], ["TC%d" % s])
-    four_ = ["0", "1", "2", "3"]
+            act(T.MD[:, hs(s, 48)], T.MK[:], F.Identity, ["MK", "T1%d" % c], ["MD%d" % s], scale=T.T1[:, c:c + 1])
+            act(T.TC[0:H, hs(s, 8)], T.ONE[0:H, 0:8], F.Identity, ["ONE", "T1%d" % (6 + c)], ["TC%d" % s], scale=T.T1[0:H, 6 + c:7 + c])
 
     def kview(buf, c, k):
         return buf[:, 1536 * c + k:1536 * c + 1536:16]
@@ -347,13 +362,16 @@ def rank_program(g, core, T, topo):
             for e in range(4):
                 mm(kcols(T.PC, j + 4 * e, 128 * c), T.EQ[:, s + e:s + 4 * H:4], T.W1[:], True, True, ["EQ%d_%d" % (c, j), "W1"], ["PC%d%d" % (c, j)], "PC")
         step("flag%s%d" % (G[0], c))
-        cs, P = hs(c, 128), "PD%d" % c
-        act(T.FL[0:H, cs], T.PC[0:H, cs], F.Sign, ["PC%d%d" % (c, j) for j in range(4)], ["FL%d" % c], ["PC"])
+        cs, P, r = hs(c, 128), "PD%d" % c, ["PC%d%d" % (c, j) for j in range(4)]
+        if G[0] + str(c) in VFLAGS:
+            ts(T.FL[0:H, cs], T.PC[0:H, cs], 1.0, None, A.min, None, r, ["FL%d" % c], ["PC"])
+        else:
+            act(T.FL[0:H, cs], T.PC[0:H, cs], F.Sign, r, ["FL%d" % c], ["PC"])
         mm(T[P][0:H, 0:128], T[I][0:H, :], T.FL[0:H, cs], False, True, [I, "FL%d" % c], [P], P)
 
-    def keys_open(c, rows):
+    def keys_open(c):
         P = "PD%d" % c
-        mm(T[P][0:H, 0:128], T.ONE[0:rows, 0:H], T.CR[0:rows, :], True, False, ["ONE", "CR"], [P], P)
+        mm(T[P][0:H, 0:128], T.ONE[0:1, 0:H], T.CR[0:1, :], True, False, ["ONE", "CR"], [P], P)
 
     def keys_add(c, src, key, rhs, after=()):
         P = "PD%d" % c
@@ -371,14 +389,13 @@ def rank_program(g, core, T, topo):
         P, cs, g8 = "PD%d" % c, hs(c, 128), hs(c, 8)
         step("scan" + tag)
         scan(T.SC[0:H, cs], T.RS[0:H, :], T[P][0:H, 0:128], 0.0, A.add, A.min, ["RS", P], ["SC%d" % c], [P])
-        step("int" + tag)
-        least = T.SC[0:H, 128 * c + 15:128 * c + 128:16]
+        least, k = T.SC[0:H, 128 * c + 15:128 * c + 128:16], "SC%d" % c
         if tag[0] == "w":
-            tt(T.S32[0:H, g8], least, T[P][0:H, 144:152], A.min, ["SC%d" % c, "FB%d" % c], ["S32%d" % c], [P])
-        else:
-            cp(T.S32[0:H, g8], least, ["SC%d" % c], ["S32%d" % c])
+            step("int" + tag)
+            tt(T.S32[0:H, g8], least, T[P][0:H, 144:152], A.min, [k, "FB%d" % c], ["S32%d" % c], [P])
+            least, k = T.S32[0:H, g8], "S32%d" % c
         step("low" + tag)
-        ts(T.O32[0:H, g8], T.S32[0:H, g8], 2047, None, A.bitwise_and, None, ["S32%d" % c], ["O32%d" % c])
+        ts(T.O32[0:H, g8], least, 2047, None, A.bitwise_and, None, [k], ["O32%d" % c])
         step("list" + tag)
         tt(T.OA[:, hs(c, 48)], T.O32[:, g8].indirect(T.CV[:, 0:3]), T.MK[:], A.mult, ["O32%d" % c, "CV", "MK"], ["OA%d" % c])
         to_list(T[P][:, 128:134], T.OA, 48 * c, 48 * c + 48, "OA%d" % c, "PL%d" % c, P)
@@ -393,35 +410,35 @@ def rank_program(g, core, T, topo):
                 o = 16 * lst + 8 * c
                 mm(T.PS[0:H, o:o + 8], T.EE[:, s0 + H * c:s0 + H * c + H], T.W1[:], False, lst == 0 and b == 11, ["EE%d" % b, "W1"], ["PS"], "PS")
 
-    def send(t, p, key):
+    def send(t, p):
         sem, buf, lo, hi, o = PIECES[p]
-        name = "%s%d" % (sem, t)
+        name, half = "%s%d" % (sem, t), "%d_%d" % (t, p // 2)
         src, via, dst = route(T, topo, rank, t)
         to = dst if via is None else via
         sent[0] += len(topo.engines(src, to))
         step("send%d" % p)
         me = record("G", lambda: put(g, T, topo, src, to, T["%sL%d" % (buf, t)][:, lo:hi], T["%sO%d" % (buf, t)][:, o:o + hi - lo], name),
-                    None, 0, [key], ["sends"])
+                    None, 0, [buf + "O" + half], ["sends"])
         far, relay, here = route(T, topo, (rank - 1 - t % (NR - 1)) % NR, t)
-        record("R", None, name, len(topo.engines(far if relay is None else relay, here)), [], [("ZL%d", "WL%d_0", "WL%d_1")[p] % t], (), [me])
+        record("R", None, name, len(topo.engines(far if relay is None else relay, here)), [], [buf + "L" + half], (), [me])
 
     for t in range(RO):
         now[0] = t
         last = t == RO - 1
         wk, zk = ("WI", "Z0") if t == 0 else ("WL%d" % (t - 1), "ZL%d" % (t - 1))
-        wl, z = T[wk][:, 0:12], T[zk]
-        wks = [wk + "_0", wk + "_1"]
-        ZO, zo = T["ZO%d" % t], "ZO%d" % t
-        step("zr")
-        act(T.ZR[:], z[:], F.Relu, [zk], ["ZR"], bias=23.0, scale=-1.0)
-        step("wb")
-        act(T.WB[:], IOw.indirect(wl), F.Identity, ["IO", "IOt"] + wks, ["WB"], bias=OFF)
+        wl, z, ZO = T[wk][:, 0:12], T[zk], T["ZO%d" % t]
+        wks, zks, zos = [wk + "_0", wk + "_1"], [zk + "_0", zk + "_1"], ["ZO%d_0" % t, "ZO%d_1" % t]
+        for c in range(2):
+            step("zr%d" % c)
+            act(T.ZR[:, hs(c)], z[:, hs(c)], F.Sign, [zks[c]], ["ZR%d" % c])
+            step("wb%d" % c)
+            act(T.WB[:, hs(c)], IOw.indirect(T[wk][:, hs(c, 6)]), F.Identity, ["IO", "IOt", wks[c]], ["WB%d" % c], bias=OFF)
         step("idw")
         cp(T.IDL[:, 12:24], wl, wks, ["IDw"])
         step("clw")
         ncode(T.CL2[:, 12:24], T.IDL[:, 12:24], ["IDw"], ["CLw"], off=0.0)
         for c in range(2):
-            wc, k, P = T[wk][:, hs(c, 6)], wks[c], "PD%d" % c
+            wc, k = T[wk][:, hs(c, 6)], wks[c]
             step("e%d" % c)
             if t == 0:
                 ts(T.E16[:, hs(c)], T.NM[:, 0:W].indirect(wc), 1.0 / 4096, None, A.mult, None, ["NM0", "NM1", "NM2", k], ["E16%d" % c])
@@ -429,19 +446,22 @@ def rank_program(g, core, T, topo):
                 ts(T.E16[:, hs(c)], MTw.indirect(wc), 1.0 / 4096, float(TOP), A.mult, A.add, ["MT", k], ["E16%d" % c])
             step("wc%d" % c)
             ncode(T.WC[:, hs(c)], IOw.indirect(wc), ["IO", "IOt", k], ["WC%d" % c], off=0.0)
+        for c in range(2):
+            P = "PD%d" % c
             step("gN%d" % c)
-            ncode(T.NG[:, hs(c, 1536)], NTw.indirect(T.E16[:, hs(c)]), ["NT", "NTt", "E16%d" % c], ["NG%d" % c])
+            ncode(T.NG[:, hs(c, 1536)], NTw.indirect(T.E16[:, hs(c)]), ["NT", "NT0", "NT1", "NTt", "E16%d" % c], ["NG%d" % c])
             step("gX%d" % c)
             if c == 0:
                 cp(T.XG[:, hs(c, 1536)], XTw.indirect(T.E16[:, hs(c)]), ["XT", "XTt", "E16%d" % c], ["XG%d" % c])
             else:
                 act(T.XG[:, hs(c, 1536)], XTw.indirect(T.E16[:, hs(c)]), F.Copy, ["XT", "XTt", "E16%d" % c], ["XG%d" % c])
             step("open%d" % c)
-            keys_open(c, 2)
-            wide = [keys_add(c, T.ZR, "ZR", "BOX")]
+            keys_open(c)
+            wide = [keys_add(c, T.ZR, "ZR%d" % c, "BX8")]
             if c == 0:
+                wide.append(keys_add(0, z, zks[0], "BOX"))
                 step("fourz")
-                four(z, zk, 0, "CB1")
+                four(z, zks[0], 0, "CB1")
                 step("sumX")
                 wide += keys_sum(0, lambda k_: kview(T.XG, 0, k_), "XG0", "Wm")
                 for j in range(4):
@@ -451,23 +471,24 @@ def rank_program(g, core, T, topo):
                     for e in range(4):
                         wide.append(mm(kcols(T.PD0, j + 4 * e), T.MX[:, s + e:s + 4 * H:4], T.W2[:], False, False, ["MX%d" % j, "W2"], [P], P))
             else:
-                wide.append(keys_add(1, z, zk, "BOX"))
                 for q in range(4):
                     X, keys = "PX%d" % (q % 2), whole[q % 2][0:2]
-                    step("diff" + "abcd"[q])
+                    step("diff1" + "abcd"[q])
                     for e in range(4):
                         o = T[X][:, H * e:H * e + H]
                         mm(o, T.Ib[:], kview(T.XG, 1, 4 * q + e), True, False, ["Ib", "XG1"], keys, X)
-                        mm(o, T.nI[:], z[:, H:L], False, True, ["nI", zk], keys, X)
-                    step("abs" + "abcd"[q])
+                        mm(o, T.nI[:], z[:, hs(1)], False, True, ["nI", zks[1]], keys, X)
+                    step("abs1" + "abcd"[q])
                     s = 1536 + 4 * H * q
                     act(T.MX[:, s:s + 4 * H], T[X][:, 0:4 * H], F.Abs, keys, ["AB%d" % q], [X])
                     keys_sum(1, lambda k_: T.MX[:, 1536 + H * k_:1536 + H * k_ + H], "AB%d" % q, "Wp", range(4 * q, 4 * q + 4))
             step("ef%d" % c)
             if t == 0:
-                ts(T.EF[:, hs(c)], MTw.indirect(wc), 1.0 / 4096, float(TOP), A.mult, A.add, ["MT", k], ["EF%d" % c])
+                ts(T.EF[:, hs(c)], MTw.indirect(T[wk][:, hs(c, 6)]), 1.0 / 4096, float(TOP), A.mult, A.add,
+                   ["MT", "MT0", "MT1", "MTt", "MTu", wks[c]], ["EF%d" % c])
+                ts(T.EF[:, hs(c)], T.EF[:, hs(c)], float(JUNK), None, A.min, None, ["EF%d" % c], ["EF%d" % c])
             else:
-                cp(T.EF[:, hs(c)], T.E16[:, hs(c)], ["E16%d" % c], ["EF%d" % c])
+                ts(T.EF[:, hs(c)], T.E16[:, hs(c)], float(JUNK), None, A.min, None, ["E16%d" % c], ["EF%d" % c])
             step("addE%d" % c)
             keys_add(c, T.EF, "EF%d" % c, "Ih", wide)
             step("fourw%d" % c)
@@ -476,116 +497,139 @@ def rank_program(g, core, T, topo):
             pick(c, "o%d" % c)
             ol, k = T.OL[:, hs(c, 6)], "OL%d" % c
             step("ol%d" % c)
-            cp(ol, T[P][:, 128:134], ["PL%d" % c], [k], [P])
+            ts(ol, T[P][:, 128:134], float(NONE), None, A.min, None, ["PL%d" % c], [k], [P])
             step("u%d" % c)
             ts(T.U16[:, hs(c)], NTw.indirect(ol), PAD - OFF, float(NONE + PAD), A.add, A.min, ["NT", k], ["U16%d" % c])
             step("ob%d" % c)
             act(T.OB[:, hs(c)], IOw.indirect(ol), F.Identity, ["IO", "IOt", k], ["OB%d" % c], bias=-OFF, scale=4096.0)
             step("oc%d" % c)
-            mcode(T.OC[:, hs(c)], T.OB[:, hs(c)], ["OB%d" % c], ["OC%d" % c])
+            ocode(T.OC[:, hs(c)], IOw.indirect(ol), ["IO", "IOt", k], ["OC%d" % c])
+            step("clo%d" % c)
+            ocode(T.CL2[:, hs(c, 6)], T[P][:, 128:134], ["PL%d" % c], ["CLo%d" % c], [P])
             step("ido%d" % c)
-            ts(T.IDL[:, hs(c, 6)], T[P][:, 128:134], float(JUNK), None, A.min, None, ["PL%d" % c], ["IDo%d" % c], [P])
-            step("miss%d" % c)
-            thk = "TH0" if t == 0 else "THR"
-            tt(T.MS[0:H, hs(c, 8)], T.SC[0:H, 128 * c + 15:128 * c + 128:16], T[thk][0:H, hs(c, 8)], A.is_ge, ["SC%d" % c, thk], ["MS%d" % c])
+            act(T.IDL[:, hs(c, 6)], T[P][:, 128:134], F.Copy, ["PL%d" % c], ["IDo%d" % c], [P])
+        step("miss")
+        thk = "TH0" if t == 0 else "THR"
+        tt(T.MS[0:H, :], T.SC[0:H, 15:256:16], T[thk][0:H, :], A.is_ge, ["SC0", "SC1", thk], ["MS"])
+        step("uh")
+        cp(T.UH[:], T.U16[:], ["U160", "U161"], ["UH"])
         ol, olk = T.OL[:, 0:12], ["OL0", "OL1"]
-        step("zo")
         if last:
-            ms(T.XT[:, TOP:TOP + 1], 255.0, ["XT"])
-            cp(ZO[:], XTw.indirect(ol), ["XT"] + olk, [zo])
-        else:
-            ts(ZO[:], XTw.indirect(ol), 31.0, None, A.min, None, ["XT"] + olk, [zo])
+            step("x255")
+            act(T.XT[:, NONE:W], T.ONE[:, 0:1], F.Copy, ["ONE"], ["XT"], scale=31.0 - 255.0)
+        for c in range(2):
+            step("zo%d" % c)
+            if last:
+                act(ZO[:, hs(c)], XTw.indirect(T.OL[:, hs(c, 6)]), F.Identity, ["XT", olk[c]], [zos[c]], bias=31.0, scale=-1.0)
+            else:
+                act(ZO[:, hs(c)], XTw.indirect(T.OL[:, hs(c, 6)]), F.Relu, ["XT", olk[c]], [zos[c]])
         for c in range(2):
             P = "PD%d" % c
             step("gM%d" % c)
             mcode(T.MG[:, hs(c, 1536)], T.MT[:, 0:WIDE].indirect(T.U16[:, hs(c)]), ["MT", "U16%d" % c], ["MG%d" % c])
+            if c == 1:
+                step("qd")
+                mm(T.PD1[:, 160:160 + L], T.Ih[:], T.EF[:], True, False, ["Ih", "EF0", "EF1"], ["QD"], P)
+                mm(T.PD1[:, 160:160 + L], T.Iq[:], T.OB[:], False, True, ["Iq", "OB0", "OB1"], ["QD"], P)
             step("back%d" % c)
-            mm(T[P][0:H, 144:152], T.ONF[0:1, 0:H], T.CK[0:1, :], True, False, ["ONF", "CK"], ["FB%d" % c], P)
-            mm(T[P][0:H, 144:152], T.WB[:, hs(c)], T.Wf[:], False, True, ["WB", "Wf"], ["FB%d" % c], P)
-            keys_open(c, 1)
+            mm(T[P][0:H, 144:152], T.ONF[0:1, :], T.CK[0:1, :], True, False, ["ONF", "CK"], ["FB%d" % c], P)
+            mm(T[P][0:H, 144:152], T.WB[:, hs(c)], T.Wf[:], False, True, ["WB%d" % c, "Wf"], ["FB%d" % c], P)
+            keys_open(c)
             step("fouro%d" % c)
             four(T.OC, "OC%d" % c, c, "CB%d" % c)
-            step("uh%d" % c)
-            cp(T.UH[:, hs(c)], T.U16[:, hs(c)], ["U16%d" % c], ["UH%d" % c])
-            keys_add(c, T.UH, "UH%d" % c, "Ih")
+            step("addU%d" % c)
+            keys_add(c, T.UH, "UH", "Ih")
             step("sumM%d" % c)
             keys_sum(c, lambda k_: kview(T.MG, c, k_), "MG%d" % c, "Wm")
             eq("MG", c, "If2")
             pick(c, "w%d" % c)
             step("wo%d" % c)
             ts(T["WO%d" % t][:, 8 * c:8 * c + 6], T[P][:, 128:134], float(PAD), None, A.subtract, None, ["PL%d" % c], ["WO%d_%d" % (t, c)], [P])
-        for p in SENDS:
-            send(t, p, (zo, "WO%d_0" % t, "WO%d_1" % t)[p])
+        for p in range(len(PIECES)):
+            send(t, p)
         step("openS")
-        mm(T.PS[0:H, 0:32], T.ONE[0:1, 0:H], T.ZERO[0:1, :], True, False, ["ONE", "ZERO"], ["PS"], "PS")
+        mm(T.PS[0:H, 0:32], T.ZB[0:1, 0:H], T.ONE[0:1, 0:32], True, False, ["ZB", "ONE"], ["PS"], "PS")
         first(T.WC, ["WC0", "WC1", "CLw"], 1)
-        step("clo")
-        act(T.CL2[:, 0:12], T.IDL[:, 0:12], F.Sigmoid, ["IDo0", "IDo1"], ["CLo"], bias=7.0 - TOP * SLOPE, scale=SLOPE)
         step("rows")
         for c in range(2):
-            mm(T.PS[0:H, 16 + 8 * c:24 + 8 * c], T.IB[0:H, :], T.MS[0:H, hs(c, 8)], False, False, ["IB", "MS%d" % c], ["PS"], "PS")
-            mm(T.PX1[0:8, hs(c)], T.MS[0:H, hs(c, 8)], T.Ib[0:H, 0:H], True, True, ["Ib", "MS%d" % c], ["PX1"], "PX1")
-        first(T.OC, ["OC0", "OC1", "CLo"], 0)
+            mm(T.PS[0:H, 16 + 8 * c:24 + 8 * c], T.IB[0:H, :], T.MS[0:H, hs(c, 8)], False, False, ["IB", "MS"], ["PS"], "PS")
+            mm(T.PX1[0:8, hs(c)], T.MS[0:H, hs(c, 8)], T.Ib[0:H, 0:H], True, True, ["Ib", "MS"], ["PX1"], "PX1")
+        first(T.OC, ["OC0", "OC1", "CLo0", "CLo1"], 0)
         step("hit")
         act(T.HR[0:8, :], T.PX1[0:8, 0:L], F.Identity, ["PX1"], ["HR", "WIN"], ["PX1"], bias=1.0, scale=-1.0, acc=T.WIN[0:8, 0:1])
         mm(T.PX0[:, 0:L], T.EXB[0:8, :], T.HR[0:8, :], True, False, ["EXB", "HR"], ["PX0"], "PX0")
         mm(T.PX0[:, 0:L], T.Ib[:], T.RN[:, t:t + L], False, True, ["Ib", "RN"], ["PX0"], "PX0")
         if not last:
-            for c in range(2):
-                o = T.PX0[:, L + H * c:L + H * c + H]
-                mm(o, T.ONE[0:1, :], T.ONE[0:1, 0:H], True, False, ["ONE"], ["miss"], "PX0")
-                mm(o, T.EXN[0:8, :], T.HR[0:8, hs(c)], False, True, ["EXN", "HR"], ["miss"], "PX0")
             mm(T.PX1[:, 400:401], T.UF[0:8, :], T.WIN[0:8, 0:1], True, False, ["UF", "WIN"], ["wins"], "PX1")
             mm(T.PX1[:, 400:401], T.ONE[0:1, :], T.HLF[0:1, 0:1], False, True, ["ONE", "HLF"], ["wins"], "PX1")
             step("dx")
-            mm(T.PX1[:, L:2 * L], T.Ib[:], z[:], True, False, ["Ib", zk], ["dx"], "PX1")
-            mm(T.PX1[:, L:2 * L], T.nI[:], ZO[:], False, True, ["nI", zo], ["dx"], "PX1")
+            mm(T.PX1[:, L:2 * L], T.Ib[:], z[:], True, False, ["Ib"] + zks, ["dx"], "PX1")
+            mm(T.PX1[:, L:2 * L], T.nI[:], ZO[:], False, False, ["nI"] + zos, ["dx"], "PX1")
+            mm(T.PX1[:, L:2 * L], T.EXN[0:8, :], T.HR[0:8, :], False, True, ["EXN", "HR"], ["dx"], "PX1")
+        step("no")
+        act(T.DN[:], NTw.indirect(ol), F.Copy, ["NT"] + olk, ["DN"])
         step("dn")
-        tt(T.DN[:], NTw.indirect(ol), T.WB[:], A.subtract, ["NT", "WB"] + olk, ["DN"])
+        mm(T.PX1[:, 0:L], T.ID[:], T.DN[:], True, False, ["ID", "DN"], ["PX1"], "PX1")
+        mm(T.PX1[:, 0:L], T.nF[:], T.WB[:], False, True, ["nF", "WB0", "WB1"], ["PX1"], "PX1")
+        step("sb")
+        act(T.SB[:], T.PX0[:, 0:L], F.Copy, ["PX0"], ["SB"], ["PX0"])
         step("q")
-        tt(T.Q[:], MTw.indirect(wl), T.OB[:], A.is_equal, ["MT", "OB0", "OB1"] + wks, ["Q"])
+        act(T.Q[:], T.PD1[:, 160:160 + L], F.Abs, ["QD"], ["Q"], ["PD1"], bias=-float(TOP))
+        act(T.Q[:], T.Q[:], F.Relu, ["Q"], ["Q"], bias=1.0, scale=-1.0)
         step("kn")
-        tt(T.KN[:], T.DN[:], T.PX0[:, 0:L], A.mult, ["DN", "PX0"], ["KN"], ["PX0"])
+        tt(T.KN[:], T.SB[:], T.PX1[:, 0:L], A.mult, ["SB", "PX1"], ["KN"], ["PX1"])
         step("ff")
-        tt(T.FF[0:H, :], T.PS[0:H, 0:32], T.TC[0:H, :], A.is_ge, ["PS"] + ["TC" + s for s in four_], ["FF"], ["PS"])
+        tt(T.FF[0:H, :], T.PS[0:H, 0:32], T.TC[0:H, :], A.is_ge, ["PS"] + ["TC" + s for s in "0123"], ["FF"], ["PS"])
         step("od")
-        tt(T.OD[:], T.FF[:, 0:32].indirect(T.CV[:, 0:12]), T.MD[:], A.mult, ["FF", "CV"] + ["MD" + s for s in four_], ["OD"])
+        tt(T.OD[:], T.FF[:, 0:32].indirect(T.CV[:, 0:12]), T.MD[:], A.mult, ["FF", "CV"] + ["MD" + s for s in "0123"], ["OD"])
         to_list(T.PS[:, 32:56], T.OD, 0, L, "OD", "PO", "PS")
         step("of")
         tt(T.OF[:], T.IDL[:], T.PS[:, 32:56], A.max, ["IDo0", "IDo1", "IDw", "PO"], ["OF"], ["PS"])
         step("ofu")
         cp(T.OFU[:], T.OF[:], ["OF"], ["OFU"])
         step("putN")
-        tt(NTw.indirect(T.OFU[:, 0:12]), T.WB[:], T.KN[:], A.add, ["WB", "KN", "OFU"], ["NT"])
+        tt(NTw.indirect(T.OFU[:, 0:12]), T.WB[:], T.KN[:], A.add, ["WB0", "WB1", "KN", "OFU"], ["NT"])
         step("putM")
         tt(MTw.indirect(T.OFU[:, 12:24]), T.OB[:], T.Q[:], A.mult, ["OB0", "OB1", "Q", "OFU"], ["MT"])
         if not last:
             step("cl")
-            ts(T.CL[:], T.PX1[:, L:2 * L], -2.0, 2.0, A.max, A.min, ["dx"], ["CL"], ["PX1"])
+            act(T.CL[:], T.PX1[:, L:2 * L], F.Abs, ["dx"], ["CL"], ["PX1"], bias=1.0, scale=0.5)
+            act(T.CM[:], T.PX1[:, L:2 * L], F.Abs, ["dx"], ["CM"], ["PX1"], bias=-1.0, scale=0.5)
+            o = T.PX0[:, L:2 * L]
+            mm(o, T.Ib[:], ZO[:], True, False, ["Ib"] + zos, ["xn"], "PX0")
+            mm(o, T.EX2[0:8, :], T.HR[0:8, :], False, False, ["EX2", "HR"], ["xn"], "PX0")
+            mm(o, T.Ib[:], T.CL[:], False, False, ["Ib", "CL"], ["xn"], "PX0")
+            mm(o, T.nI[:], T.CM[:], False, True, ["nI", "CM"], ["xn"], "PX0")
             step("cm")
-            tt(T.CM[:], T.CL[:], T.PX0[:, L:2 * L], A.mult, ["CL", "miss"], ["CM"], ["PX0"])
+            act(T.XN[:], o, F.Copy, ["xn"], ["XN"], ["PX0"])
             step("putX")
-            tt(XTw.indirect(T.OFU[:, 0:12]), ZO[:], T.CM[:], A.add, [zo, "CM", "OFU"], ["XT"])
+            cp(XTw.indirect(T.OFU[:, 0:12]), T.XN[:], ["XN", "OFU"], ["XT"])
             step("ss")
-            ts(T.SS[:, 0:1], T.PX1[:, 400:401], 1.5 * 2.0 ** 43, 1.5 * 2.0 ** 43, A.add, A.subtract, ["wins"], ["SS"], ["PX1"])
+            ts(T.WIN[:, 1:2], T.PX1[:, 400:401], 1.5 * 2.0 ** 43, 1.5 * 2.0 ** 43, A.add, A.subtract, ["wins"], ["SS"], ["PX1"])
             step("thr")
-            ts(T.THR[0:H, :], T.TH1[0:H, :], T.PX1[0:H, 400:401], T.SS[0:H, 0:1], A.add, A.subtract, ["TH1", "wins", "SS"], ["THR"], ["PX1"])
+            ts(T.THR[0:H, :], T.TH1[0:H, :], T.PX1[0:H, 400:401], T.WIN[0:H, 1:2], A.add, A.subtract, ["TH1", "wins", "SS"], ["THR"], ["PX1"])
 
     t = RO - 1
     top = NONE * 4096.0
     step("outz")
-    dma("S", T.yz[:], T["ZL%d" % t][:], "st", r=["ZL%d" % t])
+    dma("S", T.yz[:], T["ZL%d" % t][:], "st", r=["ZL%d_0" % t, "ZL%d_1" % t])
     for j in range(3):
         c = hs(j, 512)
         step("absN%d" % j)
         act(T.FT[:, c], T.NT[:, c], F.Abs, ["NT"], ["FT%d" % j], bias=-OFF)
         step("cutN%d" % j)
-        ts(T.FT[:, c], T.FT[:, c], float(NONE), top, A.min, A.add, ["FT%d" % j], ["FT%d" % j])
+        if j < FIN:
+            act(T.FT[:, c], T.FT[:, c], F.Relu, ["FT%d" % j], ["FT%d" % j], bias=float(NONE), scale=-1.0)
+            act(T.FT[:, c], T.FT[:, c], F.Identity, ["FT%d" % j], ["FT%d" % j], bias=top + NONE, scale=-1.0)
+        else:
+            ts(T.FT[:, c], T.FT[:, c], float(NONE), top, A.min, A.add, ["FT%d" % j], ["FT%d" % j])
         step("cutM%d" % j)
         act(T[banks[j]][:], T.MT[:, PAD + 512 * j:PAD + 512 * j + 512], F.Relu, ["MT"], whole[j], [banks[j]], bias=top - OFF, scale=-1.0)
-        step("out%d" % j)
-        tt(T.OUT[:, c], T.FT[:, c], T[banks[j]][:], A.subtract, ["FT%d" % j, banks[j]], ["OUT%d" % j], [banks[j]])
-        dma("S", T.ynm[:, c], T.OUT[:, c], "st", r=["OUT%d" % j])
+        for i in range(2):
+            step("out%d%s" % (j, "ab"[i]))
+            c = hs(2 * j + i, 256)
+            tt(T.OUT[:, c], T.FT[:, c], T[banks[j]][:, hs(i, 256)], A.subtract, ["FT%d" % j, banks[j]], ["OUT%d%d" % (j, i)], [banks[j]])
+            dma("SA"[i], T.ynm[:, c], T.OUT[:, c], "st", r=["OUT%d%d" % (j, i)])
     step("outw")
     dma("A", T.yw[:], T["WL%d" % t][:], "st", r=["WL%d_0" % t, "WL%d_1" % t])
     issue()

from concourse.mybir import AluOpType as A, AxisListType, ActivationFunctionType as F

W, L, RO, NR = 1536, 192, 4, 6
NONE = W - 1
H = 96
TOP = 2047
OFF = 4096.0 * TOP
JUNK, DUMP = 1536, 1600
PAD = 8
U = 32768.0
BIG = 2.0 ** 99
SLOPE = 23.0 / 512
WIDE = 2048
FIN = 1
VFLAGS = ("M0",)
EARLY = ("e0 e1 wc0 wc1 gN0 gN1 gX0 gX1 zr0 zr1 wb0 wb1 open0 open1 fourw0 fourw1 eqN0a eqN0b eqN0c eqN0d maxa maxb maxc maxd fourz sumX ef0 ef1 "
         "addE0 addE1 flagN0 idw scano0 lowo0 listo0").split()
LATE = ("dn ff od kn of ofu q putN putM no sb hit zo1 eqM1a eqM1b eqM1c eqM1d flagM1 scanw1 intw1 loww1 listw1 wo1 sumM1 gM1 scanw0 intw0 loww0 listw0 wo0 "
        "sameo0 sameo1 sameo2 sameo3 sameo4 sameo5").split()

f32, bf, f16, i32, u16 = "float32", "bfloat16", "float16", "int32", "uint16"
SCRATCH = {}
for _n, _c, _d in [
    ("NM", W, i32), ("NT", WIDE, f32), ("MT", WIDE + PAD, f32), ("XT", WIDE, bf), ("FT", W, f32), ("OUT", W, f32),
    ("IO", W, f32), ("NG", 3072, bf), ("MG", 3072, bf), ("XG", 3072, bf), ("MX", 3072, bf), ("EQ", 3072, bf),
    ("W32", 12, i32), ("TH", 1, i32), ("Z0", L, bf), ("WI", 16, u16),
    ("RP", 24, u16), ("RN", 208, bf), ("PJ", 8, i32), ("PF", 4, f32),
    ("CI", 128, f32), ("KI", 128, f32), ("RS", 128, f32), ("CR", 128, bf), ("CK", 8, f32),
    ("ONE", 128, bf), ("ONF", H, f32), ("UF", 128, f32), ("HLF", 2, bf), ("ZB", H, bf),
    ("ID", 128, f32), ("Ih", 128, f16), ("Ib", 128, bf), ("nI", 128, bf), ("IB", H, bf), ("nF", 128, f32), ("Iq", 128, f32),
    ("If1", H, bf), ("If2", H, bf), ("BOX", 128, bf), ("BX8", 128, bf), ("W1", 8, bf), ("W2", 8, bf), ("Wm", 8, bf),
    ("Wp", 8, bf), ("Wf", 8, f32), ("Wt", 8, bf), ("EXB", 128, bf), ("EXN", 128, bf), ("EX2", 128, bf), ("SEL", 240, f16), ("SI", 16, f32),
    ("P2", H, f32), ("HF", H + 12, f32), ("TP", H, f32),
    ("CV", 12, u16), ("BI", 60, f32), ("MK", 48, f32), ("MD", L, f32), ("WT", 12, bf),
    ("TC", 32, f32), ("T1", 8, f32), ("THB", H, bf), ("TH0", 16, f32), ("TH1", 16, f32), ("THR", 16, f32),
    ("E16", L, u16), ("U16", L, u16), ("EF", L, f16), ("UH", L, f16), ("WC", L, bf), ("OC", L, bf), ("ZR", L, bf),
    ("FL", 256, bf), ("SC", 256, i32), ("S32", 16, i32), ("O32", 16, i32), ("OA", 96, f16), ("OL", 12, u16),
    ("IDL", 24, f32), ("CL2", 24, bf), ("MS", 16, bf), ("HR", L, bf), ("WIN", 2, f32), ("WB", L, f32), ("OB", L, f32),
    ("EE", 18 * H, bf), ("FF", 32, bf), ("OD", L, f16), ("OF", 24, f32), ("OFU", 24, u16),
    ("DN", L, f32), ("SB", L, bf), ("KN", L, f32), ("Q", L, f32), ("CL", L, bf), ("CM", L, bf), ("XN", L, bf),
]:
    SCRATCH[_n] = ("sbuf", [128, _c], _d)
for _t in range(RO):
    SCRATCH["ZO%d" % _t] = ("sbuf", [128, L], bf)
    SCRATCH["ZL%d" % _t] = ("sbuf", [128, L], bf)
    SCRATCH["WO%d" % _t] = ("sbuf", [128, 16], u16 if _t < RO - 1 else f32)
    SCRATCH["WL%d" % _t] = ("sbuf", [128, 12], u16 if _t < RO - 1 else f32)
for _n in ["PD0", "PD1", "PC", "CB0", "CB1", "PX0", "PX1", "PS"]:
    SCRATCH[_n] = ("psum", [128, 512], f32)

SEMAPHORES = (["sV", "sA", "sP", "sG", "sent", "lw", "lz", "lt", "lx", "ln0", "ln1", "ln2", "st"]
              + ["%s%d" % (s, t) for t in range(RO) for s in ("za", "wa", "zb", "wb")])
PIECES = (("za", "Z", 0, H, 0), ("wa", "W", 0, 6, 0), ("zb", "Z", H, L, H), ("wb", "W", 6, 12, 8))

ORDER = """
load kx kpow idw_ tabY2 e1_ tabY1 e0_ tabY0 tabN2 tabN0 maxb_ +out0b tabN1 maxd_ gX0_ tabM0 eqN0a_ maxa_ gap0 wb0_ wc0_ +listw1 gN0_ +out0a gX1_
fourz_ fourw0_ sumX_ eqN0b_ open0_ eqN0d_ eqN0c_ zr1_ open1_ gap2 wc1 gap1 gN0 ef0_ kpick flagN0_ wc1_ +kn flagN0 gM0 zr0_ wb0 +outw addE0_ zr0 ef1_
openS e1 +putM gN1_ +cm fourw1_ +cl fourz +wo1 tabM2 +putN open0 wc0 diff1c +putX e0 maxc_ tabM1 gX0 +send3 fourw0 eqN0b zr1 eqN0a diff1d sumX maxd
eqN0d gX1 eqN0c addE0 gN1 diff1b maxb scano0_ lowo0 maxc maxa ef0 +ss idw open1 ef1 diff1a fourw1 scano0 addE1 listo0 abs1b lowo0_ wb1_ kdump listo0_
wb1 eqN1a addE1_ abs1a clw eqN1d ol0 eqN1b eqN1c abs1d oc0 zo0 samew0 abs1c flagN1 u0 +thr kth scano1 fouro0 samew2 back0 lowo1 samew5 miss listo1
samew4 samew1 clo0 samew3 ob1 oc1 gM1 ol1 rows sumM0 hit clo1 eqM0c ob0 u1 eqM0a eqM0b addU0 eqM0d sameo2' fouro1 sameo5 addU1 uh sameo1' sameo4'
sameo3 flagM0 sameo0' of' dn' sameo3' sameo5' scanw0' ff' gM1' qd back1 eqM1d' intw0' hit' od' sameo0 no' sameo4 loww0' eqM1b' send0 scanw0 sameo1
flagM1' x255 intw0 listw0' ido1 ido0 zo1' q' sb' ofu' eqM1c' eqM1a' kn' wo0' sumM1 scanw1' zo1 cutM2 putN' sumM1' sameo2 dn loww0 eqM1d absN2 absN1
cutM1 dx eqM1c eqM1a eqM1b ff intw1' listw0 flagM1 od wo0 send1 absN0 putM' cutM0 cutN0 loww1' listw1' out1a cutN2 no wo1' out2b out2a send2 out1b
loww1 cutN1 scanw1 outz sb of intw1 q ofu
""".split()


def route(T, topo, r, t):
    src = T.cores[r]
    dst = T.cores[(r + 1 + t % (NR - 1)) % NR]
    if topo.may_write(src, dst):
        return src, None, dst
    cand = [c for c in topo.cores_of(src) if c != src and T.rank_of(c) is None and topo.may_write(c, dst)]
    cand.sort(key=lambda c: topo.die(c) != topo.die(src))
    return src, cand[0], dst


def put(g, T, topo, src, dst, out, in_, sem):
    rid, pid = topo.addr(dst, src)
    g.remote_dma(out, in_, T.sem[sem], T.sem.sent, pid, rid, topo.mask(src, dst))
    return len(topo.engines(src, dst))


def relay_program(g, core, T, topo):
    sent = 0
    for t in range(RO):
        for r in range(NR):
            src, via, dst = route(T, topo, r, t)
            if via != core:
                continue
            n = len(topo.engines(src, core))
            for sem, buf, lo, hi, _ in PIECES:
                ap = T["%sL%d" % (buf, t)][:, lo:hi]
                g.wait_ge(T.sem["%s%d" % (sem, t)], n)
                sent += put(g, T, topo, core, dst, ap, ap, "%s%d" % (sem, t))
    if sent:
        g.wait_ge(T.sem.sent, sent)


def rank_program(g, core, T, topo):
    rank = T.rank_of(core)
    if rank is None:
        relay_program(g, core, T, topo)
        return
    Q = {"V": g.vector, "A": g.scalar, "P": g.tensor, "G": g, "S": g.sync}
    calls = []
    lastw, readers = {}, {}
    now = [0, ""]
    sent = [0]

    def step(name):
        now[1] = name + "'" * (now[0] == RO - 1 and name in LATE) + "_" * (now[0] == 0 and name in EARLY)

    def record(q, fn, sem, inc, r, w, b=(), after=()):
        pre = set(after)
        for k in r:
            pre.add(lastw[k])
        for k in w:
            if k in lastw:
                pre.add(lastw[k])
            pre.update(readers.get(k, ()))
        me = len(calls)
        calls.append((q, fn, sem, inc, tuple(b), tuple(now), sorted(pre)))
        for k in r:
            readers.setdefault(k, []).append(me)
        for k in w:
            lastw[k] = me
            readers[k] = []
        return me

    def op(q, fn, r=(), w=(), b=(), after=()):
        return record(q, fn, "s" + q, 1, r, w, b, after)

    def dma(q, out, in_, sem, r=(), w=()):
        record(q, lambda: Q[q].dma_start(out, in_), sem, 16, r, w)

    def issue():
        place = {name.lstrip("+"): i + len(ORDER) * name.count("+") for i, name in enumerate(ORDER)}
        nxt = [[] for _ in calls]
        for i, c in enumerate(calls):
            for p in c[6]:
                nxt[p].append(i)
        left = [len(c[6]) for c in calls]
        turn = [(c[5][0] * len(ORDER) + place[c[5][1]], i) for i, c in enumerate(calls)]
        ready = [i for i in range(len(calls)) if not left[i]]
        cnt, tok, bank = {}, {}, {}
        waited = {q: {} for q in Q}
        while ready:
            i = min(ready, key=lambda j: turn[j])
            ready.remove(i)
            q, fn, sem, inc, banks_, _, pre = calls[i]
            for j in nxt[i]:
                left[j] -= 1
                if not left[j]:
                    ready.append(j)
            if q == "R":
                tok[i] = (sem, inc)
                continue
            toks = [tok[p] for p in pre if tok[p]] + [x for k in banks_ for x in bank.get(k, {}).items() if x[0] != sem]
            most = {}
            for sm, m in toks:
                if not (q == "P" and sm == sem):
                    most[sm] = max(most.get(sm, 0), m)
            for sm, m in most.items():
                if waited[q].get(sm, 0) < m:
                    Q[q].wait_ge(T.sem[sm], m)
                    waited[q][sm] = m
            if sem is None:
                fn()
                tok[i] = None
                continue
            cnt[sem] = cnt.get(sem, 0) + inc
            fn().then_inc(T.sem[sem], inc)
            tok[i] = (sem, cnt[sem])
            for k in banks_:
                bank.setdefault(k, {})[sem] = cnt[sem]
        for sm, m in list(cnt.items()) + [("sent", sent[0])]:
            if waited["G"].get(sm, 0) < m:
                g.wait_ge(T.sem[sm], m)

    v, a = g.vector, g.scalar

    def ts(out, in0, s1, s2, o0, o1, r, w, b=()):
        if o1 is None:
            op("V", lambda: v.tensor_scalar(out, in0, s1, None, o0), r, w, b)
        else:
            op("V", lambda: v.tensor_scalar(out, in0, s1, s2, o0, o1), r, w, b)

    def tt(out, in0, in1, o, r, w, b=()):
        op("V", lambda: v.tensor_tensor(out, in0, in1, o), r, w, b)

    def cp(out, in_, r, w, b=()):
        op("V", lambda: v.tensor_copy(out, in_), r, w, b)

    def ms(out, c, w, b=()):
        op("V", lambda: v.memset(out, c), (), w, b)

    def scan(out, d0, d1, first_, o0, o1, r, w, b=()):
        op("V", lambda: v.tensor_tensor_scan(out, d0, d1, first_, o0, o1), r, w, b)

    def total(out, in_, r, w):
        op("V", lambda: v.tensor_reduce(out, in_, AxisListType.X, A.add), r, w)

    def act(out, in_, f, r, w, b=(), bias=0.0, scale=1.0, acc=None):
        op("A", lambda: a.activation(out, in_, f, bias=bias, scale=scale, accum_out=acc), r, w, b)

    def mm(out, lhsT, rhs, start, stop, r, w, b, after=()):
        if start and stop:
            r = list(r) + ["shut" + b] if "shut" + b in lastw else r
        elif start or stop:
            w = list(w) + ["open" + b, "shut" + b]
        else:
            r, w = list(r) + ["open" + b], []
        return op("P", lambda: g.tensor.matmul(out, lhsT, rhs, start, stop), r, w, [b], after)

    def iota(out, pat, base, cm, w, fl=True):
        if fl:
            op("G", lambda: g.iota(out, pat, base, cm, allow_small_or_imprecise_dtypes=True), (), w)
        else:
            op("G", lambda: g.iota(out, pat, base, cm), (), w)

    def mcode(out, in_, r, w):
        act(out, in_, F.Sigmoid, r, w, bias=7.0, scale=SLOPE / 4096)

    def ocode(out, in_, r, w, b=()):
        act(out, in_, F.Sigmoid, r, w, b, bias=7.0 - TOP * SLOPE, scale=SLOPE)

    def ncode(out, in_, r, w, off=OFF):
        act(out, in_, F.Sigmoid, r, w, bias=-off / 32 - 80.0, scale=1.0 / 32)

    NTw, MTw, XTw, IOw = T.NT[:, 0:WIDE], T.MT[:, PAD:PAD + WIDE], T.XT[:, 0:WIDE], T.IO[:, 0:W]

    def hs(c, n=H):
        return slice(n * c, n * c + n)

    step("load")
    dma("S", T.NM[:, 0:512], T.nm[:, 0:512], "ln0", w=["NM0"])
    dma("A", T.NM[:, 512:1024], T.nm[:, 512:1024], "ln1", w=["NM1"])
    dma("S", T.NM[:, 1024:W], T.nm[:, 1024:W], "ln2", w=["NM2"])
    dma("A", T.W32[:], T.w[:], "lw", w=["W32"])
    dma("S", T.XT[:, 0:W], T.x[:], "lx", w=["XT"])
    dma("S", T.Z0[:], T.z[:], "lz", w=["Z0"])
    dma("S", T.TH[:], T.th[:], "lt", w=["TH"])

    iota(T.PJ[:, 4:6], [[0, 2]], 0, 1, ["PI"], False)
    iota(T.CI[:], [[1, 128]], 0, 0, ["CI"])
    iota(T.KI[:], [[0, 8], [1, 16]], 0, 0, ["KI"])
    iota(T.BI[:, 0:48], [[1, 6], [0, 8]], 0, 0, ["BI"])
    iota(T.BI[:, 48:60], [[8, 4], [0, 3]], 0, 0, ["CF"])
    iota(T.IO[:, 0:NONE], [[1, NONE]], 0, 0, ["IO"])
    iota(T.NT[:, W:WIDE], [[0, WIDE - W]], int(NONE + OFF), 0, ["NTt"])
    iota(T.MT[:, PAD + W:PAD + WIDE], [[0, WIDE - W]], 0, 0, ["MTu"])
    iota(T.O32[:], [[0, 16]], 0, 0, ["O320", "O321"], False)
    iota(T.FF[:], [[0, 32]], 0, 0, ["FF"])
    iota(T.UF[0:8, :], [[0, 128]], int(U), 0, ["UF"])
    iota(T.HLF[0:1, :], [[0, 2]], int(-15.5 * U), 0, ["HLF"])
    iota(T.MT[:, 0:PAD], [[0, PAD]], 0, 0, ["MTt"])
    iota(T.ZB[0:1, :], [[0, H]], 0, 0, ["ZB"])
    iota(T.ONF[0:1, :], [[0, H]], 1, 0, ["ONF"])
    iota(T.CK[0:1, :], [[0, 8]], int(PAD - OFF - 17 * U), 0, ["CK"])
    iota(T.EE[:], [[0, 18 * H]], 0, 0, ["EEz"])
    pi, pf, pm, pg, p8 = T.PJ[:, 4:5], T.PF[:, 0:1], T.PF[:, 1:2], T.PF[:, 2:3], T.PF[:, 3:4]
    ms(T.IO[:, NONE:W], float(JUNK), ["IOt"])
    ms(T.XT[:, W:WIDE], -8.0, ["XTt"])
    act(T.ONE[:], T.CI[:], F.Sigmoid, ["CI"], ["ONE"], bias=30.0)
    ms(T.SEL[:], 0.0, ["SEL"])
    ms(T.HF[:, 0:H], 0.5, ["HFa"])
    ms(T.HF[:, H:H + 12], 2.0 ** -16, ["HFb"])
    ts(T.PJ[:, 0:1], pi, 15, None, A.bitwise_and, None, ["PI"], ["PJ0"])
    ts(T.PJ[:, 1:2], pi, 4, None, A.logical_shift_right, None, ["PI"], ["PJ1"])
    ts(T.PJ[:, 2:3], pi, 7, None, A.bitwise_and, None, ["PI"], ["PJ2"])
    cp(pf, pi, ["PI"], ["pf"])
    cp(T.PF[:, 1:4], T.PJ[:, 0:3], ["PJ0", "PJ1", "PJ2"], ["pm"])
    ts(T.ID[:], T.CI[:], pf, None, A.is_equal, None, ["CI", "pf"], ["ID"])
    ts(T.W1[:], T.CI[:, 0:8], pg, None, A.is_equal, None, ["CI", "pm"], ["W1"])
    cp(T.Wf[:], T.ID[:, 0:128:16], ["ID"], ["Wf"])
    cp(T.Ih[:], T.ID[:], ["ID"], ["Ih"])
    ts(T.SI[:], T.CI[:, 0:16], pm, None, A.is_equal, None, ["CI", "pm"], ["SI"])
    cp(T.SEL[:, 112:128], T.SI[:], ["SI"], ["SEL"])
    cp(T.RP[:, 0:8], T.CI[:, 0:8], ["CI"], ["RPa"])
    ts(T.RP[:, 8:24], T.ONE[:, 0:16], pm, None, A.mult, None, ["ONE", "pm"], ["RPb"])
    for name, c in (("W2", 2 * U), ("Wm", -U), ("Wp", U), ("Wt", U / 16)):
        act(T[name][:], T.W1[:], F.Copy, ["W1"], [name], scale=c)
    for name, c, n in (("Ib", 1.0, 128), ("nI", -1.0, 128), ("If1", -370 * U, H), ("If2", -18 * U, H), ("IB", BIG, H), ("nF", -1.0, 128),
                       ("Iq", -1.0 / 4096, 128)):
        act(T[name][0:n, :], T.ID[0:n, 0:n], F.Copy, ["ID"], [name], scale=c)
    act(T.BOX[:], T.W1[:, 0:8].indirect(T.RP[:, 0:8]), F.Copy, ["W1", "RPa"], ["BOX"], scale=-U)
    act(T.BX8[:], T.BOX[:], F.Copy, ["BOX"], ["BX8"], scale=8.0)
    act(T.EXB[:], T.ID[:, 0:8].indirect(T.RP[:, 0:8]), F.Copy, ["ID", "RPa"], ["EXB"], scale=4096.0)
    act(T.EXN[:], T.EXB[:], F.Copy, ["EXB"], ["EXN"], scale=64.0 / 4096)
    act(T.EX2[:], T.EXB[:], F.Copy, ["EXB"], ["EX2"], scale=-2.0 / 4096)
    act(T.RN[:], T.SI[:, 0:16].indirect(T.RP[:, 8:21]), F.Identity, ["SI", "RPb"], ["RN"], bias=1.0, scale=-1.0)
    act(T.CR[0:1, :], T.KI[0:1, :], F.Copy, ["KI"], ["CR"], scale=2048.0)
    act(T.RS[0:H, :], T.KI[0:H, :], F.Relu, ["KI"], ["RS"], bias=1e8, scale=-1e8)
    cp(T.WI[:, 0:12], T.W32[:], ["W32"], ["WI_0", "WI_1"])

    banks = ["PX0", "PX1", "PS"]
    whole = [["PX0", "xn"], ["PX1", "dx", "wins"], ["PS", "PO"]]
    magic = 1.5 * 2.0 ** 35
    gap = float(TOP - NONE)
    for j in range(3):
        c = hs(j, 512)
        step("tabY%d" % j)
        ts(T[banks[j]][:], T.NM[:, c], magic, magic + OFF, A.add, A.subtract, ["NM%d" % j], whole[j], [banks[j]])
        step("tabN%d" % j)
        tt(T.NT[:, c], T.NM[:, c], T[banks[j]][:], A.subtract, ["NM%d" % j] + whole[j], ["NT%d" % j] + ["NT"] * (j == 2), [banks[j]])
        step("gap%d" % j)
        act(T.FT[:, c], T[banks[j]][:], F.Relu, whole[j], ["FT%d" % j], [banks[j]], bias=(gap + 1) * gap * 4096, scale=gap)
        step("tabM%d" % j)
        tt(T.MT[:, PAD + 512 * j:PAD + 512 * j + 512], T.FT[:, c], T[banks[j]][:], A.add, ["FT%d" % j] + whole[j],
           ["MT%d" % j] + ["MT"] * (j == 2), [banks[j]])
    step("kx")
    act(T.XT[:, 0:W], T.XT[:, 0:W], F.Identity, ["XT"], ["XT"], bias=31.0, scale=-1.0)
    act(T.XT[:, NONE:W], T.ONE[:, 0:1], F.Copy, ["ONE"], ["XT"], scale=-8.0)
    act(T.Z0[:], T.Z0[:], F.Identity, ["Z0"], ["Z0_0", "Z0_1"], bias=31.0, scale=-1.0)
    step("kpick")
    ts(T.CV[:], T.BI[:, 48:60], p8, None, A.add, None, ["CF", "pm"], ["CV"])
    ts(T.MK[:], T.BI[:, 0:48], pg, None, A.is_equal, None, ["BI", "pm"], ["MK"])
    step("kpow")
    scan(T.P2[:], T.HF[:, 0:H], T.ONE[:, 0:H], 2.0 ** 97, A.mult, A.mult, ["HFa", "ONE"], ["P2"])
    tt(T.TP[:, 0:16], T.P2[:, 0:16], T.SI[:], A.mult, ["P2", "SI"], ["TP"])
    total(T.T1[:, 4:5], T.TP[:, 0:16], ["TP"], ["T14"])
    tt(T.TP[:], T.P2[:], T.ID[:, 0:H], A.mult, ["P2", "ID"], ["TP"])
    ts(T.T1[:, 5:6], T.T1[:, 4:5], 65536.0, None, A.mult, None, ["T14"], ["T15"])
    total(T.T1[:, 2:3], T.TP[:], ["TP"], ["T12"])
    scan(T.WT[:], T.HF[:, H:H + 12], T.ONE[:, 0:12], T.T1[:, 5:6], A.mult, A.mult, ["HFb", "ONE", "T15"], ["WT"])
    step("kth")
    cp(T.T1[:, 3:4], T.TH[:], ["TH"], ["T13"])
    ts(T.THB[:], T.ONE[:, 0:H], T.T1[:, 3:4], None, A.mult, None, ["ONE", "T13"], ["THB"])
    for c in range(2):
        mm(T.PC[0:H, 256 + 8 * c:264 + 8 * c], T.THB[:], T.Wt[:], True, True, ["THB", "Wt"], ["PLt"], "PC")
    ts(T.TH0[0:H, :], T.PC[0:H, 256:272], -498 * U, None, A.add, None, ["PLt"], ["TH0"], ["PC"])
    ts(T.TH1[0:H, :], T.PC[0:H, 256:272], -482.5 * U, None, A.add, None, ["PLt"], ["TH1"], ["PC"])
    step("kdump")
    for c in range(2):
        ts(T.T1[:, c:c + 1], pf, float(DUMP + H * c), None, A.add, None, ["pf"], ["T1%d" % c])
        ts(T.T1[:, 6 + c:7 + c], T.T1[:, 2:3], 2.5 * 2.0 ** (-H * c), None, A.mult, None, ["T12"], ["T1%d" % (6 + c)])
    for c in range(2):
        for lst in range(2):
            s = 2 * lst + c
            act(T.MD[:, hs(s, 48)], T.MK[:], F.Identity, ["MK", "T1%d" % c], ["MD%d" % s], scale=T.T1[:, c:c + 1])
            act(T.TC[0:H, hs(s, 8)], T.ONE[0:H, 0:8], F.Identity, ["ONE", "T1%d" % (6 + c)], ["TC%d" % s], scale=T.T1[0:H, 6 + c:7 + c])

    def kview(buf, c, k):
        return buf[:, 1536 * c + k:1536 * c + 1536:16]

    def kcols(P, k, o=0):
        return P[0:H, o + k:o + 128:16]

    def four(src, key, c, bank_):
        for e in range(4):
            mm(T[bank_][:, e:4 * H:4], T.Ib[:], src[:, hs(c)], True, True, ["Ib", key], [bank_], bank_)

    def eq(G, c, I):
        P = "CB%d" % c
        for j in range(4):
            step("eq%s%d%s" % (G[0], c, "abcd"[j]))
            s = (4 * c + j) * 4 * H
            tt(T.EQ[:, s:s + 4 * H], T[G][:, 1536 * c + j:1536 * c + 1536:4], T[P][:, 0:4 * H], A.is_equal,
               ["%s%d" % (G, c), P], ["EQ%d_%d" % (c, j)], [P])
            for e in range(4):
                mm(kcols(T.PC, j + 4 * e, 128 * c), T.EQ[:, s + e:s + 4 * H:4], T.W1[:], True, True, ["EQ%d_%d" % (c, j), "W1"], ["PC%d%d" % (c, j)], "PC")
        step("flag%s%d" % (G[0], c))
        cs, P, r = hs(c, 128), "PD%d" % c, ["PC%d%d" % (c, j) for j in range(4)]
        if G[0] + str(c) in VFLAGS:
            ts(T.FL[0:H, cs], T.PC[0:H, cs], 1.0, None, A.min, None, r, ["FL%d" % c], ["PC"])
        else:
            act(T.FL[0:H, cs], T.PC[0:H, cs], F.Sign, r, ["FL%d" % c], ["PC"])
        mm(T[P][0:H, 0:128], T[I][0:H, :], T.FL[0:H, cs], False, True, [I, "FL%d" % c], [P], P)

    def keys_open(c):
        P = "PD%d" % c
        mm(T[P][0:H, 0:128], T.ONE[0:1, 0:H], T.CR[0:1, :], True, False, ["ONE", "CR"], [P], P)

    def keys_add(c, src, key, rhs, after=()):
        P = "PD%d" % c
        return mm(T[P][0:H, 0:128], src[:, hs(c)], T[rhs][:], False, False, [key, rhs], [P], P, after)

    def keys_sum(c, view, key, rhs, ks=range(16)):
        P = "PD%d" % c
        return [mm(kcols(T[P], k), view(k), T[rhs][:], False, False, [key, rhs], [P], P) for k in ks]

    def to_list(out, src, lo, hi, key, w, P):
        for gg in range(8):
            mm(out, T.SEL[0:H, 112 - 16 * gg:240 - 16 * gg], src[0:H, lo + gg:hi:8], gg == 0, gg == 7, [key, "SEL"], [w], P)

    def pick(c, tag):
        P, cs, g8 = "PD%d" % c, hs(c, 128), hs(c, 8)
        step("scan" + tag)
        scan(T.SC[0:H, cs], T.RS[0:H, :], T[P][0:H, 0:128], 0.0, A.add, A.min, ["RS", P], ["SC%d" % c], [P])
        least, k = T.SC[0:H, 128 * c + 15:128 * c + 128:16], "SC%d" % c
        if tag[0] == "w":
            step("int" + tag)
            tt(T.S32[0:H, g8], least, T[P][0:H, 144:152], A.min, [k, "FB%d" % c], ["S32%d" % c], [P])
            least, k = T.S32[0:H, g8], "S32%d" % c
        step("low" + tag)
        ts(T.O32[0:H, g8], least, 2047, None, A.bitwise_and, None, [k], ["O32%d" % c])
        step("list" + tag)
        tt(T.OA[:, hs(c, 48)], T.O32[:, g8].indirect(T.CV[:, 0:3]), T.MK[:], A.mult, ["O32%d" % c, "CV", "MK"], ["OA%d" % c])
        to_list(T[P][:, 128:134], T.OA, 48 * c, 48 * c + 48, "OA%d" % c, "PL%d" % c, P)

    def first(src, keys, lst):
        for b in range(12):
            step("same%s%d" % ("ow"[lst], b // 2))
            lo, s0 = 16 * b, (2 * b if b < 6 else 5 + b) * H
            ts(T.EE[:, s0 + lo:s0 + L], src[:, lo:L], T.CL2[:, 12 * lst + b:12 * lst + b + 1], T.WT[:, b:b + 1], A.is_equal, A.mult,
               keys + ["WT", "EEz"], ["EE%d" % b])
            for c in range(0 if b < 6 else 1, 2):
                o = 16 * lst + 8 * c
                mm(T.PS[0:H, o:o + 8], T.EE[:, s0 + H * c:s0 + H * c + H], T.W1[:], False, lst == 0 and b == 11, ["EE%d" % b, "W1"], ["PS"], "PS")

    def send(t, p):
        sem, buf, lo, hi, o = PIECES[p]
        name, half = "%s%d" % (sem, t), "%d_%d" % (t, p // 2)
        src, via, dst = route(T, topo, rank, t)
        to = dst if via is None else via
        sent[0] += len(topo.engines(src, to))
        step("send%d" % p)
        me = record("G", lambda: put(g, T, topo, src, to, T["%sL%d" % (buf, t)][:, lo:hi], T["%sO%d" % (buf, t)][:, o:o + hi - lo], name),
                    None, 0, [buf + "O" + half], ["sends"])
        far, relay, here = route(T, topo, (rank - 1 - t % (NR - 1)) % NR, t)
        record("R", None, name, len(topo.engines(far if relay is None else relay, here)), [], [buf + "L" + half], (), [me])

    for t in range(RO):
        now[0] = t
        last = t == RO - 1
        wk, zk = ("WI", "Z0") if t == 0 else ("WL%d" % (t - 1), "ZL%d" % (t - 1))
        wl, z, ZO = T[wk][:, 0:12], T[zk], T["ZO%d" % t]
        wks, zks, zos = [wk + "_0", wk + "_1"], [zk + "_0", zk + "_1"], ["ZO%d_0" % t, "ZO%d_1" % t]
        for c in range(2):
            step("zr%d" % c)
            act(T.ZR[:, hs(c)], z[:, hs(c)], F.Sign, [zks[c]], ["ZR%d" % c])
            step("wb%d" % c)
            act(T.WB[:, hs(c)], IOw.indirect(T[wk][:, hs(c, 6)]), F.Identity, ["IO", "IOt", wks[c]], ["WB%d" % c], bias=OFF)
        step("idw")
        cp(T.IDL[:, 12:24], wl, wks, ["IDw"])
        step("clw")
        ncode(T.CL2[:, 12:24], T.IDL[:, 12:24], ["IDw"], ["CLw"], off=0.0)
        for c in range(2):
            wc, k = T[wk][:, hs(c, 6)], wks[c]
            step("e%d" % c)
            if t == 0:
                ts(T.E16[:, hs(c)], T.NM[:, 0:W].indirect(wc), 1.0 / 4096, None, A.mult, None, ["NM0", "NM1", "NM2", k], ["E16%d" % c])
            else:
                ts(T.E16[:, hs(c)], MTw.indirect(wc), 1.0 / 4096, float(TOP), A.mult, A.add, ["MT", k], ["E16%d" % c])
            step("wc%d" % c)
            ncode(T.WC[:, hs(c)], IOw.indirect(wc), ["IO", "IOt", k], ["WC%d" % c], off=0.0)
        for c in range(2):
            P = "PD%d" % c
            step("gN%d" % c)
            ncode(T.NG[:, hs(c, 1536)], NTw.indirect(T.E16[:, hs(c)]), ["NT", "NT0", "NT1", "NTt", "E16%d" % c], ["NG%d" % c])
            step("gX%d" % c)
            if c == 0:
                cp(T.XG[:, hs(c, 1536)], XTw.indirect(T.E16[:, hs(c)]), ["XT", "XTt", "E16%d" % c], ["XG%d" % c])
            else:
                act(T.XG[:, hs(c, 1536)], XTw.indirect(T.E16[:, hs(c)]), F.Copy, ["XT", "XTt", "E16%d" % c], ["XG%d" % c])
            step("open%d" % c)
            keys_open(c)
            wide = [keys_add(c, T.ZR, "ZR%d" % c, "BX8")]
            if c == 0:
                wide.append(keys_add(0, z, zks[0], "BOX"))
                step("fourz")
                four(z, zks[0], 0, "CB1")
                step("sumX")
                wide += keys_sum(0, lambda k_: kview(T.XG, 0, k_), "XG0", "Wm")
                for j in range(4):
                    step("max" + "abcd"[j])
                    s = j * 4 * H
                    tt(T.MX[:, s:s + 4 * H], T.XG[:, j:1536:4], T.CB1[:, 0:4 * H], A.max, ["XG0", "CB1"], ["MX%d" % j], ["CB1"])
                    for e in range(4):
                        wide.append(mm(kcols(T.PD0, j + 4 * e), T.MX[:, s + e:s + 4 * H:4], T.W2[:], False, False, ["MX%d" % j, "W2"], [P], P))
            else:
                for q in range(4):
                    X, keys = "PX%d" % (q % 2), whole[q % 2][0:2]
                    step("diff1" + "abcd"[q])
                    for e in range(4):
                        o = T[X][:, H * e:H * e + H]
                        mm(o, T.Ib[:], kview(T.XG, 1, 4 * q + e), True, False, ["Ib", "XG1"], keys, X)
                        mm(o, T.nI[:], z[:, hs(1)], False, True, ["nI", zks[1]], keys, X)
                    step("abs1" + "abcd"[q])
                    s = 1536 + 4 * H * q
                    act(T.MX[:, s:s + 4 * H], T[X][:, 0:4 * H], F.Abs, keys, ["AB%d" % q], [X])
                    keys_sum(1, lambda k_: T.MX[:, 1536 + H * k_:1536 + H * k_ + H], "AB%d" % q, "Wp", range(4 * q, 4 * q + 4))
            step("ef%d" % c)
            if t == 0:
                ts(T.EF[:, hs(c)], MTw.indirect(T[wk][:, hs(c, 6)]), 1.0 / 4096, float(TOP), A.mult, A.add,
                   ["MT", "MT0", "MT1", "MTt", "MTu", wks[c]], ["EF%d" % c])
                ts(T.EF[:, hs(c)], T.EF[:, hs(c)], float(JUNK), None, A.min, None, ["EF%d" % c], ["EF%d" % c])
            else:
                ts(T.EF[:, hs(c)], T.E16[:, hs(c)], float(JUNK), None, A.min, None, ["E16%d" % c], ["EF%d" % c])
            step("addE%d" % c)
            keys_add(c, T.EF, "EF%d" % c, "Ih", wide)
            step("fourw%d" % c)
            four(T.WC, "WC%d" % c, c, "CB%d" % c)
            eq("NG", c, "If1")
            pick(c, "o%d" % c)
            ol, k = T.OL[:, hs(c, 6)], "OL%d" % c
            step("ol%d" % c)
            ts(ol, T[P][:, 128:134], float(NONE), None, A.min, None, ["PL%d" % c], [k], [P])
            step("u%d" % c)
            ts(T.U16[:, hs(c)], NTw.indirect(ol), PAD - OFF, float(NONE + PAD), A.add, A.min, ["NT", k], ["U16%d" % c])
            step("ob%d" % c)
            act(T.OB[:, hs(c)], IOw.indirect(ol), F.Identity, ["IO", "IOt", k], ["OB%d" % c], bias=-OFF, scale=4096.0)
            step("oc%d" % c)
            ocode(T.OC[:, hs(c)], IOw.indirect(ol), ["IO", "IOt", k], ["OC%d" % c])
            step("clo%d" % c)
            ocode(T.CL2[:, hs(c, 6)], T[P][:, 128:134], ["PL%d" % c], ["CLo%d" % c], [P])
            step("ido%d" % c)
            act(T.IDL[:, hs(c, 6)], T[P][:, 128:134], F.Copy, ["PL%d" % c], ["IDo%d" % c], [P])
        step("miss")
        thk = "TH0" if t == 0 else "THR"
        tt(T.MS[0:H, :], T.SC[0:H, 15:256:16], T[thk][0:H, :], A.is_ge, ["SC0", "SC1", thk], ["MS"])
        step("uh")
        cp(T.UH[:], T.U16[:], ["U160", "U161"], ["UH"])
        ol, olk = T.OL[:, 0:12], ["OL0", "OL1"]
        if last:
            step("x255")
            act(T.XT[:, NONE:W], T.ONE[:, 0:1], F.Copy, ["ONE"], ["XT"], scale=31.0 - 255.0)
        for c in range(2):
            step("zo%d" % c)
            if last:
                act(ZO[:, hs(c)], XTw.indirect(T.OL[:, hs(c, 6)]), F.Identity, ["XT", olk[c]], [zos[c]], bias=31.0, scale=-1.0)
            else:
                act(ZO[:, hs(c)], XTw.indirect(T.OL[:, hs(c, 6)]), F.Relu, ["XT", olk[c]], [zos[c]])
        for c in range(2):
            P = "PD%d" % c
            step("gM%d" % c)
            mcode(T.MG[:, hs(c, 1536)], T.MT[:, 0:WIDE].indirect(T.U16[:, hs(c)]), ["MT", "U16%d" % c], ["MG%d" % c])
            if c == 1:
                step("qd")
                mm(T.PD1[:, 160:160 + L], T.Ih[:], T.EF[:], True, False, ["Ih", "EF0", "EF1"], ["QD"], P)
                mm(T.PD1[:, 160:160 + L], T.Iq[:], T.OB[:], False, True, ["Iq", "OB0", "OB1"], ["QD"], P)
            step("back%d" % c)
            mm(T[P][0:H, 144:152], T.ONF[0:1, :], T.CK[0:1, :], True, False, ["ONF", "CK"], ["FB%d" % c], P)
            mm(T[P][0:H, 144:152], T.WB[:, hs(c)], T.Wf[:], False, True, ["WB%d" % c, "Wf"], ["FB%d" % c], P)
            keys_open(c)
            step("fouro%d" % c)
            four(T.OC, "OC%d" % c, c, "CB%d" % c)
            step("addU%d" % c)
            keys_add(c, T.UH, "UH", "Ih")
            step("sumM%d" % c)
            keys_sum(c, lambda k_: kview(T.MG, c, k_), "MG%d" % c, "Wm")
            eq("MG", c, "If2")
            pick(c, "w%d" % c)
            step("wo%d" % c)
            ts(T["WO%d" % t][:, 8 * c:8 * c + 6], T[P][:, 128:134], float(PAD), None, A.subtract, None, ["PL%d" % c], ["WO%d_%d" % (t, c)], [P])
        for p in range(len(PIECES)):
            send(t, p)
        step("openS")
        mm(T.PS[0:H, 0:32], T.ZB[0:1, 0:H], T.ONE[0:1, 0:32], True, False, ["ZB", "ONE"], ["PS"], "PS")
        first(T.WC, ["WC0", "WC1", "CLw"], 1)
        step("rows")
        for c in range(2):
            mm(T.PS[0:H, 16 + 8 * c:24 + 8 * c], T.IB[0:H, :], T.MS[0:H, hs(c, 8)], False, False, ["IB", "MS"], ["PS"], "PS")
            mm(T.PX1[0:8, hs(c)], T.MS[0:H, hs(c, 8)], T.Ib[0:H, 0:H], True, True, ["Ib", "MS"], ["PX1"], "PX1")
        first(T.OC, ["OC0", "OC1", "CLo0", "CLo1"], 0)
        step("hit")
        act(T.HR[0:8, :], T.PX1[0:8, 0:L], F.Identity, ["PX1"], ["HR", "WIN"], ["PX1"], bias=1.0, scale=-1.0, acc=T.WIN[0:8, 0:1])
        mm(T.PX0[:, 0:L], T.EXB[0:8, :], T.HR[0:8, :], True, False, ["EXB", "HR"], ["PX0"], "PX0")
        mm(T.PX0[:, 0:L], T.Ib[:], T.RN[:, t:t + L], False, True, ["Ib", "RN"], ["PX0"], "PX0")
        if not last:
            mm(T.PX1[:, 400:401], T.UF[0:8, :], T.WIN[0:8, 0:1], True, False, ["UF", "WIN"], ["wins"], "PX1")
            mm(T.PX1[:, 400:401], T.ONE[0:1, :], T.HLF[0:1, 0:1], False, True, ["ONE", "HLF"], ["wins"], "PX1")
            step("dx")
            mm(T.PX1[:, L:2 * L], T.Ib[:], z[:], True, False, ["Ib"] + zks, ["dx"], "PX1")
            mm(T.PX1[:, L:2 * L], T.nI[:], ZO[:], False, False, ["nI"] + zos, ["dx"], "PX1")
            mm(T.PX1[:, L:2 * L], T.EXN[0:8, :], T.HR[0:8, :], False, True, ["EXN", "HR"], ["dx"], "PX1")
        step("no")
        act(T.DN[:], NTw.indirect(ol), F.Copy, ["NT"] + olk, ["DN"])
        step("dn")
        mm(T.PX1[:, 0:L], T.ID[:], T.DN[:], True, False, ["ID", "DN"], ["PX1"], "PX1")
        mm(T.PX1[:, 0:L], T.nF[:], T.WB[:], False, True, ["nF", "WB0", "WB1"], ["PX1"], "PX1")
        step("sb")
        act(T.SB[:], T.PX0[:, 0:L], F.Copy, ["PX0"], ["SB"], ["PX0"])
        step("q")
        act(T.Q[:], T.PD1[:, 160:160 + L], F.Abs, ["QD"], ["Q"], ["PD1"], bias=-float(TOP))
        act(T.Q[:], T.Q[:], F.Relu, ["Q"], ["Q"], bias=1.0, scale=-1.0)
        step("kn")
        tt(T.KN[:], T.SB[:], T.PX1[:, 0:L], A.mult, ["SB", "PX1"], ["KN"], ["PX1"])
        step("ff")
        tt(T.FF[0:H, :], T.PS[0:H, 0:32], T.TC[0:H, :], A.is_ge, ["PS"] + ["TC" + s for s in "0123"], ["FF"], ["PS"])
        step("od")
        tt(T.OD[:], T.FF[:, 0:32].indirect(T.CV[:, 0:12]), T.MD[:], A.mult, ["FF", "CV"] + ["MD" + s for s in "0123"], ["OD"])
        to_list(T.PS[:, 32:56], T.OD, 0, L, "OD", "PO", "PS")
        step("of")
        tt(T.OF[:], T.IDL[:], T.PS[:, 32:56], A.max, ["IDo0", "IDo1", "IDw", "PO"], ["OF"], ["PS"])
        step("ofu")
        cp(T.OFU[:], T.OF[:], ["OF"], ["OFU"])
        step("putN")
        tt(NTw.indirect(T.OFU[:, 0:12]), T.WB[:], T.KN[:], A.add, ["WB0", "WB1", "KN", "OFU"], ["NT"])
        step("putM")
        tt(MTw.indirect(T.OFU[:, 12:24]), T.OB[:], T.Q[:], A.mult, ["OB0", "OB1", "Q", "OFU"], ["MT"])
        if not last:
            step("cl")
            act(T.CL[:], T.PX1[:, L:2 * L], F.Abs, ["dx"], ["CL"], ["PX1"], bias=1.0, scale=0.5)
            act(T.CM[:], T.PX1[:, L:2 * L], F.Abs, ["dx"], ["CM"], ["PX1"], bias=-1.0, scale=0.5)
            o = T.PX0[:, L:2 * L]
            mm(o, T.Ib[:], ZO[:], True, False, ["Ib"] + zos, ["xn"], "PX0")
            mm(o, T.EX2[0:8, :], T.HR[0:8, :], False, False, ["EX2", "HR"], ["xn"], "PX0")
            mm(o, T.Ib[:], T.CL[:], False, False, ["Ib", "CL"], ["xn"], "PX0")
            mm(o, T.nI[:], T.CM[:], False, True, ["nI", "CM"], ["xn"], "PX0")
            step("cm")
            act(T.XN[:], o, F.Copy, ["xn"], ["XN"], ["PX0"])
            step("putX")
            cp(XTw.indirect(T.OFU[:, 0:12]), T.XN[:], ["XN", "OFU"], ["XT"])
            step("ss")
            ts(T.WIN[:, 1:2], T.PX1[:, 400:401], 1.5 * 2.0 ** 43, 1.5 * 2.0 ** 43, A.add, A.subtract, ["wins"], ["SS"], ["PX1"])
            step("thr")
            ts(T.THR[0:H, :], T.TH1[0:H, :], T.PX1[0:H, 400:401], T.WIN[0:H, 1:2], A.add, A.subtract, ["TH1", "wins", "SS"], ["THR"], ["PX1"])

    t = RO - 1
    top = NONE * 4096.0
    step("outz")
    dma("S", T.yz[:], T["ZL%d" % t][:], "st", r=["ZL%d_0" % t, "ZL%d_1" % t])
    for j in range(3):
        c = hs(j, 512)
        step("absN%d" % j)
        act(T.FT[:, c], T.NT[:, c], F.Abs, ["NT"], ["FT%d" % j], bias=-OFF)
        step("cutN%d" % j)
        if j < FIN:
            act(T.FT[:, c], T.FT[:, c], F.Relu, ["FT%d" % j], ["FT%d" % j], bias=float(NONE), scale=-1.0)
            act(T.FT[:, c], T.FT[:, c], F.Identity, ["FT%d" % j], ["FT%d" % j], bias=top + NONE, scale=-1.0)
        else:
            ts(T.FT[:, c], T.FT[:, c], float(NONE), top, A.min, A.add, ["FT%d" % j], ["FT%d" % j])
        step("cutM%d" % j)
        act(T[banks[j]][:], T.MT[:, PAD + 512 * j:PAD + 512 * j + 512], F.Relu, ["MT"], whole[j], [banks[j]], bias=top - OFF, scale=-1.0)
        for i in range(2):
            step("out%d%s" % (j, "ab"[i]))
            c = hs(2 * j + i, 256)
            tt(T.OUT[:, c], T.FT[:, c], T[banks[j]][:, hs(i, 256)], A.subtract, ["FT%d" % j, banks[j]], ["OUT%d%d" % (j, i)], [banks[j]])
            dma("SA"[i], T.ynm[:, c], T.OUT[:, c], "st", r=["OUT%d%d" % (j, i)])
    step("outw")
    dma("A", T.yw[:], T["WL%d" % t][:], "st", r=["WL%d_0" % t, "WL%d_1" % t])
    issue()
